import numpy as np
import ml_dtypes


def mxq(x, axis, fmt="e4m3"):
    dtype, down = {"e4m3": (ml_dtypes.float8_e4m3fn, 7), "e5m2": (ml_dtypes.float8_e5m2, 14)}[fmt]
    v = np.moveaxis(np.asarray(x, np.float32).astype(ml_dtypes.bfloat16).astype(np.float64), axis, -1)
    blocks = v.reshape(v.shape[:-1] + (-1, 32))
    amax = np.abs(blocks).max(-1, keepdims=True)
    byte = np.maximum(np.where(amax > 0, np.frexp(amax)[1] - 1 + 127, 0) - down, 1)
    scale = np.exp2(byte - 127.0)
    codes = (blocks / scale).astype(np.float32).astype(dtype).astype(np.float64)
    return np.moveaxis((codes * scale).reshape(v.shape), -1, axis)


WIDE = False


def mx_kscale(k):
    if not WIDE:
        return np.ones(k)
    levels = np.array([10, -10, 5, -5, 0])
    if k % 512:
        return np.exp2(np.random.permutation(np.resize(levels, k // 32))).repeat(32)
    a = np.empty((k // 512, 16))
    for p in range(k // 512):
        a[p, :8] = np.random.permutation(np.resize(levels, 8))
        for g in range(8):
            far = levels[np.abs(levels - a[p, g]) >= 10]
            a[p, g + 8] = far[np.random.randint(len(far))]
    return np.exp2(a.ravel()).repeat(32)


def f64(x):
    return np.asarray(x).astype(np.float64)


def striped(idx):
    return np.tile(idx.reshape(-1, 16).T, (8, 1)).astype(np.uint16)


def unstriped(offs):
    return offs[:16].T.reshape(-1).astype(np.int64)


def pack_weight(w):
    k, n = w.shape
    w = f64(np.asarray(w, np.float32).astype(ml_dtypes.bfloat16)).reshape(k // 32, 32, n)
    amax = np.abs(w).max(1)
    byte = np.clip(np.where(amax > 0, np.frexp(amax)[1] - 1 + 127 - 7, 1), 1, 254)
    scaled = (w * np.exp2(127.0 - byte)[:, None, :]).reshape(k, n).astype(np.float32)
    words = np.ascontiguousarray(scaled.reshape(k // 512, 128, 4, n).transpose(0, 1, 3, 2)).astype(ml_dtypes.float8_e4m3fn).view(np.uint8)
    return words, np.ascontiguousarray(byte.astype(np.uint8).reshape(k // 512, 16, n))


def unpack_weight(words, scales):
    g, p, n, _ = words.shape
    vals = np.ascontiguousarray(words).view(ml_dtypes.float8_e4m3fn).astype(np.float64) * np.repeat(np.exp2(scales.astype(np.float64) - 127.0), 8, axis=1)[..., None]
    return vals.transpose(0, 1, 3, 2).reshape(g * 512, n)


K, T, S, D, H, N, V = 512, 4096, 1024, 4, 512, 128, 256
P = 2 ** 7


def setup_inputs():
    n = np.random.standard_normal
    s = mx_kscale(K)[:, None]
    u = mx_kscale(H)
    packed_xT = pack_weight(n((K, T)) * s)
    return {
        "x_words": packed_xT[0],
        "x_scales": packed_xT[1],
        "w1": (n((K, H)) / np.sqrt(K) / s).astype(np.float32),
        "unit": (np.random.uniform(0.5, 1.0, (H, 1)) * u[:, None]).astype(np.float32),
        "w2": (n((H, N)) / np.sqrt(H) / u[:, None]).astype(np.float32),
        "depth": (np.tile(np.random.uniform(0.5, 3.0, V), (P, 1))).astype(np.float32),
        "offs": striped(np.random.permutation(T)[:S]),
    }


def reference(x_words, x_scales, w1, unit, w2, depth, offs):
    xq = unpack_weight(x_words, x_scales)[:, unstriped(offs)]
    y = mxq(f64(w1), 0, "e4m3").T @ xq
    y2 = (y) ** 2
    z = f64(unit) * (y2.reshape(len(y2), -1, D).mean(axis=2) - ((y.reshape(len(y), -1, D).mean(axis=2)) ** 2))
    sc = mxq(f64(w2), 0, "e4m3").T @ mxq(z, 0, "e4m3")
    top = sc.reshape(len(sc), -1, D).max(axis=2)
    ex = np.exp(sc - np.repeat(top, D, axis=1))
    total = ex.reshape(len(ex), -1, D).sum(axis=2)
    p = ex / np.repeat(total, D, axis=1)
    pd = p * f64(depth)[:1]
    return pd.reshape(len(pd), -1, D).sum(axis=2)

@@ -1,0 +1,166 @@
+import math
+from contextlib import ExitStack
+
+import concourse.mybir as mybir
+from concourse.masks import make_identity
+
+K, T, S, D, H, N, V = 512, 4096, 1024, 4, 512, 128, 256
+FLOPS = 2 * K * H * S + 2 * H * N * V
+
+F32 = mybir.dt.float32
+BF16 = mybir.dt.bfloat16
+I32 = mybir.dt.int32
+U32 = mybir.dt.uint32
+U16 = mybir.dt.uint16
+U8 = mybir.dt.uint8
+FP8X4 = mybir.dt.float8_e4m3fn_x4
+ALU = mybir.AluOpType
+ACT = mybir.ActivationFunctionType
+AXIS_X = mybir.AxisListType.X
+
+P = 128
+PACK = 4
+HALVES = V // P
+CHUNKS = ((0, 2), (2, 4))
+
+
+def tile_picked_ymvs_mean_p_kernel(tc, x_words, x_scales, w1, unit, w2, depth, offs, out):
+    nc = tc.nc
+    with ExitStack() as ctx:
+        keep = ctx.enter_context(tc.tile_pool(name="keep", bufs=1))
+        psum = ctx.enter_context(tc.psum_pool(name="psum", bufs=8))
+
+        def sb(name, shape, dtype):
+            return keep.tile(shape, dtype, name=name, align_bytes=64)
+
+        def bank(name, shape):
+            return psum.tile(shape, F32, name=name, tag="bank")
+
+        offsets = keep.tile([P, S // 16], U16, name="offsets")
+        nc.sync.dma_start(offsets[:], offs)
+
+        w1_raw = sb("w1_raw", [P, PACK, H], F32)
+        nc.scalar.dma_start(out=w1_raw[:], in_=w1.rearrange("(p j) c -> p j c", j=PACK))
+        word_table = sb("word_table", [P, T], I32)
+        nc.scalar.dma_start(out=word_table[:], in_=x_words[0].rearrange("p n t -> p (n t)").bitcast(I32))
+        w2_raw = sb("w2_raw", [P, PACK, N], F32)
+        nc.scalar.dma_start(out=w2_raw[:], in_=w2.rearrange("(p j) c -> p j c", j=PACK))
+        depth_sb = sb("depth_sb", [P, V], F32)
+        nc.scalar.dma_start(out=depth_sb[:], in_=depth)
+        unit_sb = sb("unit_sb", [P, PACK], F32)
+        nc.gpsimd.dma_start(out=unit_sb[:], in_=unit.rearrange("(p t) o -> p (t o)", t=PACK))
+
+        scale_table = sb("scale_table", [P, T], U8)
+        nc.vector.memset(scale_table[:].bitcast(I32), 0)
+        nc.sync.dma_start(out=scale_table[:].bitcast(I32)[0:P:8, :], in_=x_scales[0].bitcast(I32))
+        x_plane = sb("x_plane", [P, S], U8)
+        nc.vector.memset(x_plane[:].bitcast(I32), 0)
+
+        ident = sb("ident", [P, P], F32)
+        make_identity(nc, ident[:])
+
+        picked_scales = sb("picked_scales", [P, S], U8)
+        nc.vector.tensor_copy(picked_scales[:], scale_table[:].indirect(offsets[:]))
+        scales_by_view = sb("scales_by_view", [P, S], U8)
+        nc.vector.tensor_copy(
+            out=scales_by_view[:].rearrange("p (h d v) -> p h d v", h=HALVES, d=D),
+            in_=picked_scales[:].rearrange("p (h v d) -> p h d v", h=HALVES, d=D),
+        )
+        for r in range(4):
+            nc.sync.dma_start(out=x_plane[:].bitcast(I32)[r:P:32, :], in_=scales_by_view[:].bitcast(I32)[8 * r : P : 32, :])
+
+        w1_bf = sb("w1_bf", [P, H, PACK], BF16)
+        nc.scalar.activation(out=w1_bf[:], in_=w1_raw[:].rearrange("p j c -> p c j"), func=ACT.Copy)
+        w1_codes = sb("w1_codes", [P, H], U32)
+        w1_plane = sb("w1_plane", [P, H], U8)
+        nc.vector.quantize_mx(out=w1_codes[:].bitcast(FP8X4), scales=w1_plane[:], in_=w1_bf[:].rearrange("p c j -> p (c j)"))
+
+        w2_bf = sb("w2_bf", [P, N, PACK], BF16)
+        nc.scalar.activation(out=w2_bf[:], in_=w2_raw[:].rearrange("p j c -> p c j"), func=ACT.Copy)
+        w2_codes = sb("w2_codes", [P, N], U32)
+        w2_plane = sb("w2_plane", [P, N], U8)
+
+        entries = S // HALVES
+        banks = []
+        for h in range(HALVES):
+            codes = sb(f"x_codes{h}", [P, D, P], U32)
+            nc.vector.tensor_copy(
+                codes[:].rearrange("p d v -> p v d"),
+                word_table[:].bitcast(U32).indirect(offsets[:, h * entries // 16 : (h + 1) * entries // 16]),
+            )
+
+            def product(acc, d, start, stop):
+                c0 = h * entries + d * P
+                nc.tensor.matmul_mx(
+                    out=acc[:], lhsT=codes[:, d, :].bitcast(FP8X4), lhsT_scale=x_plane[:, c0 : c0 + P],
+                    rhs=w1_codes[:].bitcast(FP8X4), rhs_scale=w1_plane[:], start=start, stop=stop,
+                )
+
+            y1 = bank(f"y1_{h}", [P, H])
+            y01 = bank(f"y01_{h}", [P, H])
+            y3 = bank(f"y3_{h}", [P, H])
+            y2 = bank(f"y2_{h}", [P, H])
+            product(y1, 1, True, True)
+            product(y01, 1, True, False)
+            product(y01, 0, False, True)
+            product(y3, 3, True, True)
+            product(y2, 2, True, True)
+            banks.append((y1, y01, y3, y2))
+
+        nc.vector.quantize_mx(out=w2_codes[:].bitcast(FP8X4), scales=w2_plane[:], in_=w2_bf[:].rearrange("p c j -> p (c j)"))
+
+        def dealt(acc, t0, t1):
+            return acc[:].rearrange("p (m t) -> p t m", t=PACK)[:, t0:t1, :]
+
+        z_banks = []
+        for h in range(HALVES):
+            y1, y01, y3, y2 = banks[h]
+            names = ("y1s", "y3s", "a", "b", "t23", "c", "aa", "bb", "cc")
+            y1s, y3s, a, b, t23, c, aa, bb, cc = [sb(f"{n}{h}", [P, PACK, P], F32) for n in names]
+            for t0, t1 in CHUNKS:
+                nc.scalar.activation(out=y1s[:, t0:t1, :], in_=dealt(y1, t0, t1), func=ACT.Copy, scale=2.0)
+                nc.scalar.copy(out=y3s[:, t0:t1, :], in_=dealt(y3, t0, t1))
+            zb = bank(f"z{h}", [P, PACK, P])
+            for t0, t1 in CHUNKS:
+                ts = slice(t0, t1)
+                nc.vector.tensor_tensor(out=t23[:, ts, :], in0=dealt(y2, t0, t1), in1=y3s[:, ts, :], op=ALU.add)
+                nc.vector.tensor_tensor(out=a[:, ts, :], in0=dealt(y01, t0, t1), in1=y1s[:, ts, :], op=ALU.subtract)
+                nc.vector.tensor_tensor(out=c[:, ts, :], in0=dealt(y01, t0, t1), in1=t23[:, ts, :], op=ALU.subtract)
+                nc.vector.tensor_tensor(out=b[:, ts, :], in0=dealt(y2, t0, t1), in1=y3s[:, ts, :], op=ALU.subtract)
+                nc.scalar.activation(out=aa[:, ts, :], in_=a[:, ts, :], func=ACT.Square, scale=math.sqrt(0.125))
+                nc.scalar.activation(out=cc[:, ts, :], in_=c[:, ts, :], func=ACT.Square, scale=0.25)
+                nc.scalar.activation(out=bb[:, ts, :], in_=b[:, ts, :], func=ACT.Square, scale=math.sqrt(0.125))
+                for t in range(t0, t1):
+                    for i, sq in enumerate((aa, cc, bb)):
+                        nc.tensor.matmul(out=zb[:, t, :], lhsT=sq[:, t, :], rhs=ident[:], is_transpose=True, start=(i == 0), stop=(i == 2))
+            z_banks.append(zb)
+
+        result = sb("result", [P, V // D], F32)
+        groups = P // D
+        for h in range(HALVES):
+            z_bf = sb(f"z_bf{h}", [P, P, PACK], BF16)
+            nc.vector.tensor_tensor(
+                out=z_bf[:], in0=z_banks[h][:].rearrange("p t v -> p v t"),
+                in1=unit_sb[:].unsqueeze(1).to_broadcast([P, P, PACK]), op=ALU.mult,
+            )
+            z_codes = sb(f"z_codes{h}", [P, P], U32)
+            z_plane = sb(f"z_plane{h}", [P, P], U8)
+            nc.vector.quantize_mx(out=z_codes[:].bitcast(FP8X4), scales=z_plane[:], in_=z_bf[:].rearrange("p v t -> p (v t)"))
+            sc = bank(f"sc{h}", [P, groups, D])
+            nc.tensor.matmul_mx(
+                out=sc[:].rearrange("p g d -> p (g d)"), lhsT=w2_codes[:].bitcast(FP8X4), lhsT_scale=w2_plane[:],
+                rhs=z_codes[:].bitcast(FP8X4), rhs_scale=z_plane[:], start=True, stop=True,
+            )
+            top = sb(f"top{h}", [P, groups], F32)
+            nc.vector.tensor_reduce(out=top[:], in_=sc[:], axis=AXIS_X, op=ALU.max)
+            shifted = sb(f"shifted{h}", [P, groups, D], F32)
+            nc.vector.tensor_tensor(out=shifted[:], in0=sc[:], in1=top[:].unsqueeze(2).to_broadcast([P, groups, D]), op=ALU.subtract)
+            both = sb(f"both{h}", [P, 2, P], F32)
+            nc.scalar.activation(out=both[:, 0, :], in_=shifted[:].rearrange("p g d -> p (g d)"), func=ACT.Exp)
+            nc.vector.tensor_tensor(out=both[:, 1, :], in0=both[:, 0, :], in1=depth_sb[:, h * P : (h + 1) * P], op=ALU.mult)
+            sums = sb(f"sums{h}", [P, 2, groups], F32)
+            nc.vector.tensor_reduce(out=sums[:].rearrange("p s g -> p (s g)"), in_=both[:].rearrange("p s (g d) -> p (s g) d", d=D), axis=AXIS_X, op=ALU.add)
+            inv = sb(f"inv{h}", [P, groups], F32)
+            nc.vector.reciprocal(out=inv[:], in_=sums[:, 0, :])
+            nc.vector.tensor_tensor(out=result[:, h * groups : (h + 1) * groups], in0=sums[:, 1, :], in1=inv[:], op=ALU.mult)
+        nc.sync.dma_start(out=out, in_=result[:])

@@ -21,7 +21,7 @@ AXIS_X = mybir.AxisListType.X
 P = 128
 PACK = 4
 HALVES = V // P
-CHUNKS = ((0, 2), (2, 4))
+HALF = H // 2
 
 
 def tile_picked_ymvs_mean_p_kernel(tc, x_words, x_scales, w1, unit, w2, depth, offs, out):
@@ -39,22 +39,25 @@ def tile_picked_ymvs_mean_p_kernel(tc, x_words, x_scales, w1, unit, w2, depth, o
         offsets = keep.tile([P, S // 16], U16, name="offsets")
         nc.sync.dma_start(offsets[:], offs)
 
-        w1_raw = sb("w1_raw", [P, PACK, H], F32)
-        nc.scalar.dma_start(out=w1_raw[:], in_=w1.rearrange("(p j) c -> p j c", j=PACK))
+        scale_table = sb("scale_table", [P, T], U8)
+        nc.sync.dma_start(out=scale_table[:].bitcast(I32)[16:32, :], in_=x_scales[0].bitcast(I32))
+        for p0, p1 in ((0, 16), (32, 64), (64, P)):
+            nc.vector.memset(scale_table[:].bitcast(I32)[p0:p1, :], 0)
+        x_plane = sb("x_plane", [P, S], U8)
+        nc.vector.memset(x_plane[:].bitcast(I32), 0)
+
+        w1_rows = w1.rearrange("(p j) c -> p j c", j=PACK)
+        w1_raw = [sb(f"w1_raw{g}", [P, PACK, HALF], F32) for g in range(2)]
         word_table = sb("word_table", [P, T], I32)
+        nc.scalar.dma_start(out=w1_raw[0][:], in_=w1_rows[:, :, 0:HALF])
         nc.scalar.dma_start(out=word_table[:], in_=x_words[0].rearrange("p n t -> p (n t)").bitcast(I32))
+        nc.scalar.dma_start(out=w1_raw[1][:], in_=w1_rows[:, :, HALF:H])
         w2_raw = sb("w2_raw", [P, PACK, N], F32)
         nc.scalar.dma_start(out=w2_raw[:], in_=w2.rearrange("(p j) c -> p j c", j=PACK))
         depth_sb = sb("depth_sb", [P, V], F32)
         nc.scalar.dma_start(out=depth_sb[:], in_=depth)
         unit_sb = sb("unit_sb", [P, PACK], F32)
         nc.gpsimd.dma_start(out=unit_sb[:], in_=unit.rearrange("(p t) o -> p (t o)", t=PACK))
-
-        scale_table = sb("scale_table", [P, T], U8)
-        nc.vector.memset(scale_table[:].bitcast(I32), 0)
-        nc.sync.dma_start(out=scale_table[:].bitcast(I32)[0:P:8, :], in_=x_scales[0].bitcast(I32))
-        x_plane = sb("x_plane", [P, S], U8)
-        nc.vector.memset(x_plane[:].bitcast(I32), 0)
 
         ident = sb("ident", [P, P], F32)
         make_identity(nc, ident[:])
@@ -66,77 +69,130 @@ def tile_picked_ymvs_mean_p_kernel(tc, x_words, x_scales, w1, unit, w2, depth, o
             out=scales_by_view[:].rearrange("p (h d v) -> p h d v", h=HALVES, d=D),
             in_=picked_scales[:].rearrange("p (h v d) -> p h d v", h=HALVES, d=D),
         )
-        for r in range(4):
-            nc.sync.dma_start(out=x_plane[:].bitcast(I32)[r:P:32, :], in_=scales_by_view[:].bitcast(I32)[8 * r : P : 32, :])
+        for q in range(4):
+            nc.sync.dma_start(
+                out=x_plane[:].bitcast(I32)[32 * q : 32 * q + 4, :], in_=scales_by_view[:].bitcast(I32)[16 + 4 * q : 20 + 4 * q, :]
+            )
 
-        w1_bf = sb("w1_bf", [P, H, PACK], BF16)
-        nc.scalar.activation(out=w1_bf[:], in_=w1_raw[:].rearrange("p j c -> p c j"), func=ACT.Copy)
         w1_codes = sb("w1_codes", [P, H], U32)
         w1_plane = sb("w1_plane", [P, H], U8)
-        nc.vector.quantize_mx(out=w1_codes[:].bitcast(FP8X4), scales=w1_plane[:], in_=w1_bf[:].rearrange("p c j -> p (c j)"))
 
-        w2_bf = sb("w2_bf", [P, N, PACK], BF16)
-        nc.scalar.activation(out=w2_bf[:], in_=w2_raw[:].rearrange("p j c -> p c j"), func=ACT.Copy)
-        w2_codes = sb("w2_codes", [P, N], U32)
-        w2_plane = sb("w2_plane", [P, N], U8)
+        def quantize_w1(g):
+            cols = slice(g * HALF, (g + 1) * HALF)
+            grouped = keep.tile([P, HALF, PACK], BF16, name=f"w1_bf{g}", tag="weights_bf", align_bytes=64)
+            nc.scalar.activation(out=grouped[:], in_=w1_raw[g][:].rearrange("p j c -> p c j"), func=ACT.Copy)
+            nc.vector.quantize_mx(out=w1_codes[:, cols].bitcast(FP8X4), scales=w1_plane[:, cols], in_=grouped[:].rearrange("p c j -> p (c j)"))
 
         entries = S // HALVES
-        banks = []
-        for h in range(HALVES):
+
+        def gather_words(h):
             codes = sb(f"x_codes{h}", [P, D, P], U32)
             nc.vector.tensor_copy(
                 codes[:].rearrange("p d v -> p v d"),
                 word_table[:].bitcast(U32).indirect(offsets[:, h * entries // 16 : (h + 1) * entries // 16]),
             )
+            return codes
 
-            def product(acc, d, start, stop):
-                c0 = h * entries + d * P
-                nc.tensor.matmul_mx(
-                    out=acc[:], lhsT=codes[:, d, :].bitcast(FP8X4), lhsT_scale=x_plane[:, c0 : c0 + P],
-                    rhs=w1_codes[:].bitcast(FP8X4), rhs_scale=w1_plane[:], start=start, stop=stop,
-                )
+        def product(acc, h, d, cols, start, stop):
+            c0 = h * entries + d * P
+            nc.tensor.matmul_mx(
+                out=acc, lhsT=x_codes[h][:, d, :].bitcast(FP8X4), lhsT_scale=x_plane[:, c0 : c0 + P],
+                rhs=w1_codes[:, cols].bitcast(FP8X4), rhs_scale=w1_plane[:, cols], start=start, stop=stop,
+            )
 
-            y1 = bank(f"y1_{h}", [P, H])
-            y01 = bank(f"y01_{h}", [P, H])
-            y3 = bank(f"y3_{h}", [P, H])
-            y2 = bank(f"y2_{h}", [P, H])
-            product(y1, 1, True, True)
-            product(y01, 1, True, False)
-            product(y01, 0, False, True)
-            product(y3, 3, True, True)
-            product(y2, 2, True, True)
-            banks.append((y1, y01, y3, y2))
+        def products(h, cols, y1, y3, y01, y2):
+            product(y1, h, 1, cols, True, True)
+            product(y3, h, 3, cols, True, True)
+            product(y01, h, 1, cols, True, False)
+            product(y01, h, 0, cols, False, True)
+            product(y2, h, 2, cols, True, True)
 
+        quantize_w1(0)
+        x_codes = [gather_words(0)]
+        quantize_w1(1)
+        x_codes.append(gather_words(1))
+
+        odd, even = [], []
+        for g in range(2):
+            odd.append(bank(f"odd{g}", [P, 2, HALF]))
+            even.append(bank(f"even{g}", [P, 2, HALF]))
+            products(0, slice(g * HALF, (g + 1) * HALF), odd[g][:, 0, :], odd[g][:, 1, :], even[g][:, 0, :], even[g][:, 1, :])
+        y1, y3, y01, y2 = [bank(n, [P, H]) for n in ("y1", "y3", "y01", "y2")]
+        products(1, slice(0, H), y1[:], y3[:], y01[:], y2[:])
+
+        w2_bf = keep.tile([P, N, PACK], BF16, name="w2_bf", tag="weights_bf", align_bytes=64)
+        nc.gpsimd.tensor_scalar(out=w2_bf[:], in0=w2_raw[:].rearrange("p j c -> p c j"), scalar1=1.0, scalar2=0.0, op0=ALU.mult, op1=ALU.add)
+
+        copied = [sb(f"copied{h}", [P, 2, PACK, P], F32) for h in range(HALVES)]
+        ab = [sb(f"ab{h}", [P, 2, PACK, P], F32) for h in range(HALVES)]
+        y23 = [sb(f"y23_{h}", [P, PACK, P], F32) for h in range(HALVES)]
+        c = [sb(f"c{h}", [P, PACK, P], F32) for h in range(HALVES)]
+        ab_sq = [sb(f"ab_sq{h}", [P, 2, PACK, P], F32) for h in range(HALVES)]
+        c_sq = [sb(f"c_sq{h}", [P, PACK, P], F32) for h in range(HALVES)]
+        z_banks = [bank(f"z{h}", [P, PACK, P]) for h in range(HALVES)]
+
+        def add_squares(h, t):
+            for i, sq in enumerate((ab_sq[h][:, 0, t, :], ab_sq[h][:, 1, t, :], c_sq[h][:, t, :])):
+                nc.tensor.matmul(out=z_banks[h][:, t, :], lhsT=sq, rhs=ident[:], is_transpose=True, start=(i == 0), stop=(i == 2))
+
+        for g in range(2):
+            ms = slice(g * HALF // PACK, (g + 1) * HALF // PACK)
+            odd_t = odd[g][:].rearrange("p s (m t) -> p s t m", t=PACK)
+            even_t = even[g][:].rearrange("p s (m t) -> p s t m", t=PACK)
+            nc.scalar.copy(out=copied[0][:, 1, :, ms], in_=odd_t[:, 1])
+            nc.scalar.activation(out=copied[0][:, 0, :, ms], in_=odd_t[:, 0], func=ACT.Copy, scale=2.0)
+            nc.vector.tensor_tensor(out=y23[0][:, :, ms], in0=even_t[:, 1], in1=copied[0][:, 1, :, ms], op=ALU.add)
+            nc.vector.tensor_tensor(out=ab[0][:, :, :, ms], in0=even_t, in1=copied[0][:, :, :, ms], op=ALU.subtract)
+            nc.vector.tensor_tensor(out=c[0][:, :, ms], in0=even_t[:, 0], in1=y23[0][:, :, ms], op=ALU.subtract)
+
+        def dealt(acc, ts):
+            return acc[:].rearrange("p (m t) -> p t m", t=PACK)[:, ts, :]
+
+        def square_ab(h, where):
+            nc.scalar.activation(out=ab_sq[h][where], in_=ab[h][where], func=ACT.Square, scale=math.sqrt(0.125))
+
+        def square_c(h, where):
+            nc.scalar.activation(out=c_sq[h][where], in_=c[h][where], func=ACT.Square, scale=0.25)
+
+        def copy_odd_views(ts):
+            nc.scalar.copy(out=copied[1][:, 1, ts, :], in_=dealt(y3, ts))
+            nc.scalar.activation(out=copied[1][:, 0, ts, :], in_=dealt(y1, ts), func=ACT.Copy, scale=2.0)
+
+        every = slice(None)
+        first, second = slice(0, 2), slice(2, 4)
+        low, high = slice(0, P // 2), slice(P // 2, P)
+        copy_odd_views(first)
+        square_ab(0, (every, every, every, low))
+        square_c(0, (every, every, low))
+        copy_odd_views(second)
+        for ts in (first, second):
+            square_ab(0, (every, every, ts, high))
+            square_c(0, (every, ts, high))
+            for t in range(ts.start, ts.stop):
+                add_squares(0, t)
+        for ts in (first, second):
+            nc.vector.tensor_tensor(out=y23[1][:, ts, :], in0=dealt(y2, ts), in1=copied[1][:, 1, ts, :], op=ALU.add)
+            nc.vector.tensor_tensor(out=ab[1][:, 0, ts, :], in0=dealt(y01, ts), in1=copied[1][:, 0, ts, :], op=ALU.subtract)
+            nc.vector.tensor_tensor(out=ab[1][:, 1, ts, :], in0=dealt(y2, ts), in1=copied[1][:, 1, ts, :], op=ALU.subtract)
+            nc.vector.tensor_tensor(out=c[1][:, ts, :], in0=dealt(y01, ts), in1=y23[1][:, ts, :], op=ALU.subtract)
+            if ts == first:
+                square_ab(1, (every, every, ts, every))
+            else:
+                square_ab(1, (every, 0, ts, every))
+                for t in range(ts.start, ts.stop):
+                    nc.vector.scalar_tensor_tensor(
+                        out=ab_sq[1][:, 1, t, :], in0=ab[1][:, 1, t, :], scalar=0.125, in1=ab[1][:, 1, t, :], op0=ALU.mult, op1=ALU.mult
+                    )
+            square_c(1, (every, ts, every))
+            for t in range(ts.start, ts.stop):
+                add_squares(1, t)
+
+        w2_codes = sb("w2_codes", [P, N], U32)
+        w2_plane = sb("w2_plane", [P, N], U8)
         nc.vector.quantize_mx(out=w2_codes[:].bitcast(FP8X4), scales=w2_plane[:], in_=w2_bf[:].rearrange("p c j -> p (c j)"))
 
-        def dealt(acc, t0, t1):
-            return acc[:].rearrange("p (m t) -> p t m", t=PACK)[:, t0:t1, :]
-
-        z_banks = []
-        for h in range(HALVES):
-            y1, y01, y3, y2 = banks[h]
-            names = ("y1s", "y3s", "a", "b", "t23", "c", "aa", "bb", "cc")
-            y1s, y3s, a, b, t23, c, aa, bb, cc = [sb(f"{n}{h}", [P, PACK, P], F32) for n in names]
-            for t0, t1 in CHUNKS:
-                nc.scalar.activation(out=y1s[:, t0:t1, :], in_=dealt(y1, t0, t1), func=ACT.Copy, scale=2.0)
-                nc.scalar.copy(out=y3s[:, t0:t1, :], in_=dealt(y3, t0, t1))
-            zb = bank(f"z{h}", [P, PACK, P])
-            for t0, t1 in CHUNKS:
-                ts = slice(t0, t1)
-                nc.vector.tensor_tensor(out=t23[:, ts, :], in0=dealt(y2, t0, t1), in1=y3s[:, ts, :], op=ALU.add)
-                nc.vector.tensor_tensor(out=a[:, ts, :], in0=dealt(y01, t0, t1), in1=y1s[:, ts, :], op=ALU.subtract)
-                nc.vector.tensor_tensor(out=c[:, ts, :], in0=dealt(y01, t0, t1), in1=t23[:, ts, :], op=ALU.subtract)
-                nc.vector.tensor_tensor(out=b[:, ts, :], in0=dealt(y2, t0, t1), in1=y3s[:, ts, :], op=ALU.subtract)
-                nc.scalar.activation(out=aa[:, ts, :], in_=a[:, ts, :], func=ACT.Square, scale=math.sqrt(0.125))
-                nc.scalar.activation(out=cc[:, ts, :], in_=c[:, ts, :], func=ACT.Square, scale=0.25)
-                nc.scalar.activation(out=bb[:, ts, :], in_=b[:, ts, :], func=ACT.Square, scale=math.sqrt(0.125))
-                for t in range(t0, t1):
-                    for i, sq in enumerate((aa, cc, bb)):
-                        nc.tensor.matmul(out=zb[:, t, :], lhsT=sq[:, t, :], rhs=ident[:], is_transpose=True, start=(i == 0), stop=(i == 2))
-            z_banks.append(zb)
-
-        result = sb("result", [P, V // D], F32)
         groups = P // D
+        scores = []
         for h in range(HALVES):
             z_bf = sb(f"z_bf{h}", [P, P, PACK], BF16)
             nc.vector.tensor_tensor(
@@ -151,16 +207,26 @@ def tile_picked_ymvs_mean_p_kernel(tc, x_words, x_scales, w1, unit, w2, depth, o
                 out=sc[:].rearrange("p g d -> p (g d)"), lhsT=w2_codes[:].bitcast(FP8X4), lhsT_scale=w2_plane[:],
                 rhs=z_codes[:].bitcast(FP8X4), rhs_scale=z_plane[:], start=True, stop=True,
             )
+            scores.append(sc)
+
+        result = sb("result", [P, V // D], F32)
+        for h in reversed(range(HALVES)):
+            sc = scores[h]
             top = sb(f"top{h}", [P, groups], F32)
             nc.vector.tensor_reduce(out=top[:], in_=sc[:], axis=AXIS_X, op=ALU.max)
             shifted = sb(f"shifted{h}", [P, groups, D], F32)
             nc.vector.tensor_tensor(out=shifted[:], in0=sc[:], in1=top[:].unsqueeze(2).to_broadcast([P, groups, D]), op=ALU.subtract)
-            both = sb(f"both{h}", [P, 2, P], F32)
-            nc.scalar.activation(out=both[:, 0, :], in_=shifted[:].rearrange("p g d -> p (g d)"), func=ACT.Exp)
-            nc.vector.tensor_tensor(out=both[:, 1, :], in0=both[:, 0, :], in1=depth_sb[:, h * P : (h + 1) * P], op=ALU.mult)
-            sums = sb(f"sums{h}", [P, 2, groups], F32)
-            nc.vector.tensor_reduce(out=sums[:].rearrange("p s g -> p (s g)"), in_=both[:].rearrange("p s (g d) -> p (s g) d", d=D), axis=AXIS_X, op=ALU.add)
+            ex = sb(f"ex{h}", [P, groups, D], F32)
+            nc.scalar.activation(out=ex[:], in_=shifted[:], func=ACT.Exp)
+            total = sb(f"total{h}", [P, groups], F32)
+            nc.vector.tensor_reduce(out=total[:], in_=ex[:], axis=AXIS_X, op=ALU.add)
+            weighted = sb(f"weighted{h}", [P, groups, D], F32)
+            nc.vector.tensor_tensor(
+                out=weighted[:], in0=ex[:], in1=depth_sb[:, h * P : (h + 1) * P].rearrange("p (g d) -> p g d", d=D), op=ALU.mult
+            )
             inv = sb(f"inv{h}", [P, groups], F32)
-            nc.vector.reciprocal(out=inv[:], in_=sums[:, 0, :])
-            nc.vector.tensor_tensor(out=result[:, h * groups : (h + 1) * groups], in0=sums[:, 1, :], in1=inv[:], op=ALU.mult)
+            nc.vector.reciprocal(out=inv[:], in_=total[:])
+            wsum = sb(f"wsum{h}", [P, groups], F32)
+            nc.vector.tensor_reduce(out=wsum[:], in_=weighted[:], axis=AXIS_X, op=ALU.add)
+            nc.vector.tensor_tensor(out=result[:, h * groups : (h + 1) * groups], in0=wsum[:], in1=inv[:], op=ALU.mult)
         nc.sync.dma_start(out=out, in_=result[:])

@@ -39,25 +39,25 @@ def tile_picked_ymvs_mean_p_kernel(tc, x_words, x_scales, w1, unit, w2, depth, o
         offsets = keep.tile([P, S // 16], U16, name="offsets")
         nc.sync.dma_start(offsets[:], offs)
 
+        unit_raw = sb("unit_raw", [P, PACK], F32)
+        nc.sync.dma_start(out=unit_raw[:], in_=unit.rearrange("(p t) o -> p (t o)", t=PACK))
+
         scale_table = sb("scale_table", [P, T], U8)
-        nc.sync.dma_start(out=scale_table[:].bitcast(I32)[16:32, :], in_=x_scales[0].bitcast(I32))
-        for p0, p1 in ((0, 16), (32, 64), (64, P)):
-            nc.vector.memset(scale_table[:].bitcast(I32)[p0:p1, :], 0)
+        nc.scalar.dma_start(out=scale_table[:].bitcast(I32)[P - 16 : P, :], in_=x_scales[0].bitcast(I32))
+        nc.vector.memset(scale_table[:].bitcast(I32)[0 : P - 16, :], 0)
         x_plane = sb("x_plane", [P, S], U8)
         nc.vector.memset(x_plane[:].bitcast(I32), 0)
 
         w1_rows = w1.rearrange("(p j) c -> p j c", j=PACK)
-        w1_raw = [sb(f"w1_raw{g}", [P, PACK, HALF], F32) for g in range(2)]
+        w1_raw = [keep.tile([P, PACK, HALF], F32, name=f"w1_raw{g}", tag=f"staging{g}", align_bytes=64) for g in range(2)]
         word_table = sb("word_table", [P, T], I32)
-        nc.scalar.dma_start(out=w1_raw[0][:], in_=w1_rows[:, :, 0:HALF])
         nc.scalar.dma_start(out=word_table[:], in_=x_words[0].rearrange("p n t -> p (n t)").bitcast(I32))
+        nc.scalar.dma_start(out=w1_raw[0][:], in_=w1_rows[:, :, 0:HALF])
         nc.scalar.dma_start(out=w1_raw[1][:], in_=w1_rows[:, :, HALF:H])
         w2_raw = sb("w2_raw", [P, PACK, N], F32)
         nc.scalar.dma_start(out=w2_raw[:], in_=w2.rearrange("(p j) c -> p j c", j=PACK))
-        depth_sb = sb("depth_sb", [P, V], F32)
-        nc.scalar.dma_start(out=depth_sb[:], in_=depth)
         unit_sb = sb("unit_sb", [P, PACK], F32)
-        nc.gpsimd.dma_start(out=unit_sb[:], in_=unit.rearrange("(p t) o -> p (t o)", t=PACK))
+        nc.scalar.activation(out=unit_sb[:], in_=unit_raw[:], func=ACT.Copy, scale=1.0 / 16)
 
         ident = sb("ident", [P, P], F32)
         make_identity(nc, ident[:])
@@ -71,7 +71,7 @@ def tile_picked_ymvs_mean_p_kernel(tc, x_words, x_scales, w1, unit, w2, depth, o
         )
         for q in range(4):
             nc.sync.dma_start(
-                out=x_plane[:].bitcast(I32)[32 * q : 32 * q + 4, :], in_=scales_by_view[:].bitcast(I32)[16 + 4 * q : 20 + 4 * q, :]
+                out=x_plane[:].bitcast(I32)[32 * q : 32 * q + 4, :], in_=scales_by_view[:].bitcast(I32)[P - 16 + 4 * q : P - 12 + 4 * q, :]
             )
 
         w1_codes = sb("w1_codes", [P, H], U32)
@@ -79,9 +79,13 @@ def tile_picked_ymvs_mean_p_kernel(tc, x_words, x_scales, w1, unit, w2, depth, o
 
         def quantize_w1(g):
             cols = slice(g * HALF, (g + 1) * HALF)
-            grouped = keep.tile([P, HALF, PACK], BF16, name=f"w1_bf{g}", tag="weights_bf", align_bytes=64)
-            nc.scalar.activation(out=grouped[:], in_=w1_raw[g][:].rearrange("p j c -> p c j"), func=ACT.Copy)
-            nc.vector.quantize_mx(out=w1_codes[:, cols].bitcast(FP8X4), scales=w1_plane[:, cols], in_=grouped[:].rearrange("p c j -> p (c j)"))
+            grouped = sb(f"w1_bf{g}", [P, HALF, PACK], BF16)
+            dst = grouped[:].rearrange("p (c i) j -> p c j i", i=4)
+            src = w1_raw[g][:].rearrange("p j (c i) -> p c j i", i=4)
+            nc.scalar.activation(out=dst, in_=src, func=ACT.Copy)
+            nc.vector.quantize_mx(
+                out=w1_codes[:, cols].bitcast(FP8X4), scales=w1_plane[:, cols], in_=grouped[:].rearrange("p c j -> p (c j)")
+            )
 
         entries = S // HALVES
 
@@ -107,10 +111,13 @@ def tile_picked_ymvs_mean_p_kernel(tc, x_words, x_scales, w1, unit, w2, depth, o
             product(y01, h, 0, cols, False, True)
             product(y2, h, 2, cols, True, True)
 
+        x_codes = [gather_words(h) for h in range(HALVES)]
         quantize_w1(0)
-        x_codes = [gather_words(0)]
         quantize_w1(1)
-        x_codes.append(gather_words(1))
+        depth_sb = keep.tile([P, V], F32, name="depth_sb", tag="staging0", align_bytes=64)
+        nc.sync.dma_start(out=depth_sb[:], in_=depth)
+        w2_bf = sb("w2_bf", [P, N, PACK], BF16)
+        nc.vector.tensor_copy(out=w2_bf[:].rearrange("p (c i) j -> p c j i", i=4), in_=w2_raw[:].rearrange("p j (c i) -> p c j i", i=4))
 
         odd, even = [], []
         for g in range(2):
@@ -120,20 +127,18 @@ def tile_picked_ymvs_mean_p_kernel(tc, x_words, x_scales, w1, unit, w2, depth, o
         y1, y3, y01, y2 = [bank(n, [P, H]) for n in ("y1", "y3", "y01", "y2")]
         products(1, slice(0, H), y1[:], y3[:], y01[:], y2[:])
 
-        w2_bf = keep.tile([P, N, PACK], BF16, name="w2_bf", tag="weights_bf", align_bytes=64)
-        nc.gpsimd.tensor_scalar(out=w2_bf[:], in0=w2_raw[:].rearrange("p j c -> p c j"), scalar1=1.0, scalar2=0.0, op0=ALU.mult, op1=ALU.add)
-
         copied = [sb(f"copied{h}", [P, 2, PACK, P], F32) for h in range(HALVES)]
         ab = [sb(f"ab{h}", [P, 2, PACK, P], F32) for h in range(HALVES)]
         y23 = [sb(f"y23_{h}", [P, PACK, P], F32) for h in range(HALVES)]
         c = [sb(f"c{h}", [P, PACK, P], F32) for h in range(HALVES)]
         ab_sq = [sb(f"ab_sq{h}", [P, 2, PACK, P], F32) for h in range(HALVES)]
         c_sq = [sb(f"c_sq{h}", [P, PACK, P], F32) for h in range(HALVES)]
-        z_banks = [bank(f"z{h}", [P, PACK, P]) for h in range(HALVES)]
+        z0 = bank("z0", [P, PACK, P])
+        z1 = [bank(f"z1_{u}", [P, 2, P]) for u in range(2)]
 
         def add_squares(h, t):
-            for i, sq in enumerate((ab_sq[h][:, 0, t, :], ab_sq[h][:, 1, t, :], c_sq[h][:, t, :])):
-                nc.tensor.matmul(out=z_banks[h][:, t, :], lhsT=sq, rhs=ident[:], is_transpose=True, start=(i == 0), stop=(i == 2))
+            for i, sq in enumerate((ab_sq[h][:, 1, t, :], c_sq[h][:, t, :], ab_sq[h][:, 0, t, :])):
+                nc.tensor.matmul(out=z0[:, t, :] if h == 0 else z1[t // 2][:, t % 2, :], lhsT=sq, rhs=ident[:], is_transpose=True, start=(i == 0), stop=(i == 2))
 
         for g in range(2):
             ms = slice(g * HALF // PACK, (g + 1) * HALF // PACK)
@@ -149,10 +154,10 @@ def tile_picked_ymvs_mean_p_kernel(tc, x_words, x_scales, w1, unit, w2, depth, o
             return acc[:].rearrange("p (m t) -> p t m", t=PACK)[:, ts, :]
 
         def square_ab(h, where):
-            nc.scalar.activation(out=ab_sq[h][where], in_=ab[h][where], func=ACT.Square, scale=math.sqrt(0.125))
+            nc.scalar.activation(out=ab_sq[h][where], in_=ab[h][where], func=ACT.Square, scale=math.sqrt(2.0))
 
         def square_c(h, where):
-            nc.scalar.activation(out=c_sq[h][where], in_=c[h][where], func=ACT.Square, scale=0.25)
+            nc.scalar.activation(out=c_sq[h][where], in_=c[h][where], func=ACT.Square)
 
         def copy_odd_views(ts):
             nc.scalar.copy(out=copied[1][:, 1, ts, :], in_=dealt(y3, ts))
@@ -172,18 +177,22 @@ def tile_picked_ymvs_mean_p_kernel(tc, x_words, x_scales, w1, unit, w2, depth, o
                 add_squares(0, t)
         for ts in (first, second):
             nc.vector.tensor_tensor(out=y23[1][:, ts, :], in0=dealt(y2, ts), in1=copied[1][:, 1, ts, :], op=ALU.add)
-            nc.vector.tensor_tensor(out=ab[1][:, 0, ts, :], in0=dealt(y01, ts), in1=copied[1][:, 0, ts, :], op=ALU.subtract)
             nc.vector.tensor_tensor(out=ab[1][:, 1, ts, :], in0=dealt(y2, ts), in1=copied[1][:, 1, ts, :], op=ALU.subtract)
             nc.vector.tensor_tensor(out=c[1][:, ts, :], in0=dealt(y01, ts), in1=y23[1][:, ts, :], op=ALU.subtract)
             if ts == first:
+                nc.vector.tensor_tensor(out=ab[1][:, 0, ts, :], in0=dealt(y01, ts), in1=copied[1][:, 0, ts, :], op=ALU.subtract)
                 square_ab(1, (every, every, ts, every))
+                square_c(1, (every, ts, every))
             else:
-                square_ab(1, (every, 0, ts, every))
+                square_ab(1, (every, 1, ts, every))
+                square_c(1, (every, ts, every))
+                for t in range(ts.start, ts.stop):
+                    one = slice(t, t + 1)
+                    nc.vector.tensor_tensor(out=ab[1][:, 0, one, :], in0=dealt(y01, one), in1=copied[1][:, 0, one, :], op=ALU.subtract)
                 for t in range(ts.start, ts.stop):
                     nc.vector.scalar_tensor_tensor(
-                        out=ab_sq[1][:, 1, t, :], in0=ab[1][:, 1, t, :], scalar=0.125, in1=ab[1][:, 1, t, :], op0=ALU.mult, op1=ALU.mult
+                        out=ab_sq[1][:, 0, t, :], in0=ab[1][:, 0, t, :], scalar=2.0, in1=ab[1][:, 0, t, :], op0=ALU.mult, op1=ALU.mult
                     )
-            square_c(1, (every, ts, every))
             for t in range(ts.start, ts.stop):
                 add_squares(1, t)
 
@@ -191,42 +200,65 @@ def tile_picked_ymvs_mean_p_kernel(tc, x_words, x_scales, w1, unit, w2, depth, o
         w2_plane = sb("w2_plane", [P, N], U8)
         nc.vector.quantize_mx(out=w2_codes[:].bitcast(FP8X4), scales=w2_plane[:], in_=w2_bf[:].rearrange("p c j -> p (c j)"))
 
-        groups = P // D
-        scores = []
-        for h in range(HALVES):
-            z_bf = sb(f"z_bf{h}", [P, P, PACK], BF16)
+        z_bf = sb("z_bf", [P, V, PACK], BF16)
+
+        def scale_z(acc, v0, vs, ts):
+            width = vs.stop - vs.start
             nc.vector.tensor_tensor(
-                out=z_bf[:], in0=z_banks[h][:].rearrange("p t v -> p v t"),
-                in1=unit_sb[:].unsqueeze(1).to_broadcast([P, P, PACK]), op=ALU.mult,
+                out=z_bf[:, v0 + vs.start : v0 + vs.stop, ts], in0=acc[:, :, vs].rearrange("p t v -> p v t"),
+                in1=unit_sb[:, ts].unsqueeze(1).to_broadcast([P, width, ts.stop - ts.start]), op=ALU.mult,
             )
-            z_codes = sb(f"z_codes{h}", [P, P], U32)
-            z_plane = sb(f"z_plane{h}", [P, P], U8)
-            nc.vector.quantize_mx(out=z_codes[:].bitcast(FP8X4), scales=z_plane[:], in_=z_bf[:].rearrange("p v t -> p (v t)"))
-            sc = bank(f"sc{h}", [P, groups, D])
+
+        def costs(v0, v1):
+            z_codes = sb(f"z_codes{v0}", [P, v1 - v0], U32)
+            z_plane = sb(f"z_plane{v0}", [P, v1 - v0], U8)
+            nc.vector.quantize_mx(out=z_codes[:].bitcast(FP8X4), scales=z_plane[:], in_=z_bf[:, v0:v1, :].rearrange("p v t -> p (v t)"))
+            sc = bank(f"sc{v0}", [P, (v1 - v0) // D, D])
             nc.tensor.matmul_mx(
                 out=sc[:].rearrange("p g d -> p (g d)"), lhsT=w2_codes[:].bitcast(FP8X4), lhsT_scale=w2_plane[:],
                 rhs=z_codes[:].bitcast(FP8X4), rhs_scale=z_plane[:], start=True, stop=True,
             )
-            scores.append(sc)
+            return sc
+
+        scale_z(z1[0], P, slice(0, P), first)
+        scale_z(z0, 0, slice(0, P), slice(0, PACK))
+        pieces = [(0, P), (P, P + P // 2), (P + P // 2, V)]
+        scores = [costs(0, P)]
+        scale_z(z1[1], P, low, second)
+        scale_z(z1[1], P, high, second)
+        scores.extend(costs(v0, v1) for v0, v1 in pieces[1:])
 
         result = sb("result", [P, V // D], F32)
-        for h in reversed(range(HALVES)):
-            sc = scores[h]
-            top = sb(f"top{h}", [P, groups], F32)
-            nc.vector.tensor_reduce(out=top[:], in_=sc[:], axis=AXIS_X, op=ALU.max)
-            shifted = sb(f"shifted{h}", [P, groups, D], F32)
-            nc.vector.tensor_tensor(out=shifted[:], in0=sc[:], in1=top[:].unsqueeze(2).to_broadcast([P, groups, D]), op=ALU.subtract)
-            ex = sb(f"ex{h}", [P, groups, D], F32)
-            nc.scalar.activation(out=ex[:], in_=shifted[:], func=ACT.Exp)
-            total = sb(f"total{h}", [P, groups], F32)
-            nc.vector.tensor_reduce(out=total[:], in_=ex[:], axis=AXIS_X, op=ALU.add)
-            weighted = sb(f"weighted{h}", [P, groups, D], F32)
-            nc.vector.tensor_tensor(
-                out=weighted[:], in0=ex[:], in1=depth_sb[:, h * P : (h + 1) * P].rearrange("p (g d) -> p g d", d=D), op=ALU.mult
-            )
-            inv = sb(f"inv{h}", [P, groups], F32)
-            nc.vector.reciprocal(out=inv[:], in_=total[:])
-            wsum = sb(f"wsum{h}", [P, groups], F32)
-            nc.vector.tensor_reduce(out=wsum[:], in_=weighted[:], axis=AXIS_X, op=ALU.add)
-            nc.vector.tensor_tensor(out=result[:, h * groups : (h + 1) * groups], in0=wsum[:], in1=inv[:], op=ALU.mult)
+
+        def soft_depth(which):
+            tiles = {}
+            for i in which:
+                groups = (pieces[i][1] - pieces[i][0]) // D
+                wide = [sb(f"{n}{i}", [P, groups, D], F32) for n in ("shifted", "ex", "weighted")]
+                narrow = [sb(f"{n}{i}", [P, groups], F32) for n in ("top", "total", "inv", "wsum")]
+                tiles[i] = [groups] + wide + narrow
+            for stage in range(8):
+                for i in which:
+                    v0, v1 = pieces[i]
+                    sc = scores[i]
+                    groups, shifted, ex, weighted, top, total, inv, wsum = tiles[i]
+                    if stage == 0:
+                        nc.vector.tensor_reduce(out=top[:], in_=sc[:], axis=AXIS_X, op=ALU.max)
+                    elif stage == 1:
+                        nc.vector.tensor_tensor(out=shifted[:], in0=sc[:], in1=top[:].unsqueeze(2).to_broadcast([P, groups, D]), op=ALU.subtract)
+                    elif stage == 2:
+                        nc.scalar.activation(out=ex[:], in_=shifted[:], func=ACT.Exp)
+                    elif stage == 3:
+                        nc.vector.tensor_reduce(out=total[:], in_=ex[:], axis=AXIS_X, op=ALU.add)
+                    elif stage == 4:
+                        nc.vector.tensor_tensor(out=weighted[:], in0=ex[:], in1=depth_sb[:, v0:v1].rearrange("p (g d) -> p g d", d=D), op=ALU.mult)
+                    elif stage == 5:
+                        nc.vector.reciprocal(out=inv[:], in_=total[:])
+                    elif stage == 6:
+                        nc.vector.tensor_reduce(out=wsum[:], in_=weighted[:], axis=AXIS_X, op=ALU.add)
+                    else:
+                        nc.vector.tensor_tensor(out=result[:, v0 // D : v1 // D], in0=wsum[:], in1=inv[:], op=ALU.mult)
+
+        soft_depth([1, 2])
+        soft_depth([0])
         nc.sync.dma_start(out=out, in_=result[:])

@@ -20,15 +20,22 @@ AXIS_X = mybir.AxisListType.X
 
 P = 128
 PACK = 4
+BLOCKS = K // 32
+QUADRANTS = 4
+BANKS = 8
 HALVES = V // P
-HALF = H // 2
+ENTRIES = S // HALVES
+WIDE = H // 2
+LINE = 4
+SCALAR_SHARE = 24
+A, B, C = 0, 1, 2
 
 
 def tile_picked_ymvs_mean_p_kernel(tc, x_words, x_scales, w1, unit, w2, depth, offs, out):
     nc = tc.nc
     with ExitStack() as ctx:
         keep = ctx.enter_context(tc.tile_pool(name="keep", bufs=1))
-        psum = ctx.enter_context(tc.psum_pool(name="psum", bufs=8))
+        psum = ctx.enter_context(tc.psum_pool(name="psum", bufs=BANKS))
 
         def sb(name, shape, dtype):
             return keep.tile(shape, dtype, name=name, align_bytes=64)
@@ -42,22 +49,23 @@ def tile_picked_ymvs_mean_p_kernel(tc, x_words, x_scales, w1, unit, w2, depth, o
         unit_raw = sb("unit_raw", [P, PACK], F32)
         nc.sync.dma_start(out=unit_raw[:], in_=unit.rearrange("(p t) o -> p (t o)", t=PACK))
 
+        first_row = P - BLOCKS
         scale_table = sb("scale_table", [P, T], U8)
-        nc.scalar.dma_start(out=scale_table[:].bitcast(I32)[P - 16 : P, :], in_=x_scales[0].bitcast(I32))
-        nc.vector.memset(scale_table[:].bitcast(I32)[0 : P - 16, :], 0)
+        nc.scalar.dma_start(out=scale_table[:].bitcast(I32)[first_row:P, :], in_=x_scales[0].bitcast(I32))
+        nc.vector.memset(scale_table[:].bitcast(I32)[0:first_row, :], 0)
         x_plane = sb("x_plane", [P, S], U8)
         nc.vector.memset(x_plane[:].bitcast(I32), 0)
 
         w1_rows = w1.rearrange("(p j) c -> p j c", j=PACK)
-        w1_raw = [keep.tile([P, PACK, HALF], F32, name=f"w1_raw{g}", tag=f"staging{g}", align_bytes=64) for g in range(2)]
+        w1_raw = [keep.tile([P, PACK, WIDE], F32, name=f"w1_raw{g}", tag=f"staging{g}", align_bytes=64) for g in range(2)]
         word_table = sb("word_table", [P, T], I32)
         nc.scalar.dma_start(out=word_table[:], in_=x_words[0].rearrange("p n t -> p (n t)").bitcast(I32))
-        nc.scalar.dma_start(out=w1_raw[0][:], in_=w1_rows[:, :, 0:HALF])
-        nc.scalar.dma_start(out=w1_raw[1][:], in_=w1_rows[:, :, HALF:H])
+        nc.scalar.dma_start(out=w1_raw[0][:], in_=w1_rows[:, :, 0:WIDE])
+        nc.scalar.dma_start(out=w1_raw[1][:], in_=w1_rows[:, :, WIDE:H])
         w2_raw = sb("w2_raw", [P, PACK, N], F32)
         nc.scalar.dma_start(out=w2_raw[:], in_=w2.rearrange("(p j) c -> p j c", j=PACK))
         unit_sb = sb("unit_sb", [P, PACK], F32)
-        nc.scalar.activation(out=unit_sb[:], in_=unit_raw[:], func=ACT.Copy, scale=1.0 / 16)
+        nc.scalar.activation(out=unit_sb[:], in_=unit_raw[:], func=ACT.Copy, scale=1.0 / (D * D))
 
         ident = sb("ident", [P, P], F32)
         make_identity(nc, ident[:])
@@ -69,132 +77,112 @@ def tile_picked_ymvs_mean_p_kernel(tc, x_words, x_scales, w1, unit, w2, depth, o
             out=scales_by_view[:].rearrange("p (h d v) -> p h d v", h=HALVES, d=D),
             in_=picked_scales[:].rearrange("p (h v d) -> p h d v", h=HALVES, d=D),
         )
-        for q in range(4):
+        for q in range(QUADRANTS):
             nc.sync.dma_start(
-                out=x_plane[:].bitcast(I32)[32 * q : 32 * q + 4, :], in_=scales_by_view[:].bitcast(I32)[P - 16 + 4 * q : P - 12 + 4 * q, :]
+                out=x_plane[:].bitcast(I32)[32 * q : 32 * q + 4, :],
+                in_=scales_by_view[:].bitcast(I32)[first_row + 4 * q : first_row + 4 * q + 4, :],
             )
-
-        w1_codes = sb("w1_codes", [P, H], U32)
-        w1_plane = sb("w1_plane", [P, H], U8)
-
-        def quantize_w1(g):
-            cols = slice(g * HALF, (g + 1) * HALF)
-            grouped = sb(f"w1_bf{g}", [P, HALF, PACK], BF16)
-            dst = grouped[:].rearrange("p (c i) j -> p c j i", i=4)
-            src = w1_raw[g][:].rearrange("p j (c i) -> p c j i", i=4)
-            nc.scalar.activation(out=dst, in_=src, func=ACT.Copy)
-            nc.vector.quantize_mx(
-                out=w1_codes[:, cols].bitcast(FP8X4), scales=w1_plane[:, cols], in_=grouped[:].rearrange("p c j -> p (c j)")
-            )
-
-        entries = S // HALVES
 
         def gather_words(h):
             codes = sb(f"x_codes{h}", [P, D, P], U32)
             nc.vector.tensor_copy(
                 codes[:].rearrange("p d v -> p v d"),
-                word_table[:].bitcast(U32).indirect(offsets[:, h * entries // 16 : (h + 1) * entries // 16]),
+                word_table[:].bitcast(U32).indirect(offsets[:, h * ENTRIES // 16 : (h + 1) * ENTRIES // 16]),
             )
             return codes
 
-        def product(acc, h, d, cols, start, stop):
-            c0 = h * entries + d * P
+        x_codes = [gather_words(h) for h in range(HALVES)]
+
+        w1_codes = sb("w1_codes", [P, H], U32)
+        w1_plane = sb("w1_plane", [P, H], U8)
+        w1_bf = sb("w1_bf", [P, PACK, P, PACK], BF16)
+        groups_in_half = WIDE // PACK
+
+        def deal_w1(copy, g, m0, m1):
+            base = g * groups_in_half
+            copy(
+                out=w1_bf[:, :, base + m0 : base + m1, :].rearrange("p t m j -> p m t j"),
+                in_=w1_raw[g][:].rearrange("p j (m t) -> p m t j", t=PACK)[:, m0:m1],
+            )
+
+        deal_w1(nc.scalar.copy, 0, 0, groups_in_half)
+        deal_w1(nc.scalar.copy, 1, 0, SCALAR_SHARE)
+        deal_w1(nc.vector.tensor_copy, 1, SCALAR_SHARE, groups_in_half)
+        for u in range(2):
+            cols = slice(u * WIDE, (u + 1) * WIDE)
+            nc.vector.quantize_mx(
+                out=w1_codes[:, cols].bitcast(FP8X4), scales=w1_plane[:, cols],
+                in_=w1_bf[:, 2 * u : 2 * u + 2].rearrange("p t m j -> p (t m j)"),
+            )
+
+        depth_sb = keep.tile([P, V], F32, name="depth_sb", tag="staging0", align_bytes=64)
+        nc.sync.dma_start(out=depth_sb[:], in_=depth)
+        w2_bf = sb("w2_bf", [P, N, PACK], BF16)
+        nc.vector.tensor_copy(
+            out=w2_bf[:].rearrange("p (c i) j -> p c j i", i=LINE), in_=w2_raw[:].rearrange("p j (c i) -> p c j i", i=LINE)
+        )
+
+        def product(acc, h, d, u, start, stop):
+            c0 = h * ENTRIES + d * P
+            cols = slice(u * WIDE, (u + 1) * WIDE)
             nc.tensor.matmul_mx(
                 out=acc, lhsT=x_codes[h][:, d, :].bitcast(FP8X4), lhsT_scale=x_plane[:, c0 : c0 + P],
                 rhs=w1_codes[:, cols].bitcast(FP8X4), rhs_scale=w1_plane[:, cols], start=start, stop=stop,
             )
 
-        def products(h, cols, y1, y3, y01, y2):
-            product(y1, h, 1, cols, True, True)
-            product(y3, h, 3, cols, True, True)
-            product(y01, h, 1, cols, True, False)
-            product(y01, h, 0, cols, False, True)
-            product(y2, h, 2, cols, True, True)
+        steps = [(h, u) for h in range(HALVES) for u in range(2)]
+        for_scalar, for_vector = {}, {}
+        for h, u in steps:
+            sbank = for_scalar[h, u] = bank(f"for_scalar{h}{u}", [P, 2, WIDE])
+            vbank = for_vector[h, u] = bank(f"for_vector{h}{u}", [P, 2, WIDE])
+            product(sbank[:, 1, :], h, 3, u, True, True)
+            product(sbank[:, 0, :], h, 0, u, True, False)
+            product(sbank[:, 0, :], h, 1, u, False, True)
+            product(vbank[:, 0, :], h, 1, u, True, True)
+            product(vbank[:, 1, :], h, 2, u, True, True)
 
-        x_codes = [gather_words(h) for h in range(HALVES)]
-        quantize_w1(0)
-        quantize_w1(1)
-        depth_sb = keep.tile([P, V], F32, name="depth_sb", tag="staging0", align_bytes=64)
-        nc.sync.dma_start(out=depth_sb[:], in_=depth)
-        w2_bf = sb("w2_bf", [P, N, PACK], BF16)
-        nc.vector.tensor_copy(out=w2_bf[:].rearrange("p (c i) j -> p c j i", i=4), in_=w2_raw[:].rearrange("p j (c i) -> p c j i", i=4))
+        sums0 = bank("sums0", [P, PACK, P])
+        sums1 = [bank(f"sums1_{u}", [P, 2, P]) for u in range(2)]
 
-        odd, even = [], []
-        for g in range(2):
-            odd.append(bank(f"odd{g}", [P, 2, HALF]))
-            even.append(bank(f"even{g}", [P, 2, HALF]))
-            products(0, slice(g * HALF, (g + 1) * HALF), odd[g][:, 0, :], odd[g][:, 1, :], even[g][:, 0, :], even[g][:, 1, :])
-        y1, y3, y01, y2 = [bank(n, [P, H]) for n in ("y1", "y3", "y01", "y2")]
-        products(1, slice(0, H), y1[:], y3[:], y01[:], y2[:])
+        def copy_out(step):
+            copied = sb(f"copied{step[0]}{step[1]}", [P, 2, WIDE], F32)
+            nc.scalar.copy(out=copied[:], in_=for_scalar[step][:])
+            y01_less_y3 = sb(f"y01_less_y3_{step[0]}{step[1]}", [P, WIDE], F32)
+            nc.vector.tensor_tensor(out=y01_less_y3[:], in0=copied[:, 0, :], in1=copied[:, 1, :], op=ALU.subtract)
+            return copied, y01_less_y3
 
-        copied = [sb(f"copied{h}", [P, 2, PACK, P], F32) for h in range(HALVES)]
-        ab = [sb(f"ab{h}", [P, 2, PACK, P], F32) for h in range(HALVES)]
-        y23 = [sb(f"y23_{h}", [P, PACK, P], F32) for h in range(HALVES)]
-        c = [sb(f"c{h}", [P, PACK, P], F32) for h in range(HALVES)]
-        ab_sq = [sb(f"ab_sq{h}", [P, 2, PACK, P], F32) for h in range(HALVES)]
-        c_sq = [sb(f"c_sq{h}", [P, PACK, P], F32) for h in range(HALVES)]
-        z0 = bank("z0", [P, PACK, P])
-        z1 = [bank(f"z1_{u}", [P, 2, P]) for u in range(2)]
-
-        def add_squares(h, t):
-            for i, sq in enumerate((ab_sq[h][:, 1, t, :], c_sq[h][:, t, :], ab_sq[h][:, 0, t, :])):
-                nc.tensor.matmul(out=z0[:, t, :] if h == 0 else z1[t // 2][:, t % 2, :], lhsT=sq, rhs=ident[:], is_transpose=True, start=(i == 0), stop=(i == 2))
-
-        for g in range(2):
-            ms = slice(g * HALF // PACK, (g + 1) * HALF // PACK)
-            odd_t = odd[g][:].rearrange("p s (m t) -> p s t m", t=PACK)
-            even_t = even[g][:].rearrange("p s (m t) -> p s t m", t=PACK)
-            nc.scalar.copy(out=copied[0][:, 1, :, ms], in_=odd_t[:, 1])
-            nc.scalar.activation(out=copied[0][:, 0, :, ms], in_=odd_t[:, 0], func=ACT.Copy, scale=2.0)
-            nc.vector.tensor_tensor(out=y23[0][:, :, ms], in0=even_t[:, 1], in1=copied[0][:, 1, :, ms], op=ALU.add)
-            nc.vector.tensor_tensor(out=ab[0][:, :, :, ms], in0=even_t, in1=copied[0][:, :, :, ms], op=ALU.subtract)
-            nc.vector.tensor_tensor(out=c[0][:, :, ms], in0=even_t[:, 0], in1=y23[0][:, :, ms], op=ALU.subtract)
-
-        def dealt(acc, ts):
-            return acc[:].rearrange("p (m t) -> p t m", t=PACK)[:, ts, :]
-
-        def square_ab(h, where):
-            nc.scalar.activation(out=ab_sq[h][where], in_=ab[h][where], func=ACT.Square, scale=math.sqrt(2.0))
-
-        def square_c(h, where):
-            nc.scalar.activation(out=c_sq[h][where], in_=c[h][where], func=ACT.Square)
-
-        def copy_odd_views(ts):
-            nc.scalar.copy(out=copied[1][:, 1, ts, :], in_=dealt(y3, ts))
-            nc.scalar.activation(out=copied[1][:, 0, ts, :], in_=dealt(y1, ts), func=ACT.Copy, scale=2.0)
-
-        every = slice(None)
-        first, second = slice(0, 2), slice(2, 4)
-        low, high = slice(0, P // 2), slice(P // 2, P)
-        copy_odd_views(first)
-        square_ab(0, (every, every, every, low))
-        square_c(0, (every, every, low))
-        copy_odd_views(second)
-        for ts in (first, second):
-            square_ab(0, (every, every, ts, high))
-            square_c(0, (every, ts, high))
-            for t in range(ts.start, ts.stop):
-                add_squares(0, t)
-        for ts in (first, second):
-            nc.vector.tensor_tensor(out=y23[1][:, ts, :], in0=dealt(y2, ts), in1=copied[1][:, 1, ts, :], op=ALU.add)
-            nc.vector.tensor_tensor(out=ab[1][:, 1, ts, :], in0=dealt(y2, ts), in1=copied[1][:, 1, ts, :], op=ALU.subtract)
-            nc.vector.tensor_tensor(out=c[1][:, ts, :], in0=dealt(y01, ts), in1=y23[1][:, ts, :], op=ALU.subtract)
-            if ts == first:
-                nc.vector.tensor_tensor(out=ab[1][:, 0, ts, :], in0=dealt(y01, ts), in1=copied[1][:, 0, ts, :], op=ALU.subtract)
-                square_ab(1, (every, every, ts, every))
-                square_c(1, (every, ts, every))
+        def variance(step, copied, y01_less_y3):
+            h, u = step
+            y1, y2 = for_vector[step][:, 0, :], for_vector[step][:, 1, :]
+            contrasts = sb(f"contrasts{h}{u}", [P, 3, WIDE], F32)
+            squares = sb(f"squares{h}{u}", [P, 3, WIDE], F32)
+            nc.vector.tensor_tensor(out=contrasts[:, B, :], in0=y2, in1=copied[:, 1, :], op=ALU.subtract)
+            nc.vector.scalar_tensor_tensor(out=contrasts[:, A, :], in0=y1, scalar=-2.0, in1=copied[:, 0, :], op0=ALU.mult, op1=ALU.add)
+            nc.vector.tensor_tensor(out=contrasts[:, C, :], in0=y01_less_y3[:], in1=y2, op=ALU.subtract)
+            if step == steps[-1]:
+                nc.scalar.activation(out=squares[:, B, :], in_=contrasts[:, B, :], func=ACT.Square, scale=math.sqrt(2.0))
+                nc.vector.scalar_tensor_tensor(
+                    out=squares[:, A, :], in0=contrasts[:, A, :], scalar=2.0, in1=contrasts[:, A, :], op0=ALU.mult, op1=ALU.mult
+                )
+                for i in range(2):
+                    cols = slice(i * P, (i + 1) * P)
+                    nc.scalar.activation(out=squares[:, C, cols], in_=contrasts[:, C, cols], func=ACT.Square)
             else:
-                square_ab(1, (every, 1, ts, every))
-                square_c(1, (every, ts, every))
-                for t in range(ts.start, ts.stop):
-                    one = slice(t, t + 1)
-                    nc.vector.tensor_tensor(out=ab[1][:, 0, one, :], in0=dealt(y01, one), in1=copied[1][:, 0, one, :], op=ALU.subtract)
-                for t in range(ts.start, ts.stop):
-                    nc.vector.scalar_tensor_tensor(
-                        out=ab_sq[1][:, 0, t, :], in0=ab[1][:, 0, t, :], scalar=2.0, in1=ab[1][:, 0, t, :], op0=ALU.mult, op1=ALU.mult
+                nc.scalar.activation(out=squares[:, A:C, :], in_=contrasts[:, A:C, :], func=ACT.Square, scale=math.sqrt(2.0))
+                nc.scalar.activation(out=squares[:, C, :], in_=contrasts[:, C, :], func=ACT.Square)
+            for i in range(2):
+                acc = sums0[:, 2 * u + i, :] if h == 0 else sums1[u][:, i, :]
+                for which in (B, A, C):
+                    nc.tensor.matmul(
+                        out=acc, lhsT=squares[:, which, i * P : (i + 1) * P], rhs=ident[:],
+                        is_transpose=True, start=(which == B), stop=(which == C),
                     )
-            for t in range(ts.start, ts.stop):
-                add_squares(1, t)
+
+        ahead = [copy_out(steps[0]), copy_out(steps[1])]
+        for i, step in enumerate(steps):
+            if i + 2 < len(steps):
+                ahead.append(copy_out(steps[i + 2]))
+            variance(step, *ahead[i])
 
         w2_codes = sb("w2_codes", [P, N], U32)
         w2_plane = sb("w2_plane", [P, N], U8)
@@ -202,11 +190,10 @@ def tile_picked_ymvs_mean_p_kernel(tc, x_words, x_scales, w1, unit, w2, depth, o
 
         z_bf = sb("z_bf", [P, V, PACK], BF16)
 
-        def scale_z(acc, v0, vs, ts):
-            width = vs.stop - vs.start
+        def scale_z(acc, v0, v1, t0, t1):
             nc.vector.tensor_tensor(
-                out=z_bf[:, v0 + vs.start : v0 + vs.stop, ts], in0=acc[:, :, vs].rearrange("p t v -> p v t"),
-                in1=unit_sb[:, ts].unsqueeze(1).to_broadcast([P, width, ts.stop - ts.start]), op=ALU.mult,
+                out=z_bf[:, v0:v1, t0:t1], in0=acc.rearrange("p t v -> p v t"),
+                in1=unit_sb[:, t0:t1].unsqueeze(1).to_broadcast([P, v1 - v0, t1 - t0]), op=ALU.mult,
             )
 
         def costs(v0, v1):
@@ -220,45 +207,37 @@ def tile_picked_ymvs_mean_p_kernel(tc, x_words, x_scales, w1, unit, w2, depth, o
             )
             return sc
 
-        scale_z(z1[0], P, slice(0, P), first)
-        scale_z(z0, 0, slice(0, P), slice(0, PACK))
-        pieces = [(0, P), (P, P + P // 2), (P + P // 2, V)]
-        scores = [costs(0, P)]
-        scale_z(z1[1], P, low, second)
-        scale_z(z1[1], P, high, second)
-        scores.extend(costs(v0, v1) for v0, v1 in pieces[1:])
+        middle = P + P // 2
+        scale_z(sums1[0][:], P, V, 0, 2)
+        scale_z(sums0[:], 0, P, 0, PACK)
+        first_set = (0, P, costs(0, P))
+        scale_z(sums1[1][:, :, 0 : P // 2], P, middle, 2, PACK)
+        scale_z(sums1[1][:, :, P // 2 : P], middle, V, 2, PACK)
+        second_set = [(v0, v1, costs(v0, v1)) for v0, v1 in ((P, middle), (middle, V))]
 
         result = sb("result", [P, V // D], F32)
 
-        def soft_depth(which):
-            tiles = {}
-            for i in which:
-                groups = (pieces[i][1] - pieces[i][0]) // D
-                wide = [sb(f"{n}{i}", [P, groups, D], F32) for n in ("shifted", "ex", "weighted")]
-                narrow = [sb(f"{n}{i}", [P, groups], F32) for n in ("top", "total", "inv", "wsum")]
-                tiles[i] = [groups] + wide + narrow
-            for stage in range(8):
-                for i in which:
-                    v0, v1 = pieces[i]
-                    sc = scores[i]
-                    groups, shifted, ex, weighted, top, total, inv, wsum = tiles[i]
-                    if stage == 0:
-                        nc.vector.tensor_reduce(out=top[:], in_=sc[:], axis=AXIS_X, op=ALU.max)
-                    elif stage == 1:
-                        nc.vector.tensor_tensor(out=shifted[:], in0=sc[:], in1=top[:].unsqueeze(2).to_broadcast([P, groups, D]), op=ALU.subtract)
-                    elif stage == 2:
-                        nc.scalar.activation(out=ex[:], in_=shifted[:], func=ACT.Exp)
-                    elif stage == 3:
-                        nc.vector.tensor_reduce(out=total[:], in_=ex[:], axis=AXIS_X, op=ALU.add)
-                    elif stage == 4:
-                        nc.vector.tensor_tensor(out=weighted[:], in0=ex[:], in1=depth_sb[:, v0:v1].rearrange("p (g d) -> p g d", d=D), op=ALU.mult)
-                    elif stage == 5:
-                        nc.vector.reciprocal(out=inv[:], in_=total[:])
-                    elif stage == 6:
-                        nc.vector.tensor_reduce(out=wsum[:], in_=weighted[:], axis=AXIS_X, op=ALU.add)
-                    else:
-                        nc.vector.tensor_tensor(out=result[:, v0 // D : v1 // D], in0=wsum[:], in1=inv[:], op=ALU.mult)
+        def soft_depth(v0, v1, sc):
+            pixels = (v1 - v0) // D
+            shifted, ex, weighted = [sb(f"{n}{v0}", [P, pixels, D], F32) for n in ("shifted", "ex", "weighted")]
+            top, total, inverse, weighted_total = [sb(f"{n}{v0}", [P, pixels], F32) for n in ("top", "total", "inverse", "weighted_total")]
+            depths = depth_sb[:, v0:v1].rearrange("p (g d) -> p g d", d=D)
+            return [
+                lambda: nc.vector.tensor_reduce(out=top[:], in_=sc[:], axis=AXIS_X, op=ALU.max),
+                lambda: nc.vector.tensor_tensor(
+                    out=shifted[:], in0=sc[:], in1=top[:].unsqueeze(2).to_broadcast([P, pixels, D]), op=ALU.subtract
+                ),
+                lambda: nc.scalar.activation(out=ex[:], in_=shifted[:], func=ACT.Exp),
+                lambda: nc.vector.tensor_reduce(out=total[:], in_=ex[:], axis=AXIS_X, op=ALU.add),
+                lambda: nc.vector.tensor_tensor(out=weighted[:], in0=ex[:], in1=depths, op=ALU.mult),
+                lambda: nc.vector.reciprocal(out=inverse[:], in_=total[:]),
+                lambda: nc.vector.tensor_reduce(out=weighted_total[:], in_=weighted[:], axis=AXIS_X, op=ALU.add),
+                lambda: nc.vector.tensor_tensor(out=result[:, v0 // D : v1 // D], in0=weighted_total[:], in1=inverse[:], op=ALU.mult),
+            ]
 
-        soft_depth([1, 2])
-        soft_depth([0])
+        for pair in zip(*[soft_depth(*piece) for piece in second_set]):
+            for issue in pair:
+                issue()
+        for issue in soft_depth(*first_set):
+            issue()
         nc.sync.dma_start(out=out, in_=result[:])

@@ -22,30 +22,29 @@ P = 128
 PACK = 4
 BLOCKS = K // 32
 QUADRANTS = 4
-BANKS = 8
 HALVES = V // P
 ENTRIES = S // HALVES
 WIDE = H // 2
-LINE = 4
-SCALAR_SHARE = 24
-A, B, C = 0, 1, 2
+GROUPS = WIDE // PACK
+SCALAR_SHARE = 44
+FIRST_SHARE = 24
+TERMS = (4, 3)
 
 
 def tile_picked_ymvs_mean_p_kernel(tc, x_words, x_scales, w1, unit, w2, depth, offs, out):
     nc = tc.nc
     with ExitStack() as ctx:
         keep = ctx.enter_context(tc.tile_pool(name="keep", bufs=1))
-        psum = ctx.enter_context(tc.psum_pool(name="psum", bufs=BANKS))
+        psum = ctx.enter_context(tc.psum_pool(name="psum", bufs=1))
 
         def sb(name, shape, dtype):
             return keep.tile(shape, dtype, name=name, align_bytes=64)
 
-        def bank(name, shape):
-            return psum.tile(shape, F32, name=name, tag="bank")
+        def bank(name, shape, number):
+            return psum.tile(shape, F32, name=name, tag=f"bank{number}")
 
         offsets = keep.tile([P, S // 16], U16, name="offsets")
         nc.sync.dma_start(offsets[:], offs)
-
         unit_raw = sb("unit_raw", [P, PACK], F32)
         nc.sync.dma_start(out=unit_raw[:], in_=unit.rearrange("(p t) o -> p (t o)", t=PACK))
 
@@ -57,20 +56,19 @@ def tile_picked_ymvs_mean_p_kernel(tc, x_words, x_scales, w1, unit, w2, depth, o
         nc.vector.memset(x_plane[:].bitcast(I32), 0)
 
         w1_rows = w1.rearrange("(p j) c -> p j c", j=PACK)
-        w1_raw = [keep.tile([P, PACK, WIDE], F32, name=f"w1_raw{g}", tag=f"staging{g}", align_bytes=64) for g in range(2)]
+        w1_raw = [sb(f"w1_raw{g}", [P, PACK, WIDE], F32) for g in range(2)]
         word_table = sb("word_table", [P, T], I32)
         nc.scalar.dma_start(out=word_table[:], in_=x_words[0].rearrange("p n t -> p (n t)").bitcast(I32))
         nc.scalar.dma_start(out=w1_raw[0][:], in_=w1_rows[:, :, 0:WIDE])
         nc.scalar.dma_start(out=w1_raw[1][:], in_=w1_rows[:, :, WIDE:H])
-        w2_raw = sb("w2_raw", [P, PACK, N], F32)
-        nc.scalar.dma_start(out=w2_raw[:], in_=w2.rearrange("(p j) c -> p j c", j=PACK))
-        unit_sb = sb("unit_sb", [P, PACK], F32)
-        nc.scalar.activation(out=unit_sb[:], in_=unit_raw[:], func=ACT.Copy, scale=1.0 / (D * D))
+        unit_sb = sb("unit_sb", [P, HALVES, PACK], F32)
+        for h, divisor in enumerate((32, 48)):
+            nc.scalar.activation(out=unit_sb[:, h, :], in_=unit_raw[:], func=ACT.Copy, scale=1.0 / divisor)
 
         ident = sb("ident", [P, P], F32)
         make_identity(nc, ident[:])
 
-        picked_scales = sb("picked_scales", [P, S], U8)
+        picked_scales = keep.tile([P, S], U8, name="picked_scales", tag="late", align_bytes=64)
         nc.vector.tensor_copy(picked_scales[:], scale_table[:].indirect(offsets[:]))
         scales_by_view = sb("scales_by_view", [P, S], U8)
         nc.vector.tensor_copy(
@@ -83,137 +81,144 @@ def tile_picked_ymvs_mean_p_kernel(tc, x_words, x_scales, w1, unit, w2, depth, o
                 in_=scales_by_view[:].bitcast(I32)[first_row + 4 * q : first_row + 4 * q + 4, :],
             )
 
+        late = keep.tile([P, PACK * N + V], F32, name="late", tag="late", align_bytes=64)
+        w2_raw = late[:, 0 : PACK * N].rearrange("p (j c) -> p j c", j=PACK)
+        depth_sb = late[:, PACK * N :]
+        nc.sync.dma_start(out=w2_raw, in_=w2.rearrange("(p j) c -> p j c", j=PACK))
+        nc.sync.dma_start(out=depth_sb, in_=depth)
+        w1_codes = [sb(f"w1_codes{g}", [P, WIDE], U32) for g in range(2)]
+        w1_plane = [sb(f"w1_plane{g}", [P, WIDE], U8) for g in range(2)]
+        w1_bf = [keep.tile([P, PACK, GROUPS, PACK], BF16, name=f"w1_bf{g}", tag=f"dealt{g}", align_bytes=64) for g in range(2)]
+
+        def deal_w1(copy, g, m0, m1):
+            copy(
+                out=w1_bf[g][:, :, m0:m1, :].rearrange("p t m j -> p m t j"),
+                in_=w1_raw[g][:].rearrange("p j (m t) -> p m t j", t=PACK)[:, m0:m1],
+            )
+
+        def quantize_w1(g):
+            nc.vector.quantize_mx(out=w1_codes[g][:].bitcast(FP8X4), scales=w1_plane[g][:], in_=w1_bf[g][:].rearrange("p t m j -> p (t m j)"))
+
         def gather_words(h):
-            codes = sb(f"x_codes{h}", [P, D, P], U32)
+            codes = keep.tile([P, D, P], U32, name=f"x_codes{h}", tag="dealt0" if h == 1 else "x_codes0", align_bytes=64)
             nc.vector.tensor_copy(
                 codes[:].rearrange("p d v -> p v d"),
                 word_table[:].bitcast(U32).indirect(offsets[:, h * ENTRIES // 16 : (h + 1) * ENTRIES // 16]),
             )
             return codes
 
-        x_codes = [gather_words(h) for h in range(HALVES)]
-
-        w1_codes = sb("w1_codes", [P, H], U32)
-        w1_plane = sb("w1_plane", [P, H], U8)
-        w1_bf = sb("w1_bf", [P, PACK, P, PACK], BF16)
-        groups_in_half = WIDE // PACK
-
-        def deal_w1(copy, g, m0, m1):
-            base = g * groups_in_half
-            copy(
-                out=w1_bf[:, :, base + m0 : base + m1, :].rearrange("p t m j -> p m t j"),
-                in_=w1_raw[g][:].rearrange("p j (m t) -> p m t j", t=PACK)[:, m0:m1],
-            )
-
-        deal_w1(nc.scalar.copy, 0, 0, groups_in_half)
+        x_codes = [gather_words(0)]
+        deal_w1(nc.scalar.copy, 0, 0, FIRST_SHARE)
+        deal_w1(nc.vector.tensor_copy, 0, FIRST_SHARE, GROUPS)
+        quantize_w1(0)
+        x_codes.append(gather_words(1))
         deal_w1(nc.scalar.copy, 1, 0, SCALAR_SHARE)
-        deal_w1(nc.vector.tensor_copy, 1, SCALAR_SHARE, groups_in_half)
-        for u in range(2):
-            cols = slice(u * WIDE, (u + 1) * WIDE)
-            nc.vector.quantize_mx(
-                out=w1_codes[:, cols].bitcast(FP8X4), scales=w1_plane[:, cols],
-                in_=w1_bf[:, 2 * u : 2 * u + 2].rearrange("p t m j -> p (t m j)"),
-            )
+        deal_w1(nc.vector.tensor_copy, 1, SCALAR_SHARE, GROUPS)
+        quantize_w1(1)
 
-        depth_sb = keep.tile([P, V], F32, name="depth_sb", tag="staging0", align_bytes=64)
-        nc.sync.dma_start(out=depth_sb[:], in_=depth)
-        w2_bf = sb("w2_bf", [P, N, PACK], BF16)
-        nc.vector.tensor_copy(
-            out=w2_bf[:].rearrange("p (c i) j -> p c j i", i=LINE), in_=w2_raw[:].rearrange("p j (c i) -> p c j i", i=LINE)
-        )
+        w2_bf = keep.tile([P, N, PACK], BF16, name="w2_bf", tag="dealt1", align_bytes=64)
+        w2_plane = sb("w2_plane", [P, N], U8)
 
-        def product(acc, h, d, u, start, stop):
-            c0 = h * ENTRIES + d * P
-            cols = slice(u * WIDE, (u + 1) * WIDE)
-            nc.tensor.matmul_mx(
-                out=acc, lhsT=x_codes[h][:, d, :].bitcast(FP8X4), lhsT_scale=x_plane[:, c0 : c0 + P],
-                rhs=w1_codes[:, cols].bitcast(FP8X4), rhs_scale=w1_plane[:, cols], start=start, stop=stop,
-            )
+        def product(acc, h, views, g, c0, c1):
+            for d in views:
+                e0 = h * ENTRIES + d * P
+                nc.tensor.matmul_mx(
+                    out=acc, lhsT=x_codes[h][:, d, :].bitcast(FP8X4), lhsT_scale=x_plane[:, e0 : e0 + P],
+                    rhs=w1_codes[g][:, c0:c1].bitcast(FP8X4), rhs_scale=w1_plane[g][:, c0:c1],
+                    start=(d == views[0]), stop=(d == views[-1]),
+                )
 
         steps = [(h, u) for h in range(HALVES) for u in range(2)]
-        for_scalar, for_vector = {}, {}
-        for h, u in steps:
-            sbank = for_scalar[h, u] = bank(f"for_scalar{h}{u}", [P, 2, WIDE])
-            vbank = for_vector[h, u] = bank(f"for_vector{h}{u}", [P, 2, WIDE])
-            product(sbank[:, 1, :], h, 3, u, True, True)
-            product(sbank[:, 0, :], h, 0, u, True, False)
-            product(sbank[:, 0, :], h, 1, u, False, True)
-            product(vbank[:, 0, :], h, 1, u, True, True)
-            product(vbank[:, 1, :], h, 2, u, True, True)
+        step_banks = {step: (2 * i, 2 * i + 1) for i, step in enumerate(steps)}
 
-        sums0 = bank("sums0", [P, PACK, P])
-        sums1 = [bank(f"sums1_{u}", [P, 2, P]) for u in range(2)]
-
-        def copy_out(step):
-            copied = sb(f"copied{step[0]}{step[1]}", [P, 2, WIDE], F32)
-            nc.scalar.copy(out=copied[:], in_=for_scalar[step][:])
-            y01_less_y3 = sb(f"y01_less_y3_{step[0]}{step[1]}", [P, WIDE], F32)
-            nc.vector.tensor_tensor(out=y01_less_y3[:], in0=copied[:, 0, :], in1=copied[:, 1, :], op=ALU.subtract)
-            return copied, y01_less_y3
-
-        def variance(step, copied, y01_less_y3):
+        def products(step):
             h, u = step
-            y1, y2 = for_vector[step][:, 0, :], for_vector[step][:, 1, :]
+            first = bank(f"first{h}{u}", [P, 2, WIDE], step_banks[step][0])
+            second = bank(f"second{h}{u}", [P, 2, WIDE], step_banks[step][1])
+            pieces = [(u, 0, WIDE, 0)] if h == 0 else [(g, u * P, (u + 1) * P, g * P) for g in range(2)]
+            for acc, views in ((first[:, 0, :], (0, 1)), (first[:, 1, :], (3,)), (second[:, 0, :], (1,)), (second[:, 1, :], (2,))):
+                for g, c0, c1, at in pieces:
+                    product(acc[:, at : at + c1 - c0], h, views, g, c0, c1)
+            pair_sum = keep.tile([P, WIDE], F32, name=f"pair_sum{h}{u}", tag=f"pair_sum{h}{u}", align_bytes=64)
+            nc.scalar.copy(out=pair_sum[:], in_=first[:, 0, :])
+            return first, second, pair_sum
+
+        terms0 = sb("terms0", [P, TERMS[0], PACK, P], F32)
+        terms1 = [sb(f"terms1_{u}", [P, TERMS[1], 2, P], F32) for u in range(2)]
+
+        def contrasts_of_pair(h, u, second, pair_sum):
             contrasts = sb(f"contrasts{h}{u}", [P, 3, WIDE], F32)
-            squares = sb(f"squares{h}{u}", [P, 3, WIDE], F32)
-            nc.vector.tensor_tensor(out=contrasts[:, B, :], in0=y2, in1=copied[:, 1, :], op=ALU.subtract)
-            nc.vector.scalar_tensor_tensor(out=contrasts[:, A, :], in0=y1, scalar=-2.0, in1=copied[:, 0, :], op0=ALU.mult, op1=ALU.add)
-            nc.vector.tensor_tensor(out=contrasts[:, C, :], in0=y01_less_y3[:], in1=y2, op=ALU.subtract)
+            nc.vector.scalar_tensor_tensor(
+                out=contrasts[:, 0:2, :], in0=second[:], scalar=-2.0, in1=pair_sum[:].unsqueeze(1).to_broadcast([P, 2, WIDE]),
+                op0=ALU.mult, op1=ALU.add,
+            )
+            return contrasts
+
+        def four_terms(step, first, second, pair_sum):
+            h, u = step
+            contrasts = contrasts_of_pair(h, u, second, pair_sum)
+            nc.vector.scalar_tensor_tensor(out=contrasts[:, 2, :], in0=first[:, 1, :], scalar=2.0, in1=pair_sum[:], op0=ALU.mult, op1=ALU.subtract)
+            src = contrasts[:].rearrange("p k (t m) -> p k t m", t=PACK)
+            dst = terms0[:, :, :, u * GROUPS : (u + 1) * GROUPS]
+            nc.scalar.activation(out=dst[:, 0], in_=src[:, 0], func=ACT.Square, scale=2.0)
+            nc.scalar.activation(out=dst[:, 1:3], in_=src[:, 1:3], func=ACT.Square, scale=math.sqrt(1.5))
+            nc.gpsimd.tensor_tensor(out=dst[:, 3], in0=src[:, 1], in1=src[:, 2], op=ALU.mult)
+
+        def three_terms(step, first, second, pair_sum):
+            h, u = step
+            triple_sum = keep.tile([P, WIDE], F32, name=f"triple_sum{u}", tag=f"triple_sum{u}", align_bytes=64)
+            nc.vector.tensor_tensor(out=triple_sum[:], in0=second[:, 1, :], in1=pair_sum[:], op=ALU.add)
+            contrasts = contrasts_of_pair(h, u, second, pair_sum)
+            nc.vector.scalar_tensor_tensor(out=contrasts[:, 2, :], in0=first[:, 1, :], scalar=-3.0, in1=triple_sum[:], op0=ALU.mult, op1=ALU.add)
+            src = [contrasts[:, k, :].rearrange("p (g t m) -> p g t m", g=2, t=2) for k in range(3)]
+            dst = [terms1[u][:, k].rearrange("p t (g m) -> p g t m", g=2) for k in range(3)]
+            for k, weight in enumerate((6.0, 2.0)):
+                nc.scalar.activation(out=dst[k], in_=src[k], func=ACT.Square, scale=math.sqrt(weight))
             if step == steps[-1]:
-                nc.scalar.activation(out=squares[:, B, :], in_=contrasts[:, B, :], func=ACT.Square, scale=math.sqrt(2.0))
-                nc.vector.scalar_tensor_tensor(
-                    out=squares[:, A, :], in0=contrasts[:, A, :], scalar=2.0, in1=contrasts[:, A, :], op0=ALU.mult, op1=ALU.mult
-                )
-                for i in range(2):
-                    cols = slice(i * P, (i + 1) * P)
-                    nc.scalar.activation(out=squares[:, C, cols], in_=contrasts[:, C, cols], func=ACT.Square)
+                nc.scalar.activation(out=dst[2], in_=src[2], func=ACT.Square)
             else:
-                nc.scalar.activation(out=squares[:, A:C, :], in_=contrasts[:, A:C, :], func=ACT.Square, scale=math.sqrt(2.0))
-                nc.scalar.activation(out=squares[:, C, :], in_=contrasts[:, C, :], func=ACT.Square)
-            for i in range(2):
-                acc = sums0[:, 2 * u + i, :] if h == 0 else sums1[u][:, i, :]
-                for which in (B, A, C):
+                nc.gpsimd.tensor_tensor(out=dst[2], in0=src[2], in1=src[2], op=ALU.mult)
+
+        def add_terms(acc, terms, count, number, opens=True, closes=True):
+            for k in range(number):
+                for i in range(count):
                     nc.tensor.matmul(
-                        out=acc, lhsT=squares[:, which, i * P : (i + 1) * P], rhs=ident[:],
-                        is_transpose=True, start=(which == B), stop=(which == C),
+                        out=acc[:, i, :], lhsT=terms[:, k, i, :], rhs=ident[:], is_transpose=True,
+                        start=(opens and k == 0 and i == 0), stop=(closes and k == number - 1 and i == count - 1),
                     )
 
-        ahead = [copy_out(steps[0]), copy_out(steps[1])]
-        for i, step in enumerate(steps):
-            if i + 2 < len(steps):
-                ahead.append(copy_out(steps[i + 2]))
-            variance(step, *ahead[i])
-
-        w2_codes = sb("w2_codes", [P, N], U32)
-        w2_plane = sb("w2_plane", [P, N], U8)
+        made = [products(step) for step in steps[:2]]
+        nc.scalar.copy(out=w2_bf[:].rearrange("p (c i) j -> p c j i", i=4), in_=w2_raw.rearrange("p j (c i) -> p c j i", i=4))
+        made.extend(products(step) for step in steps[2:])
+        four_terms(steps[0], *made[0])
+        four_terms(steps[1], *made[1])
+        sums0 = bank("sums0", [P, PACK, P], 0)
+        add_terms(sums0, terms0, PACK, TERMS[0])
+        sums1 = bank("sums1", [P, PACK, P], 1)
+        for u in range(2):
+            three_terms(steps[2 + u], *made[2 + u])
+            add_terms(sums1[:, 2 * u : 2 * u + 2, :], terms1[u], 2, TERMS[1], u == 0, u == 1)
+        w2_codes = keep.tile([P, N], U32, name="w2_codes", tag="pair_sum11", align_bytes=64)
         nc.vector.quantize_mx(out=w2_codes[:].bitcast(FP8X4), scales=w2_plane[:], in_=w2_bf[:].rearrange("p c j -> p (c j)"))
 
-        z_bf = sb("z_bf", [P, V, PACK], BF16)
+        z_bf = [keep.tile([P, P, PACK], BF16, name="z_bf0", tag="triple_sum1", align_bytes=64), sb("z_bf1", [P, P, PACK], BF16)]
 
-        def scale_z(acc, v0, v1, t0, t1):
+        def scale_z(acc, v0, v1):
             nc.vector.tensor_tensor(
-                out=z_bf[:, v0:v1, t0:t1], in0=acc.rearrange("p t v -> p v t"),
-                in1=unit_sb[:, t0:t1].unsqueeze(1).to_broadcast([P, v1 - v0, t1 - t0]), op=ALU.mult,
+                out=z_bf[v0 // P][:, v0 % P : v0 % P + v1 - v0, :], in0=acc.rearrange("p t v -> p v t"),
+                in1=unit_sb[:, v0 // P, :].unsqueeze(1).to_broadcast([P, v1 - v0, PACK]), op=ALU.mult,
             )
 
-        def costs(v0, v1):
+        def costs(v0, v1, number):
             z_codes = sb(f"z_codes{v0}", [P, v1 - v0], U32)
             z_plane = sb(f"z_plane{v0}", [P, v1 - v0], U8)
-            nc.vector.quantize_mx(out=z_codes[:].bitcast(FP8X4), scales=z_plane[:], in_=z_bf[:, v0:v1, :].rearrange("p v t -> p (v t)"))
-            sc = bank(f"sc{v0}", [P, (v1 - v0) // D, D])
+            nc.vector.quantize_mx(out=z_codes[:].bitcast(FP8X4), scales=z_plane[:], in_=z_bf[v0 // P][:, v0 % P : v0 % P + v1 - v0, :].rearrange("p v t -> p (v t)"))
+            sc = bank(f"sc{v0}", [P, (v1 - v0) // D, D], number)
             nc.tensor.matmul_mx(
                 out=sc[:].rearrange("p g d -> p (g d)"), lhsT=w2_codes[:].bitcast(FP8X4), lhsT_scale=w2_plane[:],
                 rhs=z_codes[:].bitcast(FP8X4), rhs_scale=z_plane[:], start=True, stop=True,
             )
             return sc
-
-        middle = P + P // 2
-        scale_z(sums1[0][:], P, V, 0, 2)
-        scale_z(sums0[:], 0, P, 0, PACK)
-        first_set = (0, P, costs(0, P))
-        scale_z(sums1[1][:, :, 0 : P // 2], P, middle, 2, PACK)
-        scale_z(sums1[1][:, :, P // 2 : P], middle, V, 2, PACK)
-        second_set = [(v0, v1, costs(v0, v1)) for v0, v1 in ((P, middle), (middle, V))]
 
         result = sb("result", [P, V // D], F32)
 
@@ -235,9 +240,11 @@ def tile_picked_ymvs_mean_p_kernel(tc, x_words, x_scales, w1, unit, w2, depth, o
                 lambda: nc.vector.tensor_tensor(out=result[:, v0 // D : v1 // D], in0=weighted_total[:], in1=inverse[:], op=ALU.mult),
             ]
 
-        for pair in zip(*[soft_depth(*piece) for piece in second_set]):
-            for issue in pair:
-                issue()
+        scale_z(sums0[:], 0, P)
+        first_set = (0, P, costs(0, P, 2))
+        scale_z(sums1[:], P, V)
+        for issue in soft_depth(P, V, costs(P, V, 3)):
+            issue()
         for issue in soft_depth(*first_set):
             issue()
         nc.sync.dma_start(out=out, in_=result[:])

@@ -28,7 +28,7 @@ WIDE = H // 2
 GROUPS = WIDE // PACK
 SCALAR_SHARE = 44
 FIRST_SHARE = 24
-TERMS = (4, 3)
+TERMS = 3
 
 
 def tile_picked_ymvs_mean_p_kernel(tc, x_words, x_scales, w1, unit, w2, depth, offs, out):
@@ -61,9 +61,8 @@ def tile_picked_ymvs_mean_p_kernel(tc, x_words, x_scales, w1, unit, w2, depth, o
         nc.scalar.dma_start(out=word_table[:], in_=x_words[0].rearrange("p n t -> p (n t)").bitcast(I32))
         nc.scalar.dma_start(out=w1_raw[0][:], in_=w1_rows[:, :, 0:WIDE])
         nc.scalar.dma_start(out=w1_raw[1][:], in_=w1_rows[:, :, WIDE:H])
-        unit_sb = sb("unit_sb", [P, HALVES, PACK], F32)
-        for h, divisor in enumerate((32, 48)):
-            nc.scalar.activation(out=unit_sb[:, h, :], in_=unit_raw[:], func=ACT.Copy, scale=1.0 / divisor)
+        unit_sb = sb("unit_sb", [P, PACK], F32)
+        nc.scalar.activation(out=unit_sb[:], in_=unit_raw[:], func=ACT.Copy, scale=1.0 / 48)
 
         ident = sb("ident", [P, P], F32)
         make_identity(nc, ident[:])
@@ -143,8 +142,8 @@ def tile_picked_ymvs_mean_p_kernel(tc, x_words, x_scales, w1, unit, w2, depth, o
             nc.scalar.copy(out=pair_sum[:], in_=first[:, 0, :])
             return first, second, pair_sum
 
-        terms0 = sb("terms0", [P, TERMS[0], PACK, P], F32)
-        terms1 = [sb(f"terms1_{u}", [P, TERMS[1], 2, P], F32) for u in range(2)]
+        terms0 = sb("terms0", [P, TERMS, PACK, P], F32)
+        terms1 = [sb(f"terms1_{u}", [P, TERMS, 2, P], F32) for u in range(2)]
 
         def contrasts_of_pair(h, u, second, pair_sum):
             contrasts = sb(f"contrasts{h}{u}", [P, 3, WIDE], F32)
@@ -154,30 +153,20 @@ def tile_picked_ymvs_mean_p_kernel(tc, x_words, x_scales, w1, unit, w2, depth, o
             )
             return contrasts
 
-        def four_terms(step, first, second, pair_sum):
-            h, u = step
-            contrasts = contrasts_of_pair(h, u, second, pair_sum)
-            nc.vector.scalar_tensor_tensor(out=contrasts[:, 2, :], in0=first[:, 1, :], scalar=2.0, in1=pair_sum[:], op0=ALU.mult, op1=ALU.subtract)
-            src = contrasts[:].rearrange("p k (t m) -> p k t m", t=PACK)
-            dst = terms0[:, :, :, u * GROUPS : (u + 1) * GROUPS]
-            nc.scalar.activation(out=dst[:, 0], in_=src[:, 0], func=ACT.Square, scale=2.0)
-            nc.scalar.activation(out=dst[:, 1:3], in_=src[:, 1:3], func=ACT.Square, scale=math.sqrt(1.5))
-            nc.gpsimd.tensor_tensor(out=dst[:, 3], in0=src[:, 1], in1=src[:, 2], op=ALU.mult)
-
         def three_terms(step, first, second, pair_sum):
             h, u = step
-            triple_sum = keep.tile([P, WIDE], F32, name=f"triple_sum{u}", tag=f"triple_sum{u}", align_bytes=64)
+            triple_sum = keep.tile([P, WIDE], F32, name=f"triple_sum{h}{u}", tag=f"triple_sum{h}{u}", align_bytes=64)
             nc.vector.tensor_tensor(out=triple_sum[:], in0=second[:, 1, :], in1=pair_sum[:], op=ALU.add)
             contrasts = contrasts_of_pair(h, u, second, pair_sum)
             nc.vector.scalar_tensor_tensor(out=contrasts[:, 2, :], in0=first[:, 1, :], scalar=-3.0, in1=triple_sum[:], op0=ALU.mult, op1=ALU.add)
-            src = [contrasts[:, k, :].rearrange("p (g t m) -> p g t m", g=2, t=2) for k in range(3)]
-            dst = [terms1[u][:, k].rearrange("p t (g m) -> p g t m", g=2) for k in range(3)]
-            for k, weight in enumerate((6.0, 2.0)):
-                nc.scalar.activation(out=dst[k], in_=src[k], func=ACT.Square, scale=math.sqrt(weight))
-            if step == steps[-1]:
-                nc.scalar.activation(out=dst[2], in_=src[2], func=ACT.Square)
+            if h == 0:
+                src = [contrasts[:, k, :].rearrange("p (t m) -> p t m", t=PACK) for k in range(TERMS)]
+                dst = [terms0[:, k, :, u * GROUPS : (u + 1) * GROUPS] for k in range(TERMS)]
             else:
-                nc.gpsimd.tensor_tensor(out=dst[2], in0=src[2], in1=src[2], op=ALU.mult)
+                src = [contrasts[:, k, :].rearrange("p (g t m) -> p g t m", g=2, t=2) for k in range(TERMS)]
+                dst = [terms1[u][:, k].rearrange("p t (g m) -> p g t m", g=2) for k in range(TERMS)]
+            for k, weight in enumerate((6.0, 2.0, 1.0)):
+                nc.scalar.activation(out=dst[k], in_=src[k], func=ACT.Square, scale=math.sqrt(weight))
 
         def add_terms(acc, terms, count, number, opens=True, closes=True):
             for k in range(number):
@@ -187,26 +176,27 @@ def tile_picked_ymvs_mean_p_kernel(tc, x_words, x_scales, w1, unit, w2, depth, o
                         start=(opens and k == 0 and i == 0), stop=(closes and k == number - 1 and i == count - 1),
                     )
 
-        made = [products(step) for step in steps[:2]]
+        made = [products(steps[0]), products(steps[1])]
         nc.scalar.copy(out=w2_bf[:].rearrange("p (c i) j -> p c j i", i=4), in_=w2_raw.rearrange("p j (c i) -> p c j i", i=4))
-        made.extend(products(step) for step in steps[2:])
-        four_terms(steps[0], *made[0])
-        four_terms(steps[1], *made[1])
+        made.append(products(steps[2]))
+        three_terms(steps[0], *made[0])
+        made.append(products(steps[3]))
+        three_terms(steps[1], *made[1])
         sums0 = bank("sums0", [P, PACK, P], 0)
-        add_terms(sums0, terms0, PACK, TERMS[0])
+        add_terms(sums0, terms0, PACK, TERMS)
         sums1 = bank("sums1", [P, PACK, P], 1)
         for u in range(2):
             three_terms(steps[2 + u], *made[2 + u])
-            add_terms(sums1[:, 2 * u : 2 * u + 2, :], terms1[u], 2, TERMS[1], u == 0, u == 1)
+            add_terms(sums1[:, 2 * u : 2 * u + 2, :], terms1[u], 2, TERMS, u == 0, u == 1)
         w2_codes = keep.tile([P, N], U32, name="w2_codes", tag="pair_sum11", align_bytes=64)
         nc.vector.quantize_mx(out=w2_codes[:].bitcast(FP8X4), scales=w2_plane[:], in_=w2_bf[:].rearrange("p c j -> p (c j)"))
 
-        z_bf = [keep.tile([P, P, PACK], BF16, name="z_bf0", tag="triple_sum1", align_bytes=64), sb("z_bf1", [P, P, PACK], BF16)]
+        z_bf = [keep.tile([P, P, PACK], BF16, name="z_bf0", tag="triple_sum11", align_bytes=64), sb("z_bf1", [P, P, PACK], BF16)]
 
         def scale_z(acc, v0, v1):
             nc.vector.tensor_tensor(
                 out=z_bf[v0 // P][:, v0 % P : v0 % P + v1 - v0, :], in0=acc.rearrange("p t v -> p v t"),
-                in1=unit_sb[:, v0 // P, :].unsqueeze(1).to_broadcast([P, v1 - v0, PACK]), op=ALU.mult,
+                in1=unit_sb[:].unsqueeze(1).to_broadcast([P, v1 - v0, PACK]), op=ALU.mult,
             )
 
         def costs(v0, v1, number):

@@ -29,6 +29,8 @@ GROUPS = WIDE // PACK
 SCALAR_SHARE = 44
 FIRST_SHARE = 24
 TERMS = 3
+BANKS = 8
+WEIGHTS = (6.0, 2.0, 1.0)
 
 
 def tile_picked_ymvs_mean_p_kernel(tc, x_words, x_scales, w1, unit, w2, depth, offs, out):
@@ -127,71 +129,79 @@ def tile_picked_ymvs_mean_p_kernel(tc, x_words, x_scales, w1, unit, w2, depth, o
                     start=(d == views[0]), stop=(d == views[-1]),
                 )
 
-        steps = [(h, u) for h in range(HALVES) for u in range(2)]
-        step_banks = {step: (2 * i, 2 * i + 1) for i, step in enumerate(steps)}
-
-        def products(step):
-            h, u = step
-            first = bank(f"first{h}{u}", [P, 2, WIDE], step_banks[step][0])
-            second = bank(f"second{h}{u}", [P, 2, WIDE], step_banks[step][1])
-            pieces = [(u, 0, WIDE, 0)] if h == 0 else [(g, u * P, (u + 1) * P, g * P) for g in range(2)]
-            for acc, views in ((first[:, 0, :], (0, 1)), (first[:, 1, :], (3,)), (second[:, 0, :], (1,)), (second[:, 1, :], (2,))):
-                for g, c0, c1, at in pieces:
-                    product(acc[:, at : at + c1 - c0], h, views, g, c0, c1)
-            pair_sum = keep.tile([P, WIDE], F32, name=f"pair_sum{h}{u}", tag=f"pair_sum{h}{u}", align_bytes=64)
-            nc.scalar.copy(out=pair_sum[:], in_=first[:, 0, :])
-            return first, second, pair_sum
-
         terms0 = sb("terms0", [P, TERMS, PACK, P], F32)
         terms1 = [sb(f"terms1_{u}", [P, TERMS, 2, P], F32) for u in range(2)]
 
-        def contrasts_of_pair(h, u, second, pair_sum):
-            contrasts = sb(f"contrasts{h}{u}", [P, 3, WIDE], F32)
-            nc.vector.scalar_tensor_tensor(
-                out=contrasts[:, 0:2, :], in0=second[:], scalar=-2.0, in1=pair_sum[:].unsqueeze(1).to_broadcast([P, 2, WIDE]),
-                op0=ALU.mult, op1=ALU.add,
-            )
-            return contrasts
+        def first_set_step(g, t0, t1):
+            pieces = [(g, t0 * GROUPS, t1 * GROUPS)]
+            dst = [terms0[:, k, t0:t1, g * GROUPS : (g + 1) * GROUPS] for k in range(TERMS)]
+            return 0, pieces, dst, lambda x: x.rearrange("p (t m) -> p t m", m=GROUPS)
 
-        def three_terms(step, first, second, pair_sum):
-            h, u = step
-            triple_sum = keep.tile([P, WIDE], F32, name=f"triple_sum{h}{u}", tag=f"triple_sum{h}{u}", align_bytes=64)
+        def second_set_step(u):
+            pieces = [(g, u * P, (u + 1) * P) for g in range(2)]
+            dst = [terms1[u][:, k].rearrange("p t (g m) -> p g t m", g=2) for k in range(TERMS)]
+            return 1, pieces, dst, lambda x: x.rearrange("p (g t m) -> p g t m", g=2, t=2)
+
+        steps = [first_set_step(0, 0, 2), first_set_step(0, 2, PACK), first_set_step(1, 0, PACK), second_set_step(0), second_set_step(1)]
+
+        def products(i):
+            h, pieces = steps[i][:2]
+            width = sum(c1 - c0 for g, c0, c1 in pieces)
+            first = bank(f"first{i}", [P, 2, width], 2 * i % BANKS)
+            second = bank(f"second{i}", [P, 2, width], (2 * i + 1) % BANKS)
+            for acc, views in ((first[:, 0, :], (0, 1)), (first[:, 1, :], (3,)), (second[:, 0, :], (1,)), (second[:, 1, :], (2,))):
+                for n, (g, c0, c1) in enumerate(pieces):
+                    product(acc[:, n * (c1 - c0) : (n + 1) * (c1 - c0)], h, views, g, c0, c1)
+            pair_sum = keep.tile([P, width], F32, name=f"pair_sum{i}", align_bytes=64)
+            nc.scalar.copy(out=pair_sum[:], in_=first[:, 0, :])
+            return width, first, second, pair_sum
+
+        def three_terms(i, width, first, second, pair_sum):
+            dst, view = steps[i][2:]
+            triple_sum = sb(f"triple_sum{i}", [P, width], F32)
+            contrasts = sb(f"contrasts{i}", [P, TERMS, width], F32)
             nc.vector.tensor_tensor(out=triple_sum[:], in0=second[:, 1, :], in1=pair_sum[:], op=ALU.add)
-            contrasts = contrasts_of_pair(h, u, second, pair_sum)
-            nc.vector.scalar_tensor_tensor(out=contrasts[:, 2, :], in0=first[:, 1, :], scalar=-3.0, in1=triple_sum[:], op0=ALU.mult, op1=ALU.add)
-            if h == 0:
-                src = [contrasts[:, k, :].rearrange("p (t m) -> p t m", t=PACK) for k in range(TERMS)]
-                dst = [terms0[:, k, :, u * GROUPS : (u + 1) * GROUPS] for k in range(TERMS)]
+            if i < len(steps) - 1:
+                nc.vector.scalar_tensor_tensor(
+                    out=contrasts[:, 0:2, :], in0=second[:], scalar=-2.0, in1=pair_sum[:].unsqueeze(1).to_broadcast([P, 2, width]),
+                    op0=ALU.mult, op1=ALU.add,
+                )
+                nc.vector.scalar_tensor_tensor(out=contrasts[:, 2, :], in0=first[:, 1, :], scalar=-3.0, in1=triple_sum[:], op0=ALU.mult, op1=ALU.add)
             else:
-                src = [contrasts[:, k, :].rearrange("p (g t m) -> p g t m", g=2, t=2) for k in range(TERMS)]
-                dst = [terms1[u][:, k].rearrange("p t (g m) -> p g t m", g=2) for k in range(TERMS)]
-            for k, weight in enumerate((6.0, 2.0, 1.0)):
-                nc.scalar.activation(out=dst[k], in_=src[k], func=ACT.Square, scale=math.sqrt(weight))
+                for k, view_d, factor, rest in ((0, second[:, 0, :], -2.0, pair_sum), (2, first[:, 1, :], -3.0, triple_sum), (1, second[:, 1, :], -2.0, pair_sum)):
+                    nc.vector.scalar_tensor_tensor(out=contrasts[:, k, :], in0=view_d, scalar=factor, in1=rest[:], op0=ALU.mult, op1=ALU.add)
+            for k in (0, 2, 1):
+                nc.scalar.activation(out=dst[k], in_=view(contrasts[:, k, :]), func=ACT.Square, scale=math.sqrt(WEIGHTS[k]))
 
-        def add_terms(acc, terms, count, number, opens=True, closes=True):
-            for k in range(number):
+        def add_terms(acc, terms, count, opens=True, closes=True):
+            order = (0, 2, 1)
+            for k in order:
                 for i in range(count):
                     nc.tensor.matmul(
                         out=acc[:, i, :], lhsT=terms[:, k, i, :], rhs=ident[:], is_transpose=True,
-                        start=(opens and k == 0 and i == 0), stop=(closes and k == number - 1 and i == count - 1),
+                        start=(opens and k == order[0] and i == 0), stop=(closes and k == order[-1] and i == count - 1),
                     )
 
-        made = [products(steps[0]), products(steps[1])]
+        last = len(steps) - 1
+        made = [products(0), products(1)]
         nc.scalar.copy(out=w2_bf[:].rearrange("p (c i) j -> p c j i", i=4), in_=w2_raw.rearrange("p j (c i) -> p c j i", i=4))
-        made.append(products(steps[2]))
-        three_terms(steps[0], *made[0])
-        made.append(products(steps[3]))
-        three_terms(steps[1], *made[1])
-        sums0 = bank("sums0", [P, PACK, P], 0)
-        add_terms(sums0, terms0, PACK, TERMS)
-        sums1 = bank("sums1", [P, PACK, P], 1)
+        for i in range(last - 1):
+            if i == last - 2:
+                three_terms(i, *made[i])
+                made.append(products(i + 2))
+            else:
+                made.append(products(i + 2))
+                three_terms(i, *made[i])
+        sums0 = bank("sums0", [P, PACK, P], 2)
+        add_terms(sums0, terms0, PACK)
+        sums1 = bank("sums1", [P, PACK, P], 3)
         for u in range(2):
-            three_terms(steps[2 + u], *made[2 + u])
-            add_terms(sums1[:, 2 * u : 2 * u + 2, :], terms1[u], 2, TERMS, u == 0, u == 1)
-        w2_codes = keep.tile([P, N], U32, name="w2_codes", tag="pair_sum11", align_bytes=64)
+            three_terms(last - 1 + u, *made[last - 1 + u])
+            add_terms(sums1[:, 2 * u : 2 * u + 2, :], terms1[u], 2, u == 0, u == 1)
+        w2_codes = keep.tile([P, N], U32, name="w2_codes", tag=f"pair_sum{last}", align_bytes=64)
         nc.vector.quantize_mx(out=w2_codes[:].bitcast(FP8X4), scales=w2_plane[:], in_=w2_bf[:].rearrange("p c j -> p (c j)"))
 
-        z_bf = [keep.tile([P, P, PACK], BF16, name="z_bf0", tag="triple_sum11", align_bytes=64), sb("z_bf1", [P, P, PACK], BF16)]
+        z_bf = [keep.tile([P, P, PACK], BF16, name="z_bf0", tag=f"triple_sum{last}", align_bytes=64), sb("z_bf1", [P, P, PACK], BF16)]
 
         def scale_z(acc, v0, v1):
             nc.vector.tensor_tensor(
@@ -231,10 +241,14 @@ def tile_picked_ymvs_mean_p_kernel(tc, x_words, x_scales, w1, unit, w2, depth, o
             ]
 
         scale_z(sums0[:], 0, P)
-        first_set = (0, P, costs(0, P, 2))
-        scale_z(sums1[:], P, V)
-        for issue in soft_depth(P, V, costs(P, V, 3)):
-            issue()
+        first_set = (0, P, costs(0, P, 4))
+        middle = P + P // 2
+        scale_z(sums1[:, :, 0 : P // 2], P, middle)
+        scale_z(sums1[:, :, P // 2 : P], middle, V)
+        second_set = [(v0, v1, costs(v0, v1, number)) for v0, v1, number in ((P, middle, 5), (middle, V, 6))]
+        for pair in zip(*[soft_depth(*piece) for piece in second_set]):
+            for issue in pair:
+                issue()
         for issue in soft_depth(*first_set):
             issue()
         nc.sync.dma_start(out=out, in_=result[:])

@@ -26,7 +26,7 @@ HALVES = V // P
 ENTRIES = S // HALVES
 WIDE = H // 2
 GROUPS = WIDE // PACK
-SCALAR_SHARE = 44
+SCALAR_SHARE = 40
 FIRST_SHARE = 24
 TERMS = 3
 BANKS = 8
@@ -97,6 +97,9 @@ def tile_picked_ymvs_mean_p_kernel(tc, x_words, x_scales, w1, unit, w2, depth, o
                 in_=w1_raw[g][:].rearrange("p j (m t) -> p m t j", t=PACK)[:, m0:m1],
             )
 
+        def gpsimd_cast(out, in_):
+            nc.gpsimd.tensor_scalar(out=out, in0=in_, scalar1=1.0, scalar2=0.0, op0=ALU.mult, op1=ALU.add)
+
         def quantize_w1(g):
             nc.vector.quantize_mx(out=w1_codes[g][:].bitcast(FP8X4), scales=w1_plane[g][:], in_=w1_bf[g][:].rearrange("p t m j -> p (t m j)"))
 
@@ -114,7 +117,7 @@ def tile_picked_ymvs_mean_p_kernel(tc, x_words, x_scales, w1, unit, w2, depth, o
         quantize_w1(0)
         x_codes.append(gather_words(1))
         deal_w1(nc.scalar.copy, 1, 0, SCALAR_SHARE)
-        deal_w1(nc.vector.tensor_copy, 1, SCALAR_SHARE, GROUPS)
+        deal_w1(gpsimd_cast, 1, SCALAR_SHARE, GROUPS)
         quantize_w1(1)
 
         w2_bf = keep.tile([P, N, PACK], BF16, name="w2_bf", tag="dealt1", align_bytes=64)

@@ -27,7 +27,7 @@ ENTRIES = S // HALVES
 WIDE = H // 2
 GROUPS = WIDE // PACK
 SCALAR_SHARE = 40
-FIRST_SHARE = 24
+FIRST_SHARE = 40
 TERMS = 3
 BANKS = 8
 WEIGHTS = (6.0, 2.0, 1.0)
@@ -113,7 +113,7 @@ def tile_picked_ymvs_mean_p_kernel(tc, x_words, x_scales, w1, unit, w2, depth, o
 
         x_codes = [gather_words(0)]
         deal_w1(nc.scalar.copy, 0, 0, FIRST_SHARE)
-        deal_w1(nc.vector.tensor_copy, 0, FIRST_SHARE, GROUPS)
+        deal_w1(gpsimd_cast, 0, FIRST_SHARE, GROUPS)
         quantize_w1(0)
         x_codes.append(gather_words(1))
         deal_w1(nc.scalar.copy, 1, 0, SCALAR_SHARE)
@@ -145,7 +145,7 @@ def tile_picked_ymvs_mean_p_kernel(tc, x_words, x_scales, w1, unit, w2, depth, o
             dst = [terms1[u][:, k].rearrange("p t (g m) -> p g t m", g=2) for k in range(TERMS)]
             return 1, pieces, dst, lambda x: x.rearrange("p (g t m) -> p g t m", g=2, t=2)
 
-        steps = [first_set_step(0, 0, 2), first_set_step(0, 2, PACK), first_set_step(1, 0, PACK), second_set_step(0), second_set_step(1)]
+        steps = [first_set_step(g, t, t + 2) for g in range(2) for t in (0, 2)] + [second_set_step(u) for u in range(2)]
 
         def products(i):
             h, pieces = steps[i][:2]
@@ -195,9 +195,9 @@ def tile_picked_ymvs_mean_p_kernel(tc, x_words, x_scales, w1, unit, w2, depth, o
             else:
                 made.append(products(i + 2))
                 three_terms(i, *made[i])
-        sums0 = bank("sums0", [P, PACK, P], 2)
+        sums0 = bank("sums0", [P, PACK, P], 4)
         add_terms(sums0, terms0, PACK)
-        sums1 = bank("sums1", [P, PACK, P], 3)
+        sums1 = bank("sums1", [P, PACK, P], 5)
         for u in range(2):
             three_terms(last - 1 + u, *made[last - 1 + u])
             add_terms(sums1[:, 2 * u : 2 * u + 2, :], terms1[u], 2, u == 0, u == 1)
@@ -244,11 +244,11 @@ def tile_picked_ymvs_mean_p_kernel(tc, x_words, x_scales, w1, unit, w2, depth, o
             ]
 
         scale_z(sums0[:], 0, P)
-        first_set = (0, P, costs(0, P, 4))
+        first_set = (0, P, costs(0, P, 6))
         middle = P + P // 2
         scale_z(sums1[:, :, 0 : P // 2], P, middle)
         scale_z(sums1[:, :, P // 2 : P], middle, V)
-        second_set = [(v0, v1, costs(v0, v1, number)) for v0, v1, number in ((P, middle, 5), (middle, V, 6))]
+        second_set = [(v0, v1, costs(v0, v1, number)) for v0, v1, number in ((P, middle, 7), (middle, V, 0))]
         for pair in zip(*[soft_depth(*piece) for piece in second_set]):
             for issue in pair:
                 issue()

@@ -104,18 +104,17 @@ def tile_picked_ymvs_mean_p_kernel(tc, x_words, x_scales, w1, unit, w2, depth, o
             nc.vector.quantize_mx(out=w1_codes[g][:].bitcast(FP8X4), scales=w1_plane[g][:], in_=w1_bf[g][:].rearrange("p t m j -> p (t m j)"))
 
         def gather_words(h):
-            codes = keep.tile([P, D, P], U32, name=f"x_codes{h}", tag="dealt0" if h == 1 else "x_codes0", align_bytes=64)
+            codes = sb(f"x_codes{h}", [P, D, P], U32)
             nc.vector.tensor_copy(
                 codes[:].rearrange("p d v -> p v d"),
                 word_table[:].bitcast(U32).indirect(offsets[:, h * ENTRIES // 16 : (h + 1) * ENTRIES // 16]),
             )
             return codes
 
-        x_codes = [gather_words(0)]
+        x_codes = [gather_words(h) for h in range(HALVES)]
         deal_w1(nc.scalar.copy, 0, 0, FIRST_SHARE)
         deal_w1(gpsimd_cast, 0, FIRST_SHARE, GROUPS)
         quantize_w1(0)
-        x_codes.append(gather_words(1))
         deal_w1(nc.scalar.copy, 1, 0, SCALAR_SHARE)
         deal_w1(gpsimd_cast, 1, SCALAR_SHARE, GROUPS)
         quantize_w1(1)

@@ -131,17 +131,17 @@ def tile_picked_ymvs_mean_p_kernel(tc, x_words, x_scales, w1, unit, w2, depth, o
                     start=(d == views[0]), stop=(d == views[-1]),
                 )
 
-        terms0 = sb("terms0", [P, TERMS, PACK, P], F32)
-        terms1 = [sb(f"terms1_{u}", [P, TERMS, 2, P], F32) for u in range(2)]
+        terms0 = [sb(f"terms0_{k}", [P, PACK, P], F32) for k in range(TERMS)]
+        terms1 = [[sb(f"terms1_{u}{k}", [P, 2, P], F32) for k in range(TERMS)] for u in range(2)]
 
         def first_set_step(g, t0, t1):
             pieces = [(g, t0 * GROUPS, t1 * GROUPS)]
-            dst = [terms0[:, k, t0:t1, g * GROUPS : (g + 1) * GROUPS] for k in range(TERMS)]
+            dst = [terms0[k][:, t0:t1, g * GROUPS : (g + 1) * GROUPS] for k in range(TERMS)]
             return 0, pieces, dst, lambda x: x.rearrange("p (t m) -> p t m", m=GROUPS)
 
         def second_set_step(u):
             pieces = [(g, u * P, (u + 1) * P) for g in range(2)]
-            dst = [terms1[u][:, k].rearrange("p t (g m) -> p g t m", g=2) for k in range(TERMS)]
+            dst = [terms1[u][k][:].rearrange("p t (g m) -> p g t m", g=2) for k in range(TERMS)]
             return 1, pieces, dst, lambda x: x.rearrange("p (g t m) -> p g t m", g=2, t=2)
 
         steps = [first_set_step(g, t, t + 2) for g in range(2) for t in (0, 2)] + [second_set_step(u) for u in range(2)]
@@ -173,20 +173,24 @@ def tile_picked_ymvs_mean_p_kernel(tc, x_words, x_scales, w1, unit, w2, depth, o
                 for k, view_d, factor, rest in ((0, second[:, 0, :], -2.0, pair_sum), (2, first[:, 1, :], -3.0, triple_sum), (1, second[:, 1, :], -2.0, pair_sum)):
                     nc.vector.scalar_tensor_tensor(out=contrasts[:, k, :], in0=view_d, scalar=factor, in1=rest[:], op0=ALU.mult, op1=ALU.add)
             for k in (0, 2, 1):
-                nc.scalar.activation(out=dst[k], in_=view(contrasts[:, k, :]), func=ACT.Square, scale=math.sqrt(WEIGHTS[k]))
+                src = view(contrasts[:, k, :])
+                if k == 2 and steps[i][0] == 0:
+                    nc.gpsimd.tensor_tensor(out=dst[k], in0=src, in1=src, op=ALU.mult)
+                else:
+                    nc.scalar.activation(out=dst[k], in_=src, func=ACT.Square, scale=math.sqrt(WEIGHTS[k]))
 
         def add_terms(acc, terms, count, opens=True, closes=True):
             order = (0, 2, 1)
             for k in order:
                 for i in range(count):
                     nc.tensor.matmul(
-                        out=acc[:, i, :], lhsT=terms[:, k, i, :], rhs=ident[:], is_transpose=True,
+                        out=acc[:, i, :], lhsT=terms[k][:, i, :], rhs=ident[:], is_transpose=True,
                         start=(opens and k == order[0] and i == 0), stop=(closes and k == order[-1] and i == count - 1),
                     )
 
         last = len(steps) - 1
         made = [products(0), products(1)]
-        nc.scalar.copy(out=w2_bf[:].rearrange("p (c i) j -> p c j i", i=4), in_=w2_raw.rearrange("p j (c i) -> p c j i", i=4))
+        nc.gpsimd.tensor_scalar(out=w2_bf[:], in0=w2_raw.rearrange("p j c -> p c j"), scalar1=1.0, scalar2=0.0, op0=ALU.mult, op1=ALU.add)
         for i in range(last - 1):
             if i == last - 2:
                 three_terms(i, *made[i])
@@ -200,7 +204,7 @@ def tile_picked_ymvs_mean_p_kernel(tc, x_words, x_scales, w1, unit, w2, depth, o
         for u in range(2):
             three_terms(last - 1 + u, *made[last - 1 + u])
             add_terms(sums1[:, 2 * u : 2 * u + 2, :], terms1[u], 2, u == 0, u == 1)
-        w2_codes = keep.tile([P, N], U32, name="w2_codes", tag=f"pair_sum{last}", align_bytes=64)
+        w2_codes = keep.tile([P, N], U32, name="w2_codes", tag="pair_sum3", align_bytes=64)
         nc.vector.quantize_mx(out=w2_codes[:].bitcast(FP8X4), scales=w2_plane[:], in_=w2_bf[:].rearrange("p c j -> p (c j)"))
 
         z_bf = [keep.tile([P, P, PACK], BF16, name="z_bf0", tag=f"triple_sum{last}", align_bytes=64), sb("z_bf1", [P, P, PACK], BF16)]

@@ -100,8 +100,11 @@ def tile_picked_ymvs_mean_p_kernel(tc, x_words, x_scales, w1, unit, w2, depth, o
         def gpsimd_cast(out, in_):
             nc.gpsimd.tensor_scalar(out=out, in0=in_, scalar1=1.0, scalar2=0.0, op0=ALU.mult, op1=ALU.add)
 
-        def quantize_w1(g):
-            nc.vector.quantize_mx(out=w1_codes[g][:].bitcast(FP8X4), scales=w1_plane[g][:], in_=w1_bf[g][:].rearrange("p t m j -> p (t m j)"))
+        def quantize_w1(g, t0, t1):
+            cols = slice(t0 * GROUPS, t1 * GROUPS)
+            nc.vector.quantize_mx(
+                out=w1_codes[g][:, cols].bitcast(FP8X4), scales=w1_plane[g][:, cols], in_=w1_bf[g][:, t0:t1].rearrange("p t m j -> p (t m j)")
+            )
 
         def gather_words(h):
             codes = sb(f"x_codes{h}", [P, D, P], U32)
@@ -114,10 +117,11 @@ def tile_picked_ymvs_mean_p_kernel(tc, x_words, x_scales, w1, unit, w2, depth, o
         x_codes = [gather_words(h) for h in range(HALVES)]
         deal_w1(nc.scalar.copy, 0, 0, FIRST_SHARE)
         deal_w1(gpsimd_cast, 0, FIRST_SHARE, GROUPS)
-        quantize_w1(0)
+        quantize_w1(0, 0, 2)
+        quantize_w1(0, 2, PACK)
         deal_w1(nc.scalar.copy, 1, 0, SCALAR_SHARE)
         deal_w1(gpsimd_cast, 1, SCALAR_SHARE, GROUPS)
-        quantize_w1(1)
+        quantize_w1(1, 0, PACK)
 
         w2_bf = keep.tile([P, N, PACK], BF16, name="w2_bf", tag="dealt1", align_bytes=64)
         w2_plane = sb("w2_plane", [P, N], U8)
@@ -151,14 +155,21 @@ def tile_picked_ymvs_mean_p_kernel(tc, x_words, x_scales, w1, unit, w2, depth, o
             width = sum(c1 - c0 for g, c0, c1 in pieces)
             first = bank(f"first{i}", [P, 2, width], 2 * i % BANKS)
             second = bank(f"second{i}", [P, 2, width], (2 * i + 1) % BANKS)
-            for acc, views in ((first[:, 0, :], (0, 1)), (first[:, 1, :], (3,)), (second[:, 0, :], (1,)), (second[:, 1, :], (2,))):
+            order = [(first[:, 0, :], (0, 1)), (second[:, 0, :], (1,)), (second[:, 1, :], (2,))]
+            if i == 0:
+                y3 = bank("third0", [P, width], BANKS - 1)[:]
+                order.append((y3, (3,)))
+            else:
+                y3 = first[:, 1, :]
+                order.insert(1, (y3, (3,)))
+            for acc, views in order:
                 for n, (g, c0, c1) in enumerate(pieces):
                     product(acc[:, n * (c1 - c0) : (n + 1) * (c1 - c0)], h, views, g, c0, c1)
             pair_sum = keep.tile([P, width], F32, name=f"pair_sum{i}", align_bytes=64)
             nc.scalar.copy(out=pair_sum[:], in_=first[:, 0, :])
-            return width, first, second, pair_sum
+            return width, y3, second, pair_sum
 
-        def three_terms(i, width, first, second, pair_sum):
+        def three_terms(i, width, y3, second, pair_sum):
             dst, view = steps[i][2:]
             triple_sum = sb(f"triple_sum{i}", [P, width], F32)
             contrasts = sb(f"contrasts{i}", [P, TERMS, width], F32)
@@ -168,9 +179,9 @@ def tile_picked_ymvs_mean_p_kernel(tc, x_words, x_scales, w1, unit, w2, depth, o
                     out=contrasts[:, 0:2, :], in0=second[:], scalar=-2.0, in1=pair_sum[:].unsqueeze(1).to_broadcast([P, 2, width]),
                     op0=ALU.mult, op1=ALU.add,
                 )
-                nc.vector.scalar_tensor_tensor(out=contrasts[:, 2, :], in0=first[:, 1, :], scalar=-3.0, in1=triple_sum[:], op0=ALU.mult, op1=ALU.add)
+                nc.vector.scalar_tensor_tensor(out=contrasts[:, 2, :], in0=y3, scalar=-3.0, in1=triple_sum[:], op0=ALU.mult, op1=ALU.add)
             else:
-                for k, view_d, factor, rest in ((0, second[:, 0, :], -2.0, pair_sum), (2, first[:, 1, :], -3.0, triple_sum), (1, second[:, 1, :], -2.0, pair_sum)):
+                for k, view_d, factor, rest in ((0, second[:, 0, :], -2.0, pair_sum), (2, y3, -3.0, triple_sum), (1, second[:, 1, :], -2.0, pair_sum)):
                     nc.vector.scalar_tensor_tensor(out=contrasts[:, k, :], in0=view_d, scalar=factor, in1=rest[:], op0=ALU.mult, op1=ALU.add)
             for k in (0, 2, 1):
                 src = view(contrasts[:, k, :])

@@ -69,7 +69,7 @@ def tile_picked_ymvs_mean_p_kernel(tc, x_words, x_scales, w1, unit, w2, depth, o
         ident = sb("ident", [P, P], F32)
         make_identity(nc, ident[:])
 
-        picked_scales = keep.tile([P, S], U8, name="picked_scales", tag="late", align_bytes=64)
+        picked_scales = sb("picked_scales", [P, S], U8)
         nc.vector.tensor_copy(picked_scales[:], scale_table[:].indirect(offsets[:]))
         scales_by_view = sb("scales_by_view", [P, S], U8)
         nc.vector.tensor_copy(
@@ -82,11 +82,6 @@ def tile_picked_ymvs_mean_p_kernel(tc, x_words, x_scales, w1, unit, w2, depth, o
                 in_=scales_by_view[:].bitcast(I32)[first_row + 4 * q : first_row + 4 * q + 4, :],
             )
 
-        late = keep.tile([P, PACK * N + V], F32, name="late", tag="late", align_bytes=64)
-        w2_raw = late[:, 0 : PACK * N].rearrange("p (j c) -> p j c", j=PACK)
-        depth_sb = late[:, PACK * N :]
-        nc.sync.dma_start(out=w2_raw, in_=w2.rearrange("(p j) c -> p j c", j=PACK))
-        nc.sync.dma_start(out=depth_sb, in_=depth)
         w1_codes = [sb(f"w1_codes{g}", [P, WIDE], U32) for g in range(2)]
         w1_plane = [sb(f"w1_plane{g}", [P, WIDE], U8) for g in range(2)]
         w1_bf = [keep.tile([P, PACK, GROUPS, PACK], BF16, name=f"w1_bf{g}", tag=f"dealt{g}", align_bytes=64) for g in range(2)]
@@ -135,6 +130,10 @@ def tile_picked_ymvs_mean_p_kernel(tc, x_words, x_scales, w1, unit, w2, depth, o
                     start=(d == views[0]), stop=(d == views[-1]),
                 )
 
+        w2_raw = keep.tile([P, PACK, N], F32, name="w2_raw", tag="w1_raw0", align_bytes=64)
+        nc.sync.dma_start(out=w2_raw[:], in_=w2.rearrange("(p j) c -> p j c", j=PACK))
+        depth_sb = keep.tile([P, V], F32, name="depth_sb", tag="w1_raw1", align_bytes=64)
+        nc.sync.dma_start(out=depth_sb[:], in_=depth)
         terms0 = [sb(f"terms0_{k}", [P, PACK, P], F32) for k in range(TERMS)]
         terms1 = [[sb(f"terms1_{u}{k}", [P, 2, P], F32) for k in range(TERMS)] for u in range(2)]
 
@@ -201,7 +200,7 @@ def tile_picked_ymvs_mean_p_kernel(tc, x_words, x_scales, w1, unit, w2, depth, o
 
         last = len(steps) - 1
         made = [products(0), products(1)]
-        nc.gpsimd.tensor_scalar(out=w2_bf[:], in0=w2_raw.rearrange("p j c -> p c j"), scalar1=1.0, scalar2=0.0, op0=ALU.mult, op1=ALU.add)
+        nc.gpsimd.tensor_scalar(out=w2_bf[:], in0=w2_raw[:].rearrange("p j c -> p c j"), scalar1=1.0, scalar2=0.0, op0=ALU.mult, op1=ALU.add)
         for i in range(last - 1):
             if i == last - 2:
                 three_terms(i, *made[i])

@@ -72,10 +72,12 @@ def tile_picked_ymvs_mean_p_kernel(tc, x_words, x_scales, w1, unit, w2, depth, o
         picked_scales = sb("picked_scales", [P, S], U8)
         nc.vector.tensor_copy(picked_scales[:], scale_table[:].indirect(offsets[:]))
         scales_by_view = sb("scales_by_view", [P, S], U8)
-        nc.vector.tensor_copy(
-            out=scales_by_view[:].rearrange("p (h d v) -> p h d v", h=HALVES, d=D),
-            in_=picked_scales[:].rearrange("p (h v d) -> p h d v", h=HALVES, d=D),
-        )
+
+        def sort_by_view(out, in_):
+            nc.vector.tensor_copy(out=out.rearrange("p (d v) -> p d v", d=D), in_=in_.rearrange("p (v d) -> p d v", d=D))
+
+        sort_by_view(scales_by_view[:, 0:ENTRIES], picked_scales[:, 0:ENTRIES])
+        nc.vector.tensor_copy(out=scales_by_view[:].bitcast(I32)[:, ENTRIES // 4 :], in_=picked_scales[:].bitcast(I32)[:, ENTRIES // 4 :])
         for q in range(QUADRANTS):
             nc.sync.dma_start(
                 out=x_plane[:].bitcast(I32)[32 * q : 32 * q + 4, :],
@@ -114,6 +116,9 @@ def tile_picked_ymvs_mean_p_kernel(tc, x_words, x_scales, w1, unit, w2, depth, o
         deal_w1(gpsimd_cast, 0, FIRST_SHARE, GROUPS)
         quantize_w1(0, 0, 2)
         quantize_w1(0, 2, PACK)
+        late_plane = keep.tile([P, ENTRIES], U8, name="late_plane", tag="dealt0", align_bytes=64)
+        sort_by_view(late_plane[:], x_plane[:, ENTRIES:S])
+        set_plane = [x_plane, late_plane]
         deal_w1(nc.scalar.copy, 1, 0, SCALAR_SHARE)
         deal_w1(gpsimd_cast, 1, SCALAR_SHARE, GROUPS)
         quantize_w1(1, 0, PACK)
@@ -123,9 +128,8 @@ def tile_picked_ymvs_mean_p_kernel(tc, x_words, x_scales, w1, unit, w2, depth, o
 
         def product(acc, h, views, g, c0, c1):
             for d in views:
-                e0 = h * ENTRIES + d * P
                 nc.tensor.matmul_mx(
-                    out=acc, lhsT=x_codes[h][:, d, :].bitcast(FP8X4), lhsT_scale=x_plane[:, e0 : e0 + P],
+                    out=acc, lhsT=x_codes[h][:, d, :].bitcast(FP8X4), lhsT_scale=set_plane[h][:, d * P : (d + 1) * P],
                     rhs=w1_codes[g][:, c0:c1].bitcast(FP8X4), rhs_scale=w1_plane[g][:, c0:c1],
                     start=(d == views[0]), stop=(d == views[-1]),
                 )

@@ -29,6 +29,9 @@ GROUPS = WIDE // PACK
 SCALAR_SHARE = 40
 FIRST_SHARE = 40
 TERMS = 3
+FIRST_ROW = 32
+ROW_STEP = 4
+ZEROED_FIRST = 600
 BANKS = 8
 WEIGHTS = (6.0, 2.0, 1.0)
 
@@ -50,18 +53,18 @@ def tile_picked_ymvs_mean_p_kernel(tc, x_words, x_scales, w1, unit, w2, depth, o
         unit_raw = sb("unit_raw", [P, PACK], F32)
         nc.sync.dma_start(out=unit_raw[:], in_=unit.rearrange("(p t) o -> p (t o)", t=PACK))
 
-        first_row = P - BLOCKS
         scale_table = sb("scale_table", [P, T], U8)
-        nc.scalar.dma_start(out=scale_table[:].bitcast(I32)[first_row:P, :], in_=x_scales[0].bitcast(I32))
-        nc.vector.memset(scale_table[:].bitcast(I32)[0:first_row, :], 0)
+        nc.gpsimd.memset(scale_table[:].bitcast(I32)[:, 0:ZEROED_FIRST], 0)
+        nc.vector.memset(scale_table[:].bitcast(I32)[:, ZEROED_FIRST:], 0)
         x_plane = sb("x_plane", [P, S], U8)
         nc.vector.memset(x_plane[:].bitcast(I32), 0)
 
         w1_rows = w1.rearrange("(p j) c -> p j c", j=PACK)
         w1_raw = [sb(f"w1_raw{g}", [P, PACK, WIDE], F32) for g in range(2)]
         word_table = sb("word_table", [P, T], I32)
-        nc.scalar.dma_start(out=word_table[:], in_=x_words[0].rearrange("p n t -> p (n t)").bitcast(I32))
         nc.scalar.dma_start(out=w1_raw[0][:], in_=w1_rows[:, :, 0:WIDE])
+        nc.scalar.dma_start(out=scale_table[:].bitcast(I32)[FIRST_ROW : FIRST_ROW + ROW_STEP * BLOCKS : ROW_STEP, :], in_=x_scales[0].bitcast(I32))
+        nc.scalar.dma_start(out=word_table[:], in_=x_words[0].rearrange("p n t -> p (n t)").bitcast(I32))
         nc.scalar.dma_start(out=w1_raw[1][:], in_=w1_rows[:, :, WIDE:H])
         unit_sb = sb("unit_sb", [P, PACK], F32)
         nc.scalar.activation(out=unit_sb[:], in_=unit_raw[:], func=ACT.Copy, scale=1.0 / 48)
@@ -72,16 +75,14 @@ def tile_picked_ymvs_mean_p_kernel(tc, x_words, x_scales, w1, unit, w2, depth, o
         picked_scales = sb("picked_scales", [P, S], U8)
         nc.vector.tensor_copy(picked_scales[:], scale_table[:].indirect(offsets[:]))
         scales_by_view = sb("scales_by_view", [P, S], U8)
-
-        def sort_by_view(out, in_):
-            nc.vector.tensor_copy(out=out.rearrange("p (d v) -> p d v", d=D), in_=in_.rearrange("p (v d) -> p d v", d=D))
-
-        sort_by_view(scales_by_view[:, 0:ENTRIES], picked_scales[:, 0:ENTRIES])
-        nc.vector.tensor_copy(out=scales_by_view[:].bitcast(I32)[:, ENTRIES // 4 :], in_=picked_scales[:].bitcast(I32)[:, ENTRIES // 4 :])
+        nc.vector.tensor_copy(
+            out=scales_by_view[:].rearrange("p (h d v) -> p h d v", h=HALVES, d=D),
+            in_=picked_scales[:].rearrange("p (h v d) -> p h d v", h=HALVES, d=D),
+        )
         for q in range(QUADRANTS):
             nc.sync.dma_start(
                 out=x_plane[:].bitcast(I32)[32 * q : 32 * q + 4, :],
-                in_=scales_by_view[:].bitcast(I32)[first_row + 4 * q : first_row + 4 * q + 4, :],
+                in_=scales_by_view[:].bitcast(I32)[FIRST_ROW + ROW_STEP * 4 * q : FIRST_ROW + ROW_STEP * 4 * (q + 1) : ROW_STEP, :],
             )
 
         w1_codes = [sb(f"w1_codes{g}", [P, WIDE], U32) for g in range(2)]
@@ -104,39 +105,35 @@ def tile_picked_ymvs_mean_p_kernel(tc, x_words, x_scales, w1, unit, w2, depth, o
             )
 
         def gather_words(h):
-            codes = sb(f"x_codes{h}", [P, D, P], U32)
+            codes = keep.tile([P, D, P], U32, name=f"x_codes{h}", tag=("w1_raw0", "dealt0")[h], align_bytes=64)
             nc.vector.tensor_copy(
                 codes[:].rearrange("p d v -> p v d"),
                 word_table[:].bitcast(U32).indirect(offsets[:, h * ENTRIES // 16 : (h + 1) * ENTRIES // 16]),
             )
             return codes
 
-        x_codes = [gather_words(h) for h in range(HALVES)]
         deal_w1(nc.scalar.copy, 0, 0, FIRST_SHARE)
         deal_w1(gpsimd_cast, 0, FIRST_SHARE, GROUPS)
-        quantize_w1(0, 0, 2)
-        quantize_w1(0, 2, PACK)
-        late_plane = keep.tile([P, ENTRIES], U8, name="late_plane", tag="dealt0", align_bytes=64)
-        sort_by_view(late_plane[:], x_plane[:, ENTRIES:S])
-        set_plane = [x_plane, late_plane]
+        quantize_w1(0, 0, PACK)
+        x_codes = [gather_words(h) for h in range(HALVES)]
         deal_w1(nc.scalar.copy, 1, 0, SCALAR_SHARE)
         deal_w1(gpsimd_cast, 1, SCALAR_SHARE, GROUPS)
         quantize_w1(1, 0, PACK)
 
-        w2_bf = keep.tile([P, N, PACK], BF16, name="w2_bf", tag="dealt1", align_bytes=64)
+        w2_bf = keep.tile([P, N, PACK], BF16, name="w2_bf", tag="w2_bf", align_bytes=64)
         w2_plane = sb("w2_plane", [P, N], U8)
 
         def product(acc, h, views, g, c0, c1):
             for d in views:
                 nc.tensor.matmul_mx(
-                    out=acc, lhsT=x_codes[h][:, d, :].bitcast(FP8X4), lhsT_scale=set_plane[h][:, d * P : (d + 1) * P],
+                    out=acc, lhsT=x_codes[h][:, d, :].bitcast(FP8X4), lhsT_scale=x_plane[:, h * ENTRIES + d * P : h * ENTRIES + (d + 1) * P],
                     rhs=w1_codes[g][:, c0:c1].bitcast(FP8X4), rhs_scale=w1_plane[g][:, c0:c1],
                     start=(d == views[0]), stop=(d == views[-1]),
                 )
 
-        w2_raw = keep.tile([P, PACK, N], F32, name="w2_raw", tag="w1_raw0", align_bytes=64)
+        w2_raw = keep.tile([P, PACK, N], F32, name="w2_raw", tag="w1_raw1", align_bytes=64)
         nc.sync.dma_start(out=w2_raw[:], in_=w2.rearrange("(p j) c -> p j c", j=PACK))
-        depth_sb = keep.tile([P, V], F32, name="depth_sb", tag="w1_raw1", align_bytes=64)
+        depth_sb = keep.tile([P, V], F32, name="depth_sb", tag="dealt1", align_bytes=64)
         nc.sync.dma_start(out=depth_sb[:], in_=depth)
         terms0 = [sb(f"terms0_{k}", [P, PACK, P], F32) for k in range(TERMS)]
         terms1 = [[sb(f"terms1_{u}{k}", [P, 2, P], F32) for k in range(TERMS)] for u in range(2)]
@@ -184,9 +181,18 @@ def tile_picked_ymvs_mean_p_kernel(tc, x_words, x_scales, w1, unit, w2, depth, o
                 )
                 nc.vector.scalar_tensor_tensor(out=contrasts[:, 2, :], in0=y3, scalar=-3.0, in1=triple_sum[:], op0=ALU.mult, op1=ALU.add)
             else:
-                for k, view_d, factor, rest in ((0, second[:, 0, :], -2.0, pair_sum), (2, y3, -3.0, triple_sum), (1, second[:, 1, :], -2.0, pair_sum)):
+                for k, view_d, factor, rest in ((0, second[:, 0, :], -2.0, pair_sum), (2, y3, -3.0, triple_sum)):
                     nc.vector.scalar_tensor_tensor(out=contrasts[:, k, :], in0=view_d, scalar=factor, in1=rest[:], op0=ALU.mult, op1=ALU.add)
+                by_t = lambda x, t: x.rearrange("p (g t m) -> p g t m", g=2, t=2)[:, :, t, :]
+                for t in range(2):
+                    nc.vector.scalar_tensor_tensor(
+                        out=by_t(contrasts[:, 1, :], t), in0=by_t(second[:, 1, :], t), scalar=-2.0, in1=by_t(pair_sum[:], t), op0=ALU.mult, op1=ALU.add
+                    )
             for k in (0, 2, 1):
+                if k == 1 and i == len(steps) - 1:
+                    for t in range(2):
+                        nc.scalar.activation(out=dst[k][:, :, t, :], in_=by_t(contrasts[:, 1, :], t), func=ACT.Square, scale=math.sqrt(WEIGHTS[k]))
+                    continue
                 src = view(contrasts[:, k, :])
                 if k == 2 and steps[i][0] == 0:
                     nc.gpsimd.tensor_tensor(out=dst[k], in0=src, in1=src, op=ALU.mult)

@@ -32,6 +32,7 @@ TERMS = 3
 FIRST_ROW = 32
 ROW_STEP = 4
 ZEROED_FIRST = 600
+ROWS_AHEAD = 3
 BANKS = 8
 WEIGHTS = (6.0, 2.0, 1.0)
 
@@ -62,8 +63,9 @@ def tile_picked_ymvs_mean_p_kernel(tc, x_words, x_scales, w1, unit, w2, depth, o
         w1_rows = w1.rearrange("(p j) c -> p j c", j=PACK)
         w1_raw = [sb(f"w1_raw{g}", [P, PACK, WIDE], F32) for g in range(2)]
         word_table = sb("word_table", [P, T], I32)
-        nc.scalar.dma_start(out=w1_raw[0][:], in_=w1_rows[:, :, 0:WIDE])
+        nc.scalar.dma_start(out=w1_raw[0][:, 0:ROWS_AHEAD], in_=w1_rows[:, 0:ROWS_AHEAD, 0:WIDE])
         nc.scalar.dma_start(out=scale_table[:].bitcast(I32)[FIRST_ROW : FIRST_ROW + ROW_STEP * BLOCKS : ROW_STEP, :], in_=x_scales[0].bitcast(I32))
+        nc.scalar.dma_start(out=w1_raw[0][:, ROWS_AHEAD:PACK], in_=w1_rows[:, ROWS_AHEAD:PACK, 0:WIDE])
         nc.scalar.dma_start(out=word_table[:], in_=x_words[0].rearrange("p n t -> p (n t)").bitcast(I32))
         nc.scalar.dma_start(out=w1_raw[1][:], in_=w1_rows[:, :, WIDE:H])
         unit_sb = sb("unit_sb", [P, PACK], F32)
@@ -180,24 +182,20 @@ def tile_picked_ymvs_mean_p_kernel(tc, x_words, x_scales, w1, unit, w2, depth, o
                     op0=ALU.mult, op1=ALU.add,
                 )
                 nc.vector.scalar_tensor_tensor(out=contrasts[:, 2, :], in0=y3, scalar=-3.0, in1=triple_sum[:], op0=ALU.mult, op1=ALU.add)
+                for k in (0, 2, 1):
+                    src = view(contrasts[:, k, :])
+                    if k == 2 and steps[i][0] == 0:
+                        nc.gpsimd.tensor_tensor(out=dst[k], in0=src, in1=src, op=ALU.mult)
+                    else:
+                        nc.scalar.activation(out=dst[k], in_=src, func=ACT.Square, scale=math.sqrt(WEIGHTS[k]))
             else:
-                for k, view_d, factor, rest in ((0, second[:, 0, :], -2.0, pair_sum), (2, y3, -3.0, triple_sum)):
-                    nc.vector.scalar_tensor_tensor(out=contrasts[:, k, :], in0=view_d, scalar=factor, in1=rest[:], op0=ALU.mult, op1=ALU.add)
-                by_t = lambda x, t: x.rearrange("p (g t m) -> p g t m", g=2, t=2)[:, :, t, :]
                 for t in range(2):
-                    nc.vector.scalar_tensor_tensor(
-                        out=by_t(contrasts[:, 1, :], t), in0=by_t(second[:, 1, :], t), scalar=-2.0, in1=by_t(pair_sum[:], t), op0=ALU.mult, op1=ALU.add
-                    )
-            for k in (0, 2, 1):
-                if k == 1 and i == len(steps) - 1:
-                    for t in range(2):
-                        nc.scalar.activation(out=dst[k][:, :, t, :], in_=by_t(contrasts[:, 1, :], t), func=ACT.Square, scale=math.sqrt(WEIGHTS[k]))
-                    continue
-                src = view(contrasts[:, k, :])
-                if k == 2 and steps[i][0] == 0:
-                    nc.gpsimd.tensor_tensor(out=dst[k], in0=src, in1=src, op=ALU.mult)
-                else:
-                    nc.scalar.activation(out=dst[k], in_=src, func=ACT.Square, scale=math.sqrt(WEIGHTS[k]))
+                    for k, view_d, factor, rest in ((0, second[:, 0, :], -2.0, pair_sum), (2, y3, -3.0, triple_sum), (1, second[:, 1, :], -2.0, pair_sum)):
+                        contrast = view(contrasts[:, k, :])[:, :, t, :]
+                        nc.vector.scalar_tensor_tensor(
+                            out=contrast, in0=view(view_d)[:, :, t, :], scalar=factor, in1=view(rest[:])[:, :, t, :], op0=ALU.mult, op1=ALU.add
+                        )
+                        nc.scalar.activation(out=dst[k][:, :, t, :], in_=contrast, func=ACT.Square, scale=math.sqrt(WEIGHTS[k]))
 
         def add_terms(acc, terms, count, opens=True, closes=True):
             order = (0, 2, 1)
@@ -223,7 +221,11 @@ def tile_picked_ymvs_mean_p_kernel(tc, x_words, x_scales, w1, unit, w2, depth, o
         sums1 = bank("sums1", [P, PACK, P], 5)
         for u in range(2):
             three_terms(last - 1 + u, *made[last - 1 + u])
-            add_terms(sums1[:, 2 * u : 2 * u + 2, :], terms1[u], 2, u == 0, u == 1)
+            if u == 0:
+                add_terms(sums1[:, 0:2, :], terms1[0], 2, True, False)
+            else:
+                for t in range(2):
+                    add_terms(sums1[:, 2 + t : 3 + t, :], [term[:, t : t + 1, :] for term in terms1[1]], 1, False, t == 1)
         w2_codes = keep.tile([P, N], U32, name="w2_codes", tag="pair_sum3", align_bytes=64)
         nc.vector.quantize_mx(out=w2_codes[:].bitcast(FP8X4), scales=w2_plane[:], in_=w2_bf[:].rearrange("p c j -> p (c j)"))
 

@@ -31,7 +31,6 @@ FIRST_SHARE = 40
 TERMS = 3
 FIRST_ROW = 32
 ROW_STEP = 4
-ZEROED_FIRST = 600
 ROWS_AHEAD = 3
 BANKS = 8
 WEIGHTS = (6.0, 2.0, 1.0)
@@ -55,15 +54,15 @@ def tile_picked_ymvs_mean_p_kernel(tc, x_words, x_scales, w1, unit, w2, depth, o
         nc.sync.dma_start(out=unit_raw[:], in_=unit.rearrange("(p t) o -> p (t o)", t=PACK))
 
         scale_table = sb("scale_table", [P, T], U8)
-        nc.gpsimd.memset(scale_table[:].bitcast(I32)[:, 0:ZEROED_FIRST], 0)
-        nc.vector.memset(scale_table[:].bitcast(I32)[:, ZEROED_FIRST:], 0)
+        nc.vector.memset(scale_table[:].bitcast(I32), 0)
         x_plane = sb("x_plane", [P, S], U8)
         nc.vector.memset(x_plane[:].bitcast(I32), 0)
 
         w1_rows = w1.rearrange("(p j) c -> p j c", j=PACK)
         w1_raw = [sb(f"w1_raw{g}", [P, PACK, WIDE], F32) for g in range(2)]
         word_table = sb("word_table", [P, T], I32)
-        nc.scalar.dma_start(out=w1_raw[0][:, 0:ROWS_AHEAD], in_=w1_rows[:, 0:ROWS_AHEAD, 0:WIDE])
+        for j0, j1 in ((0, 1), (1, ROWS_AHEAD)):
+            nc.scalar.dma_start(out=w1_raw[0][:, j0:j1], in_=w1_rows[:, j0:j1, 0:WIDE])
         nc.scalar.dma_start(out=scale_table[:].bitcast(I32)[FIRST_ROW : FIRST_ROW + ROW_STEP * BLOCKS : ROW_STEP, :], in_=x_scales[0].bitcast(I32))
         nc.scalar.dma_start(out=w1_raw[0][:, ROWS_AHEAD:PACK], in_=w1_rows[:, ROWS_AHEAD:PACK, 0:WIDE])
         nc.scalar.dma_start(out=word_table[:], in_=x_words[0].rearrange("p n t -> p (n t)").bitcast(I32))
@@ -71,7 +70,7 @@ def tile_picked_ymvs_mean_p_kernel(tc, x_words, x_scales, w1, unit, w2, depth, o
         unit_sb = sb("unit_sb", [P, PACK], F32)
         nc.scalar.activation(out=unit_sb[:], in_=unit_raw[:], func=ACT.Copy, scale=1.0 / 48)
 
-        ident = sb("ident", [P, P], F32)
+        ident = keep.tile([P, P], F32, name="ident", tag="unit_raw", align_bytes=64)
         make_identity(nc, ident[:])
 
         picked_scales = sb("picked_scales", [P, S], U8)

@@ -75,16 +75,17 @@ def tile_picked_ymvs_mean_p_kernel(tc, x_words, x_scales, w1, unit, w2, depth, o
 
         picked_scales = sb("picked_scales", [P, S], U8)
         nc.vector.tensor_copy(picked_scales[:], scale_table[:].indirect(offsets[:]))
-        scales_by_view = sb("scales_by_view", [P, S], U8)
-        nc.vector.tensor_copy(
-            out=scales_by_view[:].rearrange("p (h d v) -> p h d v", h=HALVES, d=D),
-            in_=picked_scales[:].rearrange("p (h v d) -> p h d v", h=HALVES, d=D),
-        )
-        for q in range(QUADRANTS):
-            nc.sync.dma_start(
-                out=x_plane[:].bitcast(I32)[32 * q : 32 * q + 4, :],
-                in_=scales_by_view[:].bitcast(I32)[FIRST_ROW + ROW_STEP * 4 * q : FIRST_ROW + ROW_STEP * 4 * (q + 1) : ROW_STEP, :],
+        for h in range(HALVES):
+            scales_by_view = sb(f"scales_by_view{h}", [P, ENTRIES], U8)
+            nc.vector.tensor_copy(
+                out=scales_by_view[:].rearrange("p (d v) -> p d v", d=D),
+                in_=picked_scales[:, h * ENTRIES : (h + 1) * ENTRIES].rearrange("p (v d) -> p d v", d=D),
             )
+            for q in range(QUADRANTS):
+                nc.sync.dma_start(
+                    out=x_plane[:].bitcast(I32)[32 * q : 32 * q + 4, h * ENTRIES // 4 : (h + 1) * ENTRIES // 4],
+                    in_=scales_by_view[:].bitcast(I32)[FIRST_ROW + ROW_STEP * 4 * q : FIRST_ROW + ROW_STEP * 4 * (q + 1) : ROW_STEP, :],
+                )
 
         w1_codes = [sb(f"w1_codes{g}", [P, WIDE], U32) for g in range(2)]
         w1_plane = [sb(f"w1_plane{g}", [P, WIDE], U8) for g in range(2)]

@@ -66,7 +66,8 @@ def tile_picked_ymvs_mean_p_kernel(tc, x_words, x_scales, w1, unit, w2, depth, o
         nc.scalar.dma_start(out=scale_table[:].bitcast(I32)[FIRST_ROW : FIRST_ROW + ROW_STEP * BLOCKS : ROW_STEP, :], in_=x_scales[0].bitcast(I32))
         nc.scalar.dma_start(out=w1_raw[0][:, ROWS_AHEAD:PACK], in_=w1_rows[:, ROWS_AHEAD:PACK, 0:WIDE])
         nc.scalar.dma_start(out=word_table[:], in_=x_words[0].rearrange("p n t -> p (n t)").bitcast(I32))
-        nc.scalar.dma_start(out=w1_raw[1][:], in_=w1_rows[:, :, WIDE:H])
+        for j0 in (0, 2):
+            nc.scalar.dma_start(out=w1_raw[1][:, j0 : j0 + 2], in_=w1_rows[:, j0 : j0 + 2, WIDE:H])
         unit_sb = sb("unit_sb", [P, PACK], F32)
         nc.scalar.activation(out=unit_sb[:], in_=unit_raw[:], func=ACT.Copy, scale=1.0 / 48)
 
@@ -91,10 +92,10 @@ def tile_picked_ymvs_mean_p_kernel(tc, x_words, x_scales, w1, unit, w2, depth, o
         w1_plane = [sb(f"w1_plane{g}", [P, WIDE], U8) for g in range(2)]
         w1_bf = [keep.tile([P, PACK, GROUPS, PACK], BF16, name=f"w1_bf{g}", tag=f"dealt{g}", align_bytes=64) for g in range(2)]
 
-        def deal_w1(copy, g, m0, m1):
+        def deal_w1(copy, g, m0, m1, j0=0, j1=PACK):
             copy(
-                out=w1_bf[g][:, :, m0:m1, :].rearrange("p t m j -> p m t j"),
-                in_=w1_raw[g][:].rearrange("p j (m t) -> p m t j", t=PACK)[:, m0:m1],
+                out=w1_bf[g][:, :, m0:m1, j0:j1].rearrange("p t m j -> p m t j"),
+                in_=w1_raw[g][:, j0:j1].rearrange("p j (m t) -> p m t j", t=PACK)[:, m0:m1],
             )
 
         def gpsimd_cast(out, in_):
@@ -118,8 +119,9 @@ def tile_picked_ymvs_mean_p_kernel(tc, x_words, x_scales, w1, unit, w2, depth, o
         deal_w1(gpsimd_cast, 0, FIRST_SHARE, GROUPS)
         quantize_w1(0, 0, PACK)
         x_codes = [gather_words(h) for h in range(HALVES)]
-        deal_w1(nc.scalar.copy, 1, 0, SCALAR_SHARE)
-        deal_w1(gpsimd_cast, 1, SCALAR_SHARE, GROUPS)
+        for j0 in (0, 2):
+            deal_w1(nc.scalar.copy, 1, 0, SCALAR_SHARE, j0, j0 + 2)
+            deal_w1(gpsimd_cast, 1, SCALAR_SHARE, GROUPS, j0, j0 + 2)
         quantize_w1(1, 0, PACK)
 
         w2_bf = keep.tile([P, N, PACK], BF16, name="w2_bf", tag="w2_bf", align_bytes=64)

@@ -186,7 +186,7 @@ def tile_picked_ymvs_mean_p_kernel(tc, x_words, x_scales, w1, unit, w2, depth, o
                 nc.vector.scalar_tensor_tensor(out=contrasts[:, 2, :], in0=y3, scalar=-3.0, in1=triple_sum[:], op0=ALU.mult, op1=ALU.add)
                 for k in (0, 2, 1):
                     src = view(contrasts[:, k, :])
-                    if k == 2 and steps[i][0] == 0:
+                    if k == 2:
                         nc.gpsimd.tensor_tensor(out=dst[k], in0=src, in1=src, op=ALU.mult)
                     else:
                         nc.scalar.activation(out=dst[k], in_=src, func=ACT.Square, scale=math.sqrt(WEIGHTS[k]))
@@ -264,7 +264,7 @@ def tile_picked_ymvs_mean_p_kernel(tc, x_words, x_scales, w1, unit, w2, depth, o
                 ),
                 lambda: nc.scalar.activation(out=ex[:], in_=shifted[:], func=ACT.Exp),
                 lambda: nc.vector.tensor_reduce(out=total[:], in_=ex[:], axis=AXIS_X, op=ALU.add),
-                lambda: nc.vector.tensor_tensor(out=weighted[:], in0=ex[:], in1=depths, op=ALU.mult),
+                lambda: (nc.gpsimd if v0 == 0 else nc.vector).tensor_tensor(out=weighted[:], in0=ex[:], in1=depths, op=ALU.mult),
                 lambda: nc.vector.reciprocal(out=inverse[:], in_=total[:]),
                 lambda: nc.vector.tensor_reduce(out=weighted_total[:], in_=weighted[:], axis=AXIS_X, op=ALU.add),
                 lambda: nc.vector.tensor_tensor(out=result[:, v0 // D : v1 // D], in0=weighted_total[:], in1=inverse[:], op=ALU.mult),
@@ -275,10 +275,20 @@ def tile_picked_ymvs_mean_p_kernel(tc, x_words, x_scales, w1, unit, w2, depth, o
         middle = P + P // 2
         scale_z(sums1[:, :, 0 : P // 2], P, middle)
         scale_z(sums1[:, :, P // 2 : P], middle, V)
-        second_set = [(v0, v1, costs(v0, v1, number)) for v0, v1, number in ((P, middle, 7), (middle, V, 0))]
-        for pair in zip(*[soft_depth(*piece) for piece in second_set]):
-            for issue in pair:
-                issue()
-        for issue in soft_depth(*first_set):
+        early = soft_depth(*first_set)
+        late = [soft_depth(P, middle, costs(P, middle, 7))]
+        early[0]()
+        late.append(soft_depth(middle, V, costs(middle, V, 0)))
+        early[1]()
+        early[2]()
+        for stage in range(3):
+            for piece in late:
+                piece[stage]()
+        for issue in early[3:6]:
             issue()
+        for stage in range(3, len(early)):
+            for piece in late:
+                piece[stage]()
+            if stage in (4, 5):
+                early[stage + 2]()
         nc.sync.dma_start(out=out, in_=result[:])

@@ -159,18 +159,13 @@ def tile_picked_ymvs_mean_p_kernel(tc, x_words, x_scales, w1, unit, w2, depth, o
             width = sum(c1 - c0 for g, c0, c1 in pieces)
             first = bank(f"first{i}", [P, 2, width], 2 * i % BANKS)
             second = bank(f"second{i}", [P, 2, width], (2 * i + 1) % BANKS)
-            order = [(first[:, 0, :], (0, 1)), (second[:, 0, :], (1,)), (second[:, 1, :], (2,))]
-            if i == 0:
-                y3 = bank("third0", [P, width], BANKS - 1)[:]
-                order.append((y3, (3,)))
-            else:
-                y3 = first[:, 1, :]
-                order.insert(1, (y3, (3,)))
-            for acc, views in order:
+            y3 = bank("third0", [P, width], BANKS - 1)[:] if i == 0 else first[:, 1, :]
+            pair_sum = keep.tile([P, width], F32, name=f"pair_sum{i}", align_bytes=64)
+            for acc, views in ((first[:, 0, :], (0, 1)), (second[:, 0, :], (1,)), (second[:, 1, :], (2,)), (y3, (3,))):
                 for n, (g, c0, c1) in enumerate(pieces):
                     product(acc[:, n * (c1 - c0) : (n + 1) * (c1 - c0)], h, views, g, c0, c1)
-            pair_sum = keep.tile([P, width], F32, name=f"pair_sum{i}", align_bytes=64)
-            nc.scalar.copy(out=pair_sum[:], in_=first[:, 0, :])
+                if views == (0, 1):
+                    nc.scalar.copy(out=pair_sum[:], in_=first[:, 0, :])
             return width, y3, second, pair_sum
 
         def three_terms(i, width, y3, second, pair_sum):
@@ -255,7 +250,14 @@ def tile_picked_ymvs_mean_p_kernel(tc, x_words, x_scales, w1, unit, w2, depth, o
         def soft_depth(v0, v1, sc):
             pixels = (v1 - v0) // D
             shifted, ex, weighted = [sb(f"{n}{v0}", [P, pixels, D], F32) for n in ("shifted", "ex", "weighted")]
-            top, total, inverse, weighted_total = [sb(f"{n}{v0}", [P, pixels], F32) for n in ("top", "total", "inverse", "weighted_total")]
+            top, total, inverse = [sb(f"{n}{v0}", [P, pixels], F32) for n in ("top", "total", "inverse")]
+            sums = []
+
+            def weighted_sum():
+                tag = f"ex{P + P // 2}" if v0 == 0 else f"weighted_total{v0}"
+                sums.append(keep.tile([P, pixels], F32, name=f"weighted_total{v0}", tag=tag, align_bytes=64))
+                nc.vector.tensor_reduce(out=sums[0][:], in_=weighted[:], axis=AXIS_X, op=ALU.add)
+
             depths = depth_sb[:, v0:v1].rearrange("p (g d) -> p g d", d=D)
             return [
                 lambda: nc.vector.tensor_reduce(out=top[:], in_=sc[:], axis=AXIS_X, op=ALU.max),
@@ -266,8 +268,8 @@ def tile_picked_ymvs_mean_p_kernel(tc, x_words, x_scales, w1, unit, w2, depth, o
                 lambda: nc.vector.tensor_reduce(out=total[:], in_=ex[:], axis=AXIS_X, op=ALU.add),
                 lambda: (nc.gpsimd if v0 == 0 else nc.vector).tensor_tensor(out=weighted[:], in0=ex[:], in1=depths, op=ALU.mult),
                 lambda: nc.vector.reciprocal(out=inverse[:], in_=total[:]),
-                lambda: nc.vector.tensor_reduce(out=weighted_total[:], in_=weighted[:], axis=AXIS_X, op=ALU.add),
-                lambda: nc.vector.tensor_tensor(out=result[:, v0 // D : v1 // D], in0=weighted_total[:], in1=inverse[:], op=ALU.mult),
+                weighted_sum,
+                lambda: nc.vector.tensor_tensor(out=result[:, v0 // D : v1 // D], in0=sums[0][:], in1=inverse[:], op=ALU.mult),
             ]
 
         scale_z(sums0[:], 0, P)

@@ -194,8 +194,7 @@ def tile_picked_ymvs_mean_p_kernel(tc, x_words, x_scales, w1, unit, w2, depth, o
                         )
                         nc.scalar.activation(out=dst[k][:, :, t, :], in_=contrast, func=ACT.Square, scale=math.sqrt(WEIGHTS[k]))
 
-        def add_terms(acc, terms, count, opens=True, closes=True):
-            order = (0, 2, 1)
+        def add_terms(acc, terms, count, order, opens=True, closes=True):
             for k in order:
                 for i in range(count):
                     nc.tensor.matmul(
@@ -214,15 +213,15 @@ def tile_picked_ymvs_mean_p_kernel(tc, x_words, x_scales, w1, unit, w2, depth, o
                 made.append(products(i + 2))
                 three_terms(i, *made[i])
         sums0 = bank("sums0", [P, PACK, P], 4)
-        add_terms(sums0, terms0, PACK)
+        add_terms(sums0, terms0, PACK, (0, 1, 2))
         sums1 = bank("sums1", [P, PACK, P], 5)
         for u in range(2):
             three_terms(last - 1 + u, *made[last - 1 + u])
             if u == 0:
-                add_terms(sums1[:, 0:2, :], terms1[0], 2, True, False)
+                add_terms(sums1[:, 0:2, :], terms1[0], 2, (0, 1, 2), True, False)
             else:
                 for t in range(2):
-                    add_terms(sums1[:, 2 + t : 3 + t, :], [term[:, t : t + 1, :] for term in terms1[1]], 1, False, t == 1)
+                    add_terms(sums1[:, 2 + t : 3 + t, :], [term[:, t : t + 1, :] for term in terms1[1]], 1, (0, 2, 1), False, t == 1)
         w2_codes = keep.tile([P, N], U32, name="w2_codes", tag="pair_sum3", align_bytes=64)
         nc.vector.quantize_mx(out=w2_codes[:].bitcast(FP8X4), scales=w2_plane[:], in_=w2_bf[:].rearrange("p c j -> p (c j)"))
 

@@ -34,6 +34,8 @@ ROW_STEP = 4
 ROWS_AHEAD = 3
 BANKS = 8
 WEIGHTS = (6.0, 2.0, 1.0)
+CROSS_WEIGHTS = (4.0, 1.5, 1.5)
+CROSS_SCALE = math.sqrt(1.5)
 
 
 def tile_picked_ymvs_mean_p_kernel(tc, x_words, x_scales, w1, unit, w2, depth, offs, out):
@@ -88,8 +90,8 @@ def tile_picked_ymvs_mean_p_kernel(tc, x_words, x_scales, w1, unit, w2, depth, o
                     in_=scales_by_view[:].bitcast(I32)[FIRST_ROW + ROW_STEP * 4 * q : FIRST_ROW + ROW_STEP * 4 * (q + 1) : ROW_STEP, :],
                 )
 
-        w1_codes = [sb(f"w1_codes{g}", [P, WIDE], U32) for g in range(2)]
-        w1_plane = [sb(f"w1_plane{g}", [P, WIDE], U8) for g in range(2)]
+        w1_codes = sb("w1_codes", [P, H], U32)
+        w1_plane = sb("w1_plane", [P, H], U8)
         w1_bf = [keep.tile([P, PACK, GROUPS, PACK], BF16, name=f"w1_bf{g}", tag=f"dealt{g}", align_bytes=64) for g in range(2)]
 
         def deal_w1(copy, g, m0, m1, j0=0, j1=PACK):
@@ -102,9 +104,9 @@ def tile_picked_ymvs_mean_p_kernel(tc, x_words, x_scales, w1, unit, w2, depth, o
             nc.gpsimd.tensor_scalar(out=out, in0=in_, scalar1=1.0, scalar2=0.0, op0=ALU.mult, op1=ALU.add)
 
         def quantize_w1(g, t0, t1):
-            cols = slice(t0 * GROUPS, t1 * GROUPS)
+            cols = slice(t0 * P + g * P, t0 * P + (g + 1) * P)
             nc.vector.quantize_mx(
-                out=w1_codes[g][:, cols].bitcast(FP8X4), scales=w1_plane[g][:, cols], in_=w1_bf[g][:, t0:t1].rearrange("p t m j -> p (t m j)")
+                out=w1_codes[:, cols].bitcast(FP8X4), scales=w1_plane[:, cols], in_=w1_bf[g][:, t0:t1].rearrange("p t m j -> p (t m j)")
             )
 
         def gather_words(h):
@@ -117,21 +119,23 @@ def tile_picked_ymvs_mean_p_kernel(tc, x_words, x_scales, w1, unit, w2, depth, o
 
         deal_w1(nc.scalar.copy, 0, 0, FIRST_SHARE)
         deal_w1(gpsimd_cast, 0, FIRST_SHARE, GROUPS)
-        quantize_w1(0, 0, PACK)
+        for t in (0, 2):
+            quantize_w1(0, t, t + 2)
         x_codes = [gather_words(h) for h in range(HALVES)]
         for j0 in (0, 2):
             deal_w1(nc.scalar.copy, 1, 0, SCALAR_SHARE, j0, j0 + 2)
             deal_w1(gpsimd_cast, 1, SCALAR_SHARE, GROUPS, j0, j0 + 2)
-        quantize_w1(1, 0, PACK)
+        for t in (0, 2):
+            quantize_w1(1, t, t + 2)
 
         w2_bf = keep.tile([P, N, PACK], BF16, name="w2_bf", tag="w2_bf", align_bytes=64)
         w2_plane = sb("w2_plane", [P, N], U8)
 
-        def product(acc, h, views, g, c0, c1):
+        def product(acc, h, views, c0, c1):
             for d in views:
                 nc.tensor.matmul_mx(
                     out=acc, lhsT=x_codes[h][:, d, :].bitcast(FP8X4), lhsT_scale=x_plane[:, h * ENTRIES + d * P : h * ENTRIES + (d + 1) * P],
-                    rhs=w1_codes[g][:, c0:c1].bitcast(FP8X4), rhs_scale=w1_plane[g][:, c0:c1],
+                    rhs=w1_codes[:, c0:c1].bitcast(FP8X4), rhs_scale=w1_plane[:, c0:c1],
                     start=(d == views[0]), stop=(d == views[-1]),
                 )
 
@@ -140,32 +144,34 @@ def tile_picked_ymvs_mean_p_kernel(tc, x_words, x_scales, w1, unit, w2, depth, o
         depth_sb = keep.tile([P, V], F32, name="depth_sb", tag="dealt1", align_bytes=64)
         nc.sync.dma_start(out=depth_sb[:], in_=depth)
         terms0 = [sb(f"terms0_{k}", [P, PACK, P], F32) for k in range(TERMS)]
-        terms1 = [[sb(f"terms1_{u}{k}", [P, 2, P], F32) for k in range(TERMS)] for u in range(2)]
+        terms1 = [[sb(f"terms1_{u}{k}", [P, 2, P], F32) for k in range(TERMS + 1 - u)] for u in range(2)]
 
         def first_set_step(g, t0, t1):
-            pieces = [(g, t0 * GROUPS, t1 * GROUPS)]
+            pieces = (t0 * P + g * P, t0 * P + (g + 1) * P)
             dst = [terms0[k][:, t0:t1, g * GROUPS : (g + 1) * GROUPS] for k in range(TERMS)]
             return 0, pieces, dst, lambda x: x.rearrange("p (t m) -> p t m", m=GROUPS)
 
         def second_set_step(u):
-            pieces = [(g, u * P, (u + 1) * P) for g in range(2)]
-            dst = [terms1[u][k][:].rearrange("p t (g m) -> p g t m", g=2) for k in range(TERMS)]
+            pieces = (u * WIDE, (u + 1) * WIDE)
+            dst = [term[:].rearrange("p t (g m) -> p g t m", g=2) for term in terms1[u]]
             return 1, pieces, dst, lambda x: x.rearrange("p (g t m) -> p g t m", g=2, t=2)
 
         steps = [first_set_step(g, t, t + 2) for g in range(2) for t in (0, 2)] + [second_set_step(u) for u in range(2)]
 
         def products(i):
-            h, pieces = steps[i][:2]
-            width = sum(c1 - c0 for g, c0, c1 in pieces)
+            h, (c0, c1) = steps[i][:2]
+            width = c1 - c0
             first = bank(f"first{i}", [P, 2, width], 2 * i % BANKS)
             second = bank(f"second{i}", [P, 2, width], (2 * i + 1) % BANKS)
             y3 = bank("third0", [P, width], BANKS - 1)[:] if i == 0 else first[:, 1, :]
             pair_sum = keep.tile([P, width], F32, name=f"pair_sum{i}", align_bytes=64)
             for acc, views in ((first[:, 0, :], (0, 1)), (second[:, 0, :], (1,)), (second[:, 1, :], (2,)), (y3, (3,))):
-                for n, (g, c0, c1) in enumerate(pieces):
-                    product(acc[:, n * (c1 - c0) : (n + 1) * (c1 - c0)], h, views, g, c0, c1)
+                product(acc, h, views, c0, c1)
                 if views == (0, 1):
-                    nc.scalar.copy(out=pair_sum[:], in_=first[:, 0, :])
+                    if i == len(steps) - 2:
+                        nc.scalar.activation(out=pair_sum[:], in_=first[:, 0, :], func=ACT.Copy, scale=CROSS_SCALE)
+                    else:
+                        nc.scalar.copy(out=pair_sum[:], in_=first[:, 0, :])
             return width, y3, second, pair_sum
 
         def three_terms(i, width, y3, second, pair_sum):
@@ -194,6 +200,18 @@ def tile_picked_ymvs_mean_p_kernel(tc, x_words, x_scales, w1, unit, w2, depth, o
                         )
                         nc.scalar.activation(out=dst[k][:, :, t, :], in_=contrast, func=ACT.Square, scale=math.sqrt(WEIGHTS[k]))
 
+        def four_terms(i, width, y3, second, pair_sum):
+            dst, view = steps[i][2:]
+            contrasts = sb(f"contrasts{i}", [P, TERMS, width], F32)
+            nc.vector.scalar_tensor_tensor(
+                out=contrasts[:, 0:2, :], in0=second[:], scalar=-2.0 * CROSS_SCALE, in1=pair_sum[:].unsqueeze(1).to_broadcast([P, 2, width]),
+                op0=ALU.mult, op1=ALU.add,
+            )
+            nc.vector.scalar_tensor_tensor(out=contrasts[:, 2, :], in0=y3, scalar=2.0 * CROSS_SCALE, in1=pair_sum[:], op0=ALU.mult, op1=ALU.subtract)
+            for k in range(TERMS):
+                nc.scalar.activation(out=dst[k], in_=view(contrasts[:, k, :]), func=ACT.Square, scale=math.sqrt(CROSS_WEIGHTS[k]))
+            nc.gpsimd.tensor_tensor(out=dst[TERMS], in0=view(contrasts[:, 1, :]), in1=view(contrasts[:, 2, :]), op=ALU.mult)
+
         def add_terms(acc, terms, count, order, opens=True, closes=True):
             for k in order:
                 for i in range(count):
@@ -216,9 +234,9 @@ def tile_picked_ymvs_mean_p_kernel(tc, x_words, x_scales, w1, unit, w2, depth, o
         add_terms(sums0, terms0, PACK, (0, 1, 2))
         sums1 = bank("sums1", [P, PACK, P], 5)
         for u in range(2):
-            three_terms(last - 1 + u, *made[last - 1 + u])
+            (four_terms, three_terms)[u](last - 1 + u, *made[last - 1 + u])
             if u == 0:
-                add_terms(sums1[:, 0:2, :], terms1[0], 2, (0, 1, 2), True, False)
+                add_terms(sums1[:, 0:2, :], terms1[0], 2, (0, 1, 2, 3), True, False)
             else:
                 for t in range(2):
                     add_terms(sums1[:, 2 + t : 3 + t, :], [term[:, t : t + 1, :] for term in terms1[1]], 1, (0, 2, 1), False, t == 1)

@@ -36,6 +36,7 @@ BANKS = 8
 WEIGHTS = (6.0, 2.0, 1.0)
 CROSS_WEIGHTS = (4.0, 1.5, 1.5)
 CROSS_SCALE = math.sqrt(1.5)
+FOUR_TERMS = (4,)
 
 
 def tile_picked_ymvs_mean_p_kernel(tc, x_words, x_scales, w1, unit, w2, depth, offs, out):
@@ -139,21 +140,21 @@ def tile_picked_ymvs_mean_p_kernel(tc, x_words, x_scales, w1, unit, w2, depth, o
                     start=(d == views[0]), stop=(d == views[-1]),
                 )
 
-        w2_raw = keep.tile([P, PACK, N], F32, name="w2_raw", tag="w1_raw1", align_bytes=64)
+        w2_raw = keep.tile([P, PACK, N], F32, name="w2_raw", tag="picked_scales", align_bytes=64)
         nc.sync.dma_start(out=w2_raw[:], in_=w2.rearrange("(p j) c -> p j c", j=PACK))
         depth_sb = keep.tile([P, V], F32, name="depth_sb", tag="dealt1", align_bytes=64)
         nc.sync.dma_start(out=depth_sb[:], in_=depth)
-        terms0 = [sb(f"terms0_{k}", [P, PACK, P], F32) for k in range(TERMS)]
-        terms1 = [[sb(f"terms1_{u}{k}", [P, 2, P], F32) for k in range(TERMS + 1 - u)] for u in range(2)]
+        terms0 = [sb(f"terms0_{u}", [P, TERMS + (u in FOUR_TERMS), 2, P], F32) for u in range(2)]
+        terms1 = [sb(f"terms1_{u}", [P, TERMS + (4 + u in FOUR_TERMS), 2, P], F32) for u in range(2)]
 
         def first_set_step(g, t0, t1):
             pieces = (t0 * P + g * P, t0 * P + (g + 1) * P)
-            dst = [terms0[k][:, t0:t1, g * GROUPS : (g + 1) * GROUPS] for k in range(TERMS)]
+            dst = [terms0[t0 // 2][:, k, :, g * GROUPS : (g + 1) * GROUPS] for k in range(terms0[t0 // 2].shape[1])]
             return 0, pieces, dst, lambda x: x.rearrange("p (t m) -> p t m", m=GROUPS)
 
         def second_set_step(u):
             pieces = (u * WIDE, (u + 1) * WIDE)
-            dst = [term[:].rearrange("p t (g m) -> p g t m", g=2) for term in terms1[u]]
+            dst = [terms1[u][:, k].rearrange("p t (g m) -> p g t m", g=2) for k in range(terms1[u].shape[1])]
             return 1, pieces, dst, lambda x: x.rearrange("p (g t m) -> p g t m", g=2, t=2)
 
         steps = [first_set_step(g, t, t + 2) for g in range(2) for t in (0, 2)] + [second_set_step(u) for u in range(2)]
@@ -168,7 +169,7 @@ def tile_picked_ymvs_mean_p_kernel(tc, x_words, x_scales, w1, unit, w2, depth, o
             for acc, views in ((first[:, 0, :], (0, 1)), (second[:, 0, :], (1,)), (second[:, 1, :], (2,)), (y3, (3,))):
                 product(acc, h, views, c0, c1)
                 if views == (0, 1):
-                    if i == len(steps) - 2:
+                    if i in FOUR_TERMS:
                         nc.scalar.activation(out=pair_sum[:], in_=first[:, 0, :], func=ACT.Copy, scale=CROSS_SCALE)
                     else:
                         nc.scalar.copy(out=pair_sum[:], in_=first[:, 0, :])
@@ -198,7 +199,10 @@ def tile_picked_ymvs_mean_p_kernel(tc, x_words, x_scales, w1, unit, w2, depth, o
                         nc.vector.scalar_tensor_tensor(
                             out=contrast, in0=view(view_d)[:, :, t, :], scalar=factor, in1=view(rest[:])[:, :, t, :], op0=ALU.mult, op1=ALU.add
                         )
-                        nc.scalar.activation(out=dst[k][:, :, t, :], in_=contrast, func=ACT.Square, scale=math.sqrt(WEIGHTS[k]))
+                        if (t, k) == (0, 2):
+                            nc.gpsimd.tensor_tensor(out=dst[k][:, :, t, :], in0=contrast, in1=contrast, op=ALU.mult)
+                        else:
+                            nc.scalar.activation(out=dst[k][:, :, t, :], in_=contrast, func=ACT.Square, scale=math.sqrt(WEIGHTS[k]))
 
         def four_terms(i, width, y3, second, pair_sum):
             dst, view = steps[i][2:]
@@ -208,15 +212,26 @@ def tile_picked_ymvs_mean_p_kernel(tc, x_words, x_scales, w1, unit, w2, depth, o
                 op0=ALU.mult, op1=ALU.add,
             )
             nc.vector.scalar_tensor_tensor(out=contrasts[:, 2, :], in0=y3, scalar=2.0 * CROSS_SCALE, in1=pair_sum[:], op0=ALU.mult, op1=ALU.subtract)
-            for k in range(TERMS):
-                nc.scalar.activation(out=dst[k], in_=view(contrasts[:, k, :]), func=ACT.Square, scale=math.sqrt(CROSS_WEIGHTS[k]))
+            nc.scalar.activation(out=dst[0], in_=view(contrasts[:, 0, :]), func=ACT.Square, scale=math.sqrt(CROSS_WEIGHTS[0]))
+            if width == P:
+                g, u = divmod(i, 2)
+                nc.scalar.activation(
+                    out=terms0[u][:, 1:TERMS, :, g * GROUPS : (g + 1) * GROUPS], in_=contrasts[:, 1:TERMS, :].rearrange("p k (t m) -> p k t m", t=2),
+                    func=ACT.Square, scale=math.sqrt(CROSS_WEIGHTS[1]),
+                )
+            else:
+                for k in range(1, TERMS):
+                    nc.scalar.activation(out=dst[k], in_=view(contrasts[:, k, :]), func=ACT.Square, scale=math.sqrt(CROSS_WEIGHTS[k]))
             nc.gpsimd.tensor_tensor(out=dst[TERMS], in0=view(contrasts[:, 1, :]), in1=view(contrasts[:, 2, :]), op=ALU.mult)
+
+        def terms_of(i):
+            (four_terms if i in FOUR_TERMS else three_terms)(i, *made[i])
 
         def add_terms(acc, terms, count, order, opens=True, closes=True):
             for k in order:
                 for i in range(count):
                     nc.tensor.matmul(
-                        out=acc[:, i, :], lhsT=terms[k][:, i, :], rhs=ident[:], is_transpose=True,
+                        out=acc[:, i, :], lhsT=terms[:, k, i, :], rhs=ident[:], is_transpose=True,
                         start=(opens and k == order[0] and i == 0), stop=(closes and k == order[-1] and i == count - 1),
                     )
 
@@ -225,21 +240,22 @@ def tile_picked_ymvs_mean_p_kernel(tc, x_words, x_scales, w1, unit, w2, depth, o
         nc.gpsimd.tensor_scalar(out=w2_bf[:], in0=w2_raw[:].rearrange("p j c -> p c j"), scalar1=1.0, scalar2=0.0, op0=ALU.mult, op1=ALU.add)
         for i in range(last - 1):
             if i == last - 2:
-                three_terms(i, *made[i])
+                terms_of(i)
                 made.append(products(i + 2))
             else:
                 made.append(products(i + 2))
-                three_terms(i, *made[i])
+                terms_of(i)
         sums0 = bank("sums0", [P, PACK, P], 4)
-        add_terms(sums0, terms0, PACK, (0, 1, 2))
+        for u in range(2):
+            add_terms(sums0[:, 2 * u : 2 * u + 2, :], terms0[u], 2, range(terms0[u].shape[1]), u == 0, u == 1)
         sums1 = bank("sums1", [P, PACK, P], 5)
         for u in range(2):
-            (four_terms, three_terms)[u](last - 1 + u, *made[last - 1 + u])
+            terms_of(last - 1 + u)
             if u == 0:
-                add_terms(sums1[:, 0:2, :], terms1[0], 2, (0, 1, 2, 3), True, False)
+                add_terms(sums1[:, 0:2, :], terms1[0], 2, range(terms1[0].shape[1]), True, False)
             else:
                 for t in range(2):
-                    add_terms(sums1[:, 2 + t : 3 + t, :], [term[:, t : t + 1, :] for term in terms1[1]], 1, (0, 2, 1), False, t == 1)
+                    add_terms(sums1[:, 2 + t : 3 + t, :], terms1[1][:, :, t : t + 1, :], 1, ((0, 1, 2), (0, 2, 1))[t], False, t == 1)
         w2_codes = keep.tile([P, N], U32, name="w2_codes", tag="pair_sum3", align_bytes=64)
         nc.vector.quantize_mx(out=w2_codes[:].bitcast(FP8X4), scales=w2_plane[:], in_=w2_bf[:].rearrange("p c j -> p (c j)"))
 
@@ -262,52 +278,43 @@ def tile_picked_ymvs_mean_p_kernel(tc, x_words, x_scales, w1, unit, w2, depth, o
             )
             return sc
 
-        result = sb("result", [P, V // D], F32)
+        pixels = V // D
+        shifted, ex, weighted = [sb(n, [P, pixels, D], F32) for n in ("shifted", "ex", "weighted")]
+        top, total, inverse, weighted_total, result = [sb(n, [P, pixels], F32) for n in ("top", "total", "inverse", "weighted_total", "result")]
+        depths = depth_sb[:].rearrange("p (g d) -> p g d", d=D)
 
-        def soft_depth(v0, v1, sc):
-            pixels = (v1 - v0) // D
-            shifted, ex, weighted = [sb(f"{n}{v0}", [P, pixels, D], F32) for n in ("shifted", "ex", "weighted")]
-            top, total, inverse = [sb(f"{n}{v0}", [P, pixels], F32) for n in ("top", "total", "inverse")]
-            sums = []
+        def largest(g, sc):
+            nc.vector.tensor_reduce(out=top[:, g], in_=sc[:], axis=AXIS_X, op=ALU.max)
 
-            def weighted_sum():
-                tag = f"ex{P + P // 2}" if v0 == 0 else f"weighted_total{v0}"
-                sums.append(keep.tile([P, pixels], F32, name=f"weighted_total{v0}", tag=tag, align_bytes=64))
-                nc.vector.tensor_reduce(out=sums[0][:], in_=weighted[:], axis=AXIS_X, op=ALU.add)
+        def exponentials(g, sc):
+            nc.vector.tensor_tensor(out=shifted[:, g], in0=sc[:], in1=top[:, g].unsqueeze(2).to_broadcast(sc.shape), op=ALU.subtract)
+            nc.scalar.activation(out=ex[:, g], in_=shifted[:, g], func=ACT.Exp)
 
-            depths = depth_sb[:, v0:v1].rearrange("p (g d) -> p g d", d=D)
-            return [
-                lambda: nc.vector.tensor_reduce(out=top[:], in_=sc[:], axis=AXIS_X, op=ALU.max),
-                lambda: nc.vector.tensor_tensor(
-                    out=shifted[:], in0=sc[:], in1=top[:].unsqueeze(2).to_broadcast([P, pixels, D]), op=ALU.subtract
-                ),
-                lambda: nc.scalar.activation(out=ex[:], in_=shifted[:], func=ACT.Exp),
-                lambda: nc.vector.tensor_reduce(out=total[:], in_=ex[:], axis=AXIS_X, op=ALU.add),
-                lambda: (nc.gpsimd if v0 == 0 else nc.vector).tensor_tensor(out=weighted[:], in0=ex[:], in1=depths, op=ALU.mult),
-                lambda: nc.vector.reciprocal(out=inverse[:], in_=total[:]),
-                weighted_sum,
-                lambda: nc.vector.tensor_tensor(out=result[:, v0 // D : v1 // D], in0=sums[0][:], in1=inverse[:], op=ALU.mult),
-            ]
+        def sums(g, engine):
+            nc.vector.tensor_reduce(out=total[:, g], in_=ex[:, g], axis=AXIS_X, op=ALU.add)
+            engine.tensor_tensor(out=weighted[:, g], in0=ex[:, g], in1=depths[:, g], op=ALU.mult)
 
-        scale_z(sums0[:], 0, P)
-        first_set = (0, P, costs(0, P, 6))
         middle = P + P // 2
+        early, late = slice(0, P // D), (slice(P // D, middle // D), slice(middle // D, pixels))
+        scale_z(sums0[:], 0, P)
+        early_costs = costs(0, P, 6)
         scale_z(sums1[:, :, 0 : P // 2], P, middle)
         scale_z(sums1[:, :, P // 2 : P], middle, V)
-        early = soft_depth(*first_set)
-        late = [soft_depth(P, middle, costs(P, middle, 7))]
-        early[0]()
-        late.append(soft_depth(middle, V, costs(middle, V, 0)))
-        early[1]()
-        early[2]()
-        for stage in range(3):
-            for piece in late:
-                piece[stage]()
-        for issue in early[3:6]:
-            issue()
-        for stage in range(3, len(early)):
-            for piece in late:
-                piece[stage]()
-            if stage in (4, 5):
-                early[stage + 2]()
+        late_costs = [costs(P, middle, 7)]
+        largest(early, early_costs)
+        late_costs.append(costs(middle, V, 0))
+        exponentials(early, early_costs)
+        for stage in (largest, exponentials):
+            for g, sc in zip(late, late_costs):
+                stage(g, sc)
+        sums(early, nc.gpsimd)
+        nc.vector.reciprocal(out=inverse[:, early], in_=total[:, early])
+        for g in late:
+            sums(g, nc.vector)
+        ahead = slice(0, middle // D)
+        for g, piece in ((ahead, late[0]), (late[1], late[1])):
+            nc.vector.tensor_reduce(out=weighted_total[:, g], in_=weighted[:, g], axis=AXIS_X, op=ALU.add)
+            nc.vector.reciprocal(out=inverse[:, piece], in_=total[:, piece])
+        for g in (ahead, late[1]):
+            nc.vector.tensor_tensor(out=result[:, g], in0=weighted_total[:, g], in1=inverse[:, g], op=ALU.mult)
         nc.sync.dma_start(out=out, in_=result[:])

@@ -32,7 +32,9 @@ TERMS = 3
 FIRST_ROW = 32
 ROW_STEP = 4
 ROWS_AHEAD = 3
-BANKS = 8
+PAIR_BANKS = (0, 2)
+VIEW_BANKS = (1, 3, 4, 5, 6, 1)
+LAST_VIEW_BANKS = (7, 3)
 WEIGHTS = (6.0, 2.0, 1.0)
 CROSS_WEIGHTS = (4.0, 1.5, 1.5)
 CROSS_SCALE = math.sqrt(1.5)
@@ -162,9 +164,13 @@ def tile_picked_ymvs_mean_p_kernel(tc, x_words, x_scales, w1, unit, w2, depth, o
         def products(i):
             h, (c0, c1) = steps[i][:2]
             width = c1 - c0
-            first = bank(f"first{i}", [P, 2, width], 2 * i % BANKS)
-            second = bank(f"second{i}", [P, 2, width], (2 * i + 1) % BANKS)
-            y3 = bank("third0", [P, width], BANKS - 1)[:] if i == 0 else first[:, 1, :]
+            first = bank(f"first{i}", [P, 1, width], PAIR_BANKS[i % 2])
+            if width == P:
+                views_bank = bank(f"views{i}", [P, TERMS, width], VIEW_BANKS[i])
+                second, y3 = views_bank[:, 0:2, :], views_bank[:, 2, :]
+            else:
+                second = bank(f"second{i}", [P, 2, width], VIEW_BANKS[i])
+                y3 = bank(f"third{i}", [P, width], LAST_VIEW_BANKS[i % 2])[:]
             pair_sum = keep.tile([P, width], F32, name=f"pair_sum{i}", align_bytes=64)
             for acc, views in ((first[:, 0, :], (0, 1)), (second[:, 0, :], (1,)), (second[:, 1, :], (2,)), (y3, (3,))):
                 product(acc, h, views, c0, c1)
@@ -297,12 +303,12 @@ def tile_picked_ymvs_mean_p_kernel(tc, x_words, x_scales, w1, unit, w2, depth, o
         middle = P + P // 2
         early, late = slice(0, P // D), (slice(P // D, middle // D), slice(middle // D, pixels))
         scale_z(sums0[:], 0, P)
-        early_costs = costs(0, P, 6)
+        early_costs = costs(0, P, 0)
         scale_z(sums1[:, :, 0 : P // 2], P, middle)
         scale_z(sums1[:, :, P // 2 : P], middle, V)
-        late_costs = [costs(P, middle, 7)]
+        late_costs = [costs(P, middle, 2)]
         largest(early, early_costs)
-        late_costs.append(costs(middle, V, 0))
+        late_costs.append(costs(middle, V, 6))
         exponentials(early, early_costs)
         for stage in (largest, exponentials):
             for g, sc in zip(late, late_costs):

@@ -38,7 +38,7 @@ LAST_VIEW_BANKS = (7, 3)
 WEIGHTS = (6.0, 2.0, 1.0)
 CROSS_WEIGHTS = (4.0, 1.5, 1.5)
 CROSS_SCALE = math.sqrt(1.5)
-FOUR_TERMS = (4,)
+FOUR_TERMS = (4, 5)
 
 
 def tile_picked_ymvs_mean_p_kernel(tc, x_words, x_scales, w1, unit, w2, depth, offs, out):
@@ -88,6 +88,9 @@ def tile_picked_ymvs_mean_p_kernel(tc, x_words, x_scales, w1, unit, w2, depth, o
                 in_=picked_scales[:, h * ENTRIES : (h + 1) * ENTRIES].rearrange("p (v d) -> p d v", d=D),
             )
             for q in range(QUADRANTS):
+                if (h, q) == (1, 2):
+                    w2_raw = keep.tile([P, PACK, N], F32, name="w2_raw", tag="picked_scales", align_bytes=64)
+                    nc.sync.dma_start(out=w2_raw[:], in_=w2.rearrange("(p j) c -> p j c", j=PACK))
                 nc.sync.dma_start(
                     out=x_plane[:].bitcast(I32)[32 * q : 32 * q + 4, h * ENTRIES // 4 : (h + 1) * ENTRIES // 4],
                     in_=scales_by_view[:].bitcast(I32)[FIRST_ROW + ROW_STEP * 4 * q : FIRST_ROW + ROW_STEP * 4 * (q + 1) : ROW_STEP, :],
@@ -142,8 +145,6 @@ def tile_picked_ymvs_mean_p_kernel(tc, x_words, x_scales, w1, unit, w2, depth, o
                     start=(d == views[0]), stop=(d == views[-1]),
                 )
 
-        w2_raw = keep.tile([P, PACK, N], F32, name="w2_raw", tag="picked_scales", align_bytes=64)
-        nc.sync.dma_start(out=w2_raw[:], in_=w2.rearrange("(p j) c -> p j c", j=PACK))
         depth_sb = keep.tile([P, V], F32, name="depth_sb", tag="dealt1", align_bytes=64)
         nc.sync.dma_start(out=depth_sb[:], in_=depth)
         terms0 = [sb(f"terms0_{u}", [P, TERMS + (u in FOUR_TERMS), 2, P], F32) for u in range(2)]
@@ -186,52 +187,40 @@ def tile_picked_ymvs_mean_p_kernel(tc, x_words, x_scales, w1, unit, w2, depth, o
             triple_sum = sb(f"triple_sum{i}", [P, width], F32)
             contrasts = sb(f"contrasts{i}", [P, TERMS, width], F32)
             nc.vector.tensor_tensor(out=triple_sum[:], in0=second[:, 1, :], in1=pair_sum[:], op=ALU.add)
-            if i < len(steps) - 1:
-                nc.vector.scalar_tensor_tensor(
-                    out=contrasts[:, 0:2, :], in0=second[:], scalar=-2.0, in1=pair_sum[:].unsqueeze(1).to_broadcast([P, 2, width]),
-                    op0=ALU.mult, op1=ALU.add,
-                )
-                nc.vector.scalar_tensor_tensor(out=contrasts[:, 2, :], in0=y3, scalar=-3.0, in1=triple_sum[:], op0=ALU.mult, op1=ALU.add)
-                for k in (0, 2, 1):
-                    src = view(contrasts[:, k, :])
-                    if k == 2:
-                        nc.gpsimd.tensor_tensor(out=dst[k], in0=src, in1=src, op=ALU.mult)
-                    else:
-                        nc.scalar.activation(out=dst[k], in_=src, func=ACT.Square, scale=math.sqrt(WEIGHTS[k]))
-            else:
-                for t in range(2):
-                    for k, view_d, factor, rest in ((0, second[:, 0, :], -2.0, pair_sum), (2, y3, -3.0, triple_sum), (1, second[:, 1, :], -2.0, pair_sum)):
-                        contrast = view(contrasts[:, k, :])[:, :, t, :]
-                        nc.vector.scalar_tensor_tensor(
-                            out=contrast, in0=view(view_d)[:, :, t, :], scalar=factor, in1=view(rest[:])[:, :, t, :], op0=ALU.mult, op1=ALU.add
-                        )
-                        if (t, k) == (0, 2):
-                            nc.gpsimd.tensor_tensor(out=dst[k][:, :, t, :], in0=contrast, in1=contrast, op=ALU.mult)
-                        else:
-                            nc.scalar.activation(out=dst[k][:, :, t, :], in_=contrast, func=ACT.Square, scale=math.sqrt(WEIGHTS[k]))
+            nc.vector.scalar_tensor_tensor(
+                out=contrasts[:, 0:2, :], in0=second[:], scalar=-2.0, in1=pair_sum[:].unsqueeze(1).to_broadcast([P, 2, width]),
+                op0=ALU.mult, op1=ALU.add,
+            )
+            nc.vector.scalar_tensor_tensor(out=contrasts[:, 2, :], in0=y3, scalar=-3.0, in1=triple_sum[:], op0=ALU.mult, op1=ALU.add)
+            for k in (0, 2, 1):
+                src = view(contrasts[:, k, :])
+                if k == 2:
+                    nc.gpsimd.tensor_tensor(out=dst[k], in0=src, in1=src, op=ALU.mult)
+                else:
+                    nc.scalar.activation(out=dst[k], in_=src, func=ACT.Square, scale=math.sqrt(WEIGHTS[k]))
 
         def four_terms(i, width, y3, second, pair_sum):
             dst, view = steps[i][2:]
             contrasts = sb(f"contrasts{i}", [P, TERMS, width], F32)
-            nc.vector.scalar_tensor_tensor(
-                out=contrasts[:, 0:2, :], in0=second[:], scalar=-2.0 * CROSS_SCALE, in1=pair_sum[:].unsqueeze(1).to_broadcast([P, 2, width]),
-                op0=ALU.mult, op1=ALU.add,
-            )
-            nc.vector.scalar_tensor_tensor(out=contrasts[:, 2, :], in0=y3, scalar=2.0 * CROSS_SCALE, in1=pair_sum[:], op0=ALU.mult, op1=ALU.subtract)
-            nc.scalar.activation(out=dst[0], in_=view(contrasts[:, 0, :]), func=ACT.Square, scale=math.sqrt(CROSS_WEIGHTS[0]))
-            if width == P:
-                g, u = divmod(i, 2)
-                nc.scalar.activation(
-                    out=terms0[u][:, 1:TERMS, :, g * GROUPS : (g + 1) * GROUPS], in_=contrasts[:, 1:TERMS, :].rearrange("p k (t m) -> p k t m", t=2),
-                    func=ACT.Square, scale=math.sqrt(CROSS_WEIGHTS[1]),
-                )
-            else:
-                for k in range(1, TERMS):
-                    nc.scalar.activation(out=dst[k], in_=view(contrasts[:, k, :]), func=ACT.Square, scale=math.sqrt(CROSS_WEIGHTS[k]))
+            for k, view_d, factor, op in ((1, second[:, 1, :], -2.0, ALU.add), (2, y3, 2.0, ALU.subtract), (0, second[:, 0, :], -2.0, ALU.add)):
+                nc.vector.scalar_tensor_tensor(out=contrasts[:, k, :], in0=view_d, scalar=factor * CROSS_SCALE, in1=pair_sum[:], op0=ALU.mult, op1=op)
+                nc.scalar.activation(out=dst[k], in_=view(contrasts[:, k, :]), func=ACT.Square, scale=math.sqrt(CROSS_WEIGHTS[k]))
             nc.gpsimd.tensor_tensor(out=dst[TERMS], in0=view(contrasts[:, 1, :]), in1=view(contrasts[:, 2, :]), op=ALU.mult)
 
+        def last_terms(i, width, y3, second, pair_sum):
+            dst, view = steps[i][2:]
+            contrasts = sb(f"contrasts{i}", [P, TERMS, width], F32)
+            for t in range(2):
+                parts = [view(contrasts[:, k, :])[:, :, t, :] for k in range(TERMS)]
+                for k, view_d, factor, op in ((1, second[:, 1, :], -2.0, ALU.add), (2, y3, 2.0, ALU.subtract), (0, second[:, 0, :], -2.0, ALU.add)):
+                    nc.vector.scalar_tensor_tensor(
+                        out=parts[k], in0=view(view_d)[:, :, t, :], scalar=factor * CROSS_SCALE, in1=view(pair_sum[:])[:, :, t, :], op0=ALU.mult, op1=op
+                    )
+                    nc.scalar.activation(out=dst[k][:, :, t, :], in_=parts[k], func=ACT.Square, scale=math.sqrt(CROSS_WEIGHTS[k]))
+                nc.gpsimd.tensor_tensor(out=dst[TERMS][:, :, t, :], in0=parts[1], in1=parts[2], op=ALU.mult)
+
         def terms_of(i):
-            (four_terms if i in FOUR_TERMS else three_terms)(i, *made[i])
+            (last_terms if i == last else four_terms if i in FOUR_TERMS else three_terms)(i, *made[i])
 
         def add_terms(acc, terms, count, order, opens=True, closes=True):
             for k in order:
@@ -258,14 +247,14 @@ def tile_picked_ymvs_mean_p_kernel(tc, x_words, x_scales, w1, unit, w2, depth, o
         for u in range(2):
             terms_of(last - 1 + u)
             if u == 0:
-                add_terms(sums1[:, 0:2, :], terms1[0], 2, range(terms1[0].shape[1]), True, False)
+                add_terms(sums1[:, 0:2, :], terms1[0], 2, (1, 2, 0, 3), True, False)
             else:
                 for t in range(2):
-                    add_terms(sums1[:, 2 + t : 3 + t, :], terms1[1][:, :, t : t + 1, :], 1, ((0, 1, 2), (0, 2, 1))[t], False, t == 1)
+                    add_terms(sums1[:, 2 + t : 3 + t, :], terms1[1][:, :, t : t + 1, :], 1, (1, 2, 0, 3), False, t == 1)
         w2_codes = keep.tile([P, N], U32, name="w2_codes", tag="pair_sum3", align_bytes=64)
         nc.vector.quantize_mx(out=w2_codes[:].bitcast(FP8X4), scales=w2_plane[:], in_=w2_bf[:].rearrange("p c j -> p (c j)"))
 
-        z_bf = [keep.tile([P, P, PACK], BF16, name="z_bf0", tag=f"triple_sum{last}", align_bytes=64), sb("z_bf1", [P, P, PACK], BF16)]
+        z_bf = [keep.tile([P, P, PACK], BF16, name="z_bf0", tag=f"pair_sum{last}", align_bytes=64), sb("z_bf1", [P, P, PACK], BF16)]
 
         def scale_z(acc, v0, v1):
             nc.vector.tensor_tensor(

@@ -134,7 +134,7 @@ def tile_picked_ymvs_mean_p_kernel(tc, x_words, x_scales, w1, unit, w2, depth, o
         for t in (0, 2):
             quantize_w1(1, t, t + 2)
 
-        w2_bf = keep.tile([P, N, PACK], BF16, name="w2_bf", tag="w2_bf", align_bytes=64)
+        w2_bf = keep.tile([P, N, PACK], BF16, name="w2_bf", tag="dealt1", align_bytes=64)
         w2_plane = sb("w2_plane", [P, N], U8)
 
         def product(acc, h, views, c0, c1):
@@ -145,7 +145,7 @@ def tile_picked_ymvs_mean_p_kernel(tc, x_words, x_scales, w1, unit, w2, depth, o
                     start=(d == views[0]), stop=(d == views[-1]),
                 )
 
-        depth_sb = keep.tile([P, V], F32, name="depth_sb", tag="dealt1", align_bytes=64)
+        depth_sb = keep.tile([P, V], F32, name="depth_sb", tag="w1_raw1", align_bytes=64)
         nc.sync.dma_start(out=depth_sb[:], in_=depth)
         terms0 = [sb(f"terms0_{u}", [P, TERMS + (u in FOUR_TERMS), 2, P], F32) for u in range(2)]
         terms1 = [sb(f"terms1_{u}", [P, TERMS + (4 + u in FOUR_TERMS), 2, P], F32) for u in range(2)]
@@ -210,14 +210,26 @@ def tile_picked_ymvs_mean_p_kernel(tc, x_words, x_scales, w1, unit, w2, depth, o
         def last_terms(i, width, y3, second, pair_sum):
             dst, view = steps[i][2:]
             contrasts = sb(f"contrasts{i}", [P, TERMS, width], F32)
-            for t in range(2):
-                parts = [view(contrasts[:, k, :])[:, :, t, :] for k in range(TERMS)]
-                for k, view_d, factor, op in ((1, second[:, 1, :], -2.0, ALU.add), (2, y3, 2.0, ALU.subtract), (0, second[:, 0, :], -2.0, ALU.add)):
-                    nc.vector.scalar_tensor_tensor(
-                        out=parts[k], in0=view(view_d)[:, :, t, :], scalar=factor * CROSS_SCALE, in1=view(pair_sum[:])[:, :, t, :], op0=ALU.mult, op1=op
-                    )
-                    nc.scalar.activation(out=dst[k][:, :, t, :], in_=parts[k], func=ACT.Square, scale=math.sqrt(CROSS_WEIGHTS[k]))
-                nc.gpsimd.tensor_tensor(out=dst[TERMS][:, :, t, :], in0=parts[1], in1=parts[2], op=ALU.mult)
+            parts = [[view(contrasts[:, k, :])[:, :, t, :] for k in range(TERMS)] for t in range(2)]
+
+            def contrast(t, k, view_d, factor, rest, op, weight):
+                nc.vector.scalar_tensor_tensor(
+                    out=parts[t][k], in0=view(view_d)[:, :, t, :], scalar=factor * CROSS_SCALE, in1=rest, op0=ALU.mult, op1=op
+                )
+                nc.scalar.activation(out=dst[k][:, :, t, :], in_=parts[t][k], func=ACT.Square, scale=math.sqrt(weight))
+
+            pair = [view(pair_sum[:])[:, :, t, :] for t in range(2)]
+            contrast(0, 1, second[:, 1, :], -2.0, pair[0], ALU.add, CROSS_WEIGHTS[1])
+            contrast(0, 2, y3, 2.0, pair[0], ALU.subtract, CROSS_WEIGHTS[2])
+            nc.gpsimd.tensor_tensor(out=dst[TERMS][:, :, 0, :], in0=parts[0][1], in1=parts[0][2], op=ALU.mult)
+            triple_sum = sb(f"triple_sum{i}", [P, 2, GROUPS], F32)
+            nc.vector.scalar_tensor_tensor(
+                out=triple_sum[:], in0=view(second[:, 1, :])[:, :, 1, :], scalar=CROSS_SCALE, in1=pair[1], op0=ALU.mult, op1=ALU.add
+            )
+            contrast(0, 0, second[:, 0, :], -2.0, pair[0], ALU.add, CROSS_WEIGHTS[0])
+            contrast(1, 0, second[:, 0, :], -2.0, pair[1], ALU.add, WEIGHTS[0] / 1.5)
+            contrast(1, 2, y3, -3.0, triple_sum[:], ALU.add, WEIGHTS[2] / 1.5)
+            contrast(1, 1, second[:, 1, :], -2.0, pair[1], ALU.add, WEIGHTS[1] / 1.5)
 
         def terms_of(i):
             (last_terms if i == last else four_terms if i in FOUR_TERMS else three_terms)(i, *made[i])
@@ -250,7 +262,7 @@ def tile_picked_ymvs_mean_p_kernel(tc, x_words, x_scales, w1, unit, w2, depth, o
                 add_terms(sums1[:, 0:2, :], terms1[0], 2, (1, 2, 0, 3), True, False)
             else:
                 for t in range(2):
-                    add_terms(sums1[:, 2 + t : 3 + t, :], terms1[1][:, :, t : t + 1, :], 1, (1, 2, 0, 3), False, t == 1)
+                    add_terms(sums1[:, 2 + t : 3 + t, :], terms1[1][:, :, t : t + 1, :], 1, ((1, 2, 0, 3), (0, 2, 1))[t], False, t == 1)
         w2_codes = keep.tile([P, N], U32, name="w2_codes", tag="pair_sum3", align_bytes=64)
         nc.vector.quantize_mx(out=w2_codes[:].bitcast(FP8X4), scales=w2_plane[:], in_=w2_bf[:].rearrange("p c j -> p (c j)"))
 

@@ -27,7 +27,6 @@ ENTRIES = S // HALVES
 WIDE = H // 2
 GROUPS = WIDE // PACK
 SCALAR_SHARE = 40
-FIRST_SHARE = 40
 TERMS = 3
 FIRST_ROW = 32
 ROW_STEP = 4
@@ -123,14 +122,13 @@ def tile_picked_ymvs_mean_p_kernel(tc, x_words, x_scales, w1, unit, w2, depth, o
             )
             return codes
 
-        deal_w1(nc.scalar.copy, 0, 0, FIRST_SHARE)
-        deal_w1(gpsimd_cast, 0, FIRST_SHARE, GROUPS)
+        deal_w1(nc.scalar.copy, 0, 0, GROUPS)
         for t in (0, 2):
             quantize_w1(0, t, t + 2)
         x_codes = [gather_words(h) for h in range(HALVES)]
-        for j0 in (0, 2):
-            deal_w1(nc.scalar.copy, 1, 0, SCALAR_SHARE, j0, j0 + 2)
-            deal_w1(gpsimd_cast, 1, SCALAR_SHARE, GROUPS, j0, j0 + 2)
+        deal_w1(nc.scalar.copy, 1, 0, SCALAR_SHARE, 0, 2)
+        deal_w1(gpsimd_cast, 1, SCALAR_SHARE, GROUPS, 0, 2)
+        deal_w1(nc.scalar.copy, 1, 0, GROUPS, 2, PACK)
         for t in (0, 2):
             quantize_w1(1, t, t + 2)
 

@@ -61,6 +61,9 @@ def tile_picked_ymvs_mean_p_kernel(tc, x_words, x_scales, w1, unit, w2, depth, o
         nc.vector.memset(scale_table[:].bitcast(I32), 0)
         x_plane = sb("x_plane", [P, S], U8)
         nc.vector.memset(x_plane[:].bitcast(I32), 0)
+        ident = sb("ident", [P, P], F32)
+        nc.vector.memset(ident[:], 0.0)
+        make_identity(nc, ident[:], nomemset=True)
 
         w1_rows = w1.rearrange("(p j) c -> p j c", j=PACK)
         w1_raw = [sb(f"w1_raw{g}", [P, PACK, WIDE], F32) for g in range(2)]
@@ -75,8 +78,6 @@ def tile_picked_ymvs_mean_p_kernel(tc, x_words, x_scales, w1, unit, w2, depth, o
         unit_sb = sb("unit_sb", [P, PACK], F32)
         nc.scalar.activation(out=unit_sb[:], in_=unit_raw[:], func=ACT.Copy, scale=1.0 / 48)
 
-        ident = keep.tile([P, P], F32, name="ident", tag="unit_raw", align_bytes=64)
-        make_identity(nc, ident[:])
 
         picked_scales = sb("picked_scales", [P, S], U8)
         nc.vector.tensor_copy(picked_scales[:], scale_table[:].indirect(offsets[:]))

@@ -36,7 +36,8 @@ VIEW_BANKS = (1, 3, 4, 5, 6, 1)
 LAST_VIEW_BANKS = (7, 3)
 WEIGHTS = (6.0, 2.0, 1.0)
 CROSS_WEIGHTS = (4.0, 1.5, 1.5)
-CROSS_SCALE = math.sqrt(1.5)
+CROSS_SCALE = math.sqrt(0.5)
+ROOT_TWO = math.sqrt(2.0)
 FOUR_TERMS = (4, 5)
 
 
@@ -76,7 +77,7 @@ def tile_picked_ymvs_mean_p_kernel(tc, x_words, x_scales, w1, unit, w2, depth, o
         for j0 in (0, 2):
             nc.scalar.dma_start(out=w1_raw[1][:, j0 : j0 + 2], in_=w1_rows[:, j0 : j0 + 2, WIDE:H])
         unit_sb = sb("unit_sb", [P, PACK], F32)
-        nc.scalar.activation(out=unit_sb[:], in_=unit_raw[:], func=ACT.Copy, scale=1.0 / 48)
+        nc.scalar.activation(out=unit_sb[:], in_=unit_raw[:], func=ACT.Copy, scale=1.0 / 16)
 
 
         picked_scales = sb("picked_scales", [P, S], U8)
@@ -175,28 +176,25 @@ def tile_picked_ymvs_mean_p_kernel(tc, x_words, x_scales, w1, unit, w2, depth, o
             for acc, views in ((first[:, 0, :], (0, 1)), (second[:, 0, :], (1,)), (second[:, 1, :], (2,)), (y3, (3,))):
                 product(acc, h, views, c0, c1)
                 if views == (0, 1):
-                    if i in FOUR_TERMS:
-                        nc.scalar.activation(out=pair_sum[:], in_=first[:, 0, :], func=ACT.Copy, scale=CROSS_SCALE)
-                    else:
-                        nc.scalar.copy(out=pair_sum[:], in_=first[:, 0, :])
+                    nc.scalar.activation(out=pair_sum[:], in_=first[:, 0, :], func=ACT.Copy, scale=CROSS_SCALE if i in FOUR_TERMS else ROOT_TWO)
             return width, y3, second, pair_sum
 
         def three_terms(i, width, y3, second, pair_sum):
             dst, view = steps[i][2:]
+            g, u = divmod(i, 2)
             triple_sum = sb(f"triple_sum{i}", [P, width], F32)
             contrasts = sb(f"contrasts{i}", [P, TERMS, width], F32)
-            nc.vector.tensor_tensor(out=triple_sum[:], in0=second[:, 1, :], in1=pair_sum[:], op=ALU.add)
+            nc.vector.scalar_tensor_tensor(out=triple_sum[:], in0=pair_sum[:], scalar=1.0 / ROOT_TWO, in1=second[:, 1, :], op0=ALU.mult, op1=ALU.add)
             nc.vector.scalar_tensor_tensor(
-                out=contrasts[:, 0:2, :], in0=second[:], scalar=-2.0, in1=pair_sum[:].unsqueeze(1).to_broadcast([P, 2, width]),
+                out=contrasts[:, 0:2, :], in0=second[:], scalar=-2.0 * ROOT_TWO, in1=pair_sum[:].unsqueeze(1).to_broadcast([P, 2, width]),
                 op0=ALU.mult, op1=ALU.add,
             )
             nc.vector.scalar_tensor_tensor(out=contrasts[:, 2, :], in0=y3, scalar=-3.0, in1=triple_sum[:], op0=ALU.mult, op1=ALU.add)
-            for k in (0, 2, 1):
-                src = view(contrasts[:, k, :])
-                if k == 2:
-                    nc.gpsimd.tensor_tensor(out=dst[k], in0=src, in1=src, op=ALU.mult)
-                else:
-                    nc.scalar.activation(out=dst[k], in_=src, func=ACT.Square, scale=math.sqrt(WEIGHTS[k]))
+            nc.gpsimd.tensor_tensor(out=dst[0], in0=view(contrasts[:, 0, :]), in1=view(contrasts[:, 0, :]), op=ALU.mult)
+            nc.scalar.activation(
+                out=terms0[u][:, 1:TERMS, :, g * GROUPS : (g + 1) * GROUPS], in_=contrasts[:, 1:TERMS, :].rearrange("p k (t m) -> p k t m", t=2),
+                func=ACT.Square, scale=math.sqrt(1.0 / 3),
+            )
 
         def four_terms(i, width, y3, second, pair_sum):
             dst, view = steps[i][2:]

import math
from contextlib import ExitStack

import concourse.mybir as mybir
from concourse.masks import make_identity

K, T, S, D, H, N, V = 512, 4096, 1024, 4, 512, 128, 256
FLOPS = 2 * K * H * S + 2 * H * N * V

F32 = mybir.dt.float32
BF16 = mybir.dt.bfloat16
I32 = mybir.dt.int32
U32 = mybir.dt.uint32
U16 = mybir.dt.uint16
U8 = mybir.dt.uint8
FP8X4 = mybir.dt.float8_e4m3fn_x4
ALU = mybir.AluOpType
ACT = mybir.ActivationFunctionType
AXIS_X = mybir.AxisListType.X

P = 128
PACK = 4
BLOCKS = K // 32
QUADRANTS = 4
HALVES = V // P
ENTRIES = S // HALVES
WIDE = H // 2
GROUPS = WIDE // PACK
SCALAR_SHARE = 40
TERMS = 3
FIRST_ROW = 32
ROW_STEP = 4
ROWS_AHEAD = 3
PAIR_BANKS = (0, 2)
VIEW_BANKS = (1, 3, 4, 5, 6, 1)
LAST_VIEW_BANKS = (7, 3)
WEIGHTS = (6.0, 2.0, 1.0)
CROSS_WEIGHTS = (4.0, 1.5, 1.5)
CROSS_SCALE = math.sqrt(0.5)
ROOT_TWO = math.sqrt(2.0)
FOUR_TERMS = (4, 5)


def tile_picked_ymvs_mean_p_kernel(tc, x_words, x_scales, w1, unit, w2, depth, offs, out):
    nc = tc.nc
    with ExitStack() as ctx:
        keep = ctx.enter_context(tc.tile_pool(name="keep", bufs=1))
        psum = ctx.enter_context(tc.psum_pool(name="psum", bufs=1))

        def sb(name, shape, dtype):
            return keep.tile(shape, dtype, name=name, align_bytes=64)

        def bank(name, shape, number):
            return psum.tile(shape, F32, name=name, tag=f"bank{number}")

        offsets = keep.tile([P, S // 16], U16, name="offsets")
        nc.sync.dma_start(offsets[:], offs)
        unit_raw = sb("unit_raw", [P, PACK], F32)
        nc.sync.dma_start(out=unit_raw[:], in_=unit.rearrange("(p t) o -> p (t o)", t=PACK))

        scale_table = sb("scale_table", [P, T], U8)
        nc.vector.memset(scale_table[:].bitcast(I32), 0)
        x_plane = sb("x_plane", [P, S], U8)
        nc.vector.memset(x_plane[:].bitcast(I32), 0)
        ident = sb("ident", [P, P], F32)
        nc.vector.memset(ident[:], 0.0)
        make_identity(nc, ident[:], nomemset=True)

        w1_rows = w1.rearrange("(p j) c -> p j c", j=PACK)
        w1_raw = [sb(f"w1_raw{g}", [P, PACK, WIDE], F32) for g in range(2)]
        word_table = sb("word_table", [P, T], I32)
        for j0, j1 in ((0, 1), (1, ROWS_AHEAD)):
            nc.scalar.dma_start(out=w1_raw[0][:, j0:j1], in_=w1_rows[:, j0:j1, 0:WIDE])
        nc.scalar.dma_start(out=scale_table[:].bitcast(I32)[FIRST_ROW : FIRST_ROW + ROW_STEP * BLOCKS : ROW_STEP, :], in_=x_scales[0].bitcast(I32))
        nc.scalar.dma_start(out=w1_raw[0][:, ROWS_AHEAD:PACK], in_=w1_rows[:, ROWS_AHEAD:PACK, 0:WIDE])
        nc.scalar.dma_start(out=word_table[:], in_=x_words[0].rearrange("p n t -> p (n t)").bitcast(I32))
        for j0 in (0, 2):
            nc.scalar.dma_start(out=w1_raw[1][:, j0 : j0 + 2], in_=w1_rows[:, j0 : j0 + 2, WIDE:H])
        unit_sb = sb("unit_sb", [P, PACK], F32)
        nc.scalar.activation(out=unit_sb[:], in_=unit_raw[:], func=ACT.Copy, scale=1.0 / 16)


        picked_scales = sb("picked_scales", [P, S], U8)
        nc.vector.tensor_copy(picked_scales[:], scale_table[:].indirect(offsets[:]))
        for h in range(HALVES):
            scales_by_view = sb(f"scales_by_view{h}", [P, ENTRIES], U8)
            nc.vector.tensor_copy(
                out=scales_by_view[:].rearrange("p (d v) -> p d v", d=D),
                in_=picked_scales[:, h * ENTRIES : (h + 1) * ENTRIES].rearrange("p (v d) -> p d v", d=D),
            )
            for q in range(QUADRANTS):
                if (h, q) == (1, 2):
                    w2_raw = keep.tile([P, PACK, N], F32, name="w2_raw", tag="picked_scales", align_bytes=64)
                    nc.sync.dma_start(out=w2_raw[:], in_=w2.rearrange("(p j) c -> p j c", j=PACK))
                nc.sync.dma_start(
                    out=x_plane[:].bitcast(I32)[32 * q : 32 * q + 4, h * ENTRIES // 4 : (h + 1) * ENTRIES // 4],
                    in_=scales_by_view[:].bitcast(I32)[FIRST_ROW + ROW_STEP * 4 * q : FIRST_ROW + ROW_STEP * 4 * (q + 1) : ROW_STEP, :],
                )

        w1_codes = sb("w1_codes", [P, H], U32)
        w1_plane = sb("w1_plane", [P, H], U8)
        w1_bf = [keep.tile([P, PACK, GROUPS, PACK], BF16, name=f"w1_bf{g}", tag=f"dealt{g}", align_bytes=64) for g in range(2)]

        def deal_w1(copy, g, m0, m1, j0=0, j1=PACK):
            copy(
                out=w1_bf[g][:, :, m0:m1, j0:j1].rearrange("p t m j -> p m t j"),
                in_=w1_raw[g][:, j0:j1].rearrange("p j (m t) -> p m t j", t=PACK)[:, m0:m1],
            )

        def gpsimd_cast(out, in_):
            nc.gpsimd.tensor_scalar(out=out, in0=in_, scalar1=1.0, scalar2=0.0, op0=ALU.mult, op1=ALU.add)

        def quantize_w1(g, t0, t1):
            cols = slice(t0 * P + g * P, t0 * P + (g + 1) * P)
            nc.vector.quantize_mx(
                out=w1_codes[:, cols].bitcast(FP8X4), scales=w1_plane[:, cols], in_=w1_bf[g][:, t0:t1].rearrange("p t m j -> p (t m j)")
            )

        def gather_words(h):
            codes = keep.tile([P, D, P], U32, name=f"x_codes{h}", tag=("w1_raw0", "dealt0")[h], align_bytes=64)
            nc.vector.tensor_copy(
                codes[:].rearrange("p d v -> p v d"),
                word_table[:].bitcast(U32).indirect(offsets[:, h * ENTRIES // 16 : (h + 1) * ENTRIES // 16]),
            )
            return codes

        deal_w1(nc.scalar.copy, 0, 0, GROUPS)
        for t in (0, 2):
            quantize_w1(0, t, t + 2)
        x_codes = [gather_words(h) for h in range(HALVES)]
        deal_w1(nc.scalar.copy, 1, 0, SCALAR_SHARE, 0, 2)
        deal_w1(gpsimd_cast, 1, SCALAR_SHARE, GROUPS, 0, 2)
        deal_w1(nc.scalar.copy, 1, 0, GROUPS, 2, PACK)
        for t in (0, 2):
            quantize_w1(1, t, t + 2)

        w2_bf = keep.tile([P, N, PACK], BF16, name="w2_bf", tag="dealt1", align_bytes=64)
        w2_plane = sb("w2_plane", [P, N], U8)

        def product(acc, h, views, c0, c1):
            for d in views:
                nc.tensor.matmul_mx(
                    out=acc, lhsT=x_codes[h][:, d, :].bitcast(FP8X4), lhsT_scale=x_plane[:, h * ENTRIES + d * P : h * ENTRIES + (d + 1) * P],
                    rhs=w1_codes[:, c0:c1].bitcast(FP8X4), rhs_scale=w1_plane[:, c0:c1],
                    start=(d == views[0]), stop=(d == views[-1]),
                )

        depth_sb = keep.tile([P, V], F32, name="depth_sb", tag="w1_raw1", align_bytes=64)
        nc.sync.dma_start(out=depth_sb[:], in_=depth)
        terms0 = [sb(f"terms0_{u}", [P, TERMS + (u in FOUR_TERMS), 2, P], F32) for u in range(2)]
        terms1 = [sb(f"terms1_{u}", [P, TERMS + (4 + u in FOUR_TERMS), 2, P], F32) for u in range(2)]

        def first_set_step(g, t0, t1):
            pieces = (t0 * P + g * P, t0 * P + (g + 1) * P)
            dst = [terms0[t0 // 2][:, k, :, g * GROUPS : (g + 1) * GROUPS] for k in range(terms0[t0 // 2].shape[1])]
            return 0, pieces, dst, lambda x: x.rearrange("p (t m) -> p t m", m=GROUPS)

        def second_set_step(u):
            pieces = (u * WIDE, (u + 1) * WIDE)
            dst = [terms1[u][:, k].rearrange("p t (g m) -> p g t m", g=2) for k in range(terms1[u].shape[1])]
            return 1, pieces, dst, lambda x: x.rearrange("p (g t m) -> p g t m", g=2, t=2)

        steps = [first_set_step(g, t, t + 2) for g in range(2) for t in (0, 2)] + [second_set_step(u) for u in range(2)]

        def products(i):
            h, (c0, c1) = steps[i][:2]
            width = c1 - c0
            first = bank(f"first{i}", [P, 1, width], PAIR_BANKS[i % 2])
            if width == P:
                views_bank = bank(f"views{i}", [P, TERMS, width], VIEW_BANKS[i])
                second, y3 = views_bank[:, 0:2, :], views_bank[:, 2, :]
            else:
                second = bank(f"second{i}", [P, 2, width], VIEW_BANKS[i])
                y3 = bank(f"third{i}", [P, width], LAST_VIEW_BANKS[i % 2])[:]
            pair_sum = keep.tile([P, width], F32, name=f"pair_sum{i}", align_bytes=64)
            for acc, views in ((first[:, 0, :], (0, 1)), (second[:, 0, :], (1,)), (second[:, 1, :], (2,)), (y3, (3,))):
                product(acc, h, views, c0, c1)
                if views == (0, 1):
                    nc.scalar.activation(out=pair_sum[:], in_=first[:, 0, :], func=ACT.Copy, scale=CROSS_SCALE if i in FOUR_TERMS else ROOT_TWO)
            return width, y3, second, pair_sum

        def three_terms(i, width, y3, second, pair_sum):
            dst, view = steps[i][2:]
            g, u = divmod(i, 2)
            triple_sum = sb(f"triple_sum{i}", [P, width], F32)
            contrasts = sb(f"contrasts{i}", [P, TERMS, width], F32)
            nc.vector.scalar_tensor_tensor(out=triple_sum[:], in0=pair_sum[:], scalar=1.0 / ROOT_TWO, in1=second[:, 1, :], op0=ALU.mult, op1=ALU.add)
            nc.vector.scalar_tensor_tensor(
                out=contrasts[:, 0:2, :], in0=second[:], scalar=-2.0 * ROOT_TWO, in1=pair_sum[:].unsqueeze(1).to_broadcast([P, 2, width]),
                op0=ALU.mult, op1=ALU.add,
            )
            nc.vector.scalar_tensor_tensor(out=contrasts[:, 2, :], in0=y3, scalar=-3.0, in1=triple_sum[:], op0=ALU.mult, op1=ALU.add)
            nc.gpsimd.tensor_tensor(out=dst[0], in0=view(contrasts[:, 0, :]), in1=view(contrasts[:, 0, :]), op=ALU.mult)
            nc.scalar.activation(
                out=terms0[u][:, 1:TERMS, :, g * GROUPS : (g + 1) * GROUPS], in_=contrasts[:, 1:TERMS, :].rearrange("p k (t m) -> p k t m", t=2),
                func=ACT.Square, scale=math.sqrt(1.0 / 3),
            )

        def four_terms(i, width, y3, second, pair_sum):
            dst, view = steps[i][2:]
            contrasts = sb(f"contrasts{i}", [P, TERMS, width], F32)
            for k, view_d, factor, op in ((1, second[:, 1, :], -2.0, ALU.add), (2, y3, 2.0, ALU.subtract), (0, second[:, 0, :], -2.0, ALU.add)):
                nc.vector.scalar_tensor_tensor(out=contrasts[:, k, :], in0=view_d, scalar=factor * CROSS_SCALE, in1=pair_sum[:], op0=ALU.mult, op1=op)
                nc.scalar.activation(out=dst[k], in_=view(contrasts[:, k, :]), func=ACT.Square, scale=math.sqrt(CROSS_WEIGHTS[k]))
            nc.gpsimd.tensor_tensor(out=dst[TERMS], in0=view(contrasts[:, 1, :]), in1=view(contrasts[:, 2, :]), op=ALU.mult)

        def last_terms(i, width, y3, second, pair_sum):
            dst, view = steps[i][2:]
            contrasts = sb(f"contrasts{i}", [P, TERMS, width], F32)
            parts = [[view(contrasts[:, k, :])[:, :, t, :] for k in range(TERMS)] for t in range(2)]

            def contrast(t, k, view_d, factor, rest, op, weight):
                nc.vector.scalar_tensor_tensor(
                    out=parts[t][k], in0=view(view_d)[:, :, t, :], scalar=factor * CROSS_SCALE, in1=rest, op0=ALU.mult, op1=op
                )
                nc.scalar.activation(out=dst[k][:, :, t, :], in_=parts[t][k], func=ACT.Square, scale=math.sqrt(weight))

            pair = [view(pair_sum[:])[:, :, t, :] for t in range(2)]
            contrast(0, 1, second[:, 1, :], -2.0, pair[0], ALU.add, CROSS_WEIGHTS[1])
            contrast(0, 2, y3, 2.0, pair[0], ALU.subtract, CROSS_WEIGHTS[2])
            nc.gpsimd.tensor_tensor(out=dst[TERMS][:, :, 0, :], in0=parts[0][1], in1=parts[0][2], op=ALU.mult)
            triple_sum = sb(f"triple_sum{i}", [P, 2, GROUPS], F32)
            nc.vector.scalar_tensor_tensor(
                out=triple_sum[:], in0=view(second[:, 1, :])[:, :, 1, :], scalar=CROSS_SCALE, in1=pair[1], op0=ALU.mult, op1=ALU.add
            )
            contrast(0, 0, second[:, 0, :], -2.0, pair[0], ALU.add, CROSS_WEIGHTS[0])
            contrast(1, 0, second[:, 0, :], -2.0, pair[1], ALU.add, WEIGHTS[0] / 1.5)
            contrast(1, 2, y3, -3.0, triple_sum[:], ALU.add, WEIGHTS[2] / 1.5)
            contrast(1, 1, second[:, 1, :], -2.0, pair[1], ALU.add, WEIGHTS[1] / 1.5)

        def terms_of(i):
            (last_terms if i == last else four_terms if i in FOUR_TERMS else three_terms)(i, *made[i])

        def add_terms(acc, terms, count, order, opens=True, closes=True):
            for k in order:
                for i in range(count):
                    nc.tensor.matmul(
                        out=acc[:, i, :], lhsT=terms[:, k, i, :], rhs=ident[:], is_transpose=True,
                        start=(opens and k == order[0] and i == 0), stop=(closes and k == order[-1] and i == count - 1),
                    )

        last = len(steps) - 1
        made = [products(0), products(1)]
        nc.gpsimd.tensor_scalar(out=w2_bf[:], in0=w2_raw[:].rearrange("p j c -> p c j"), scalar1=1.0, scalar2=0.0, op0=ALU.mult, op1=ALU.add)
        for i in range(last - 1):
            if i == last - 2:
                terms_of(i)
                made.append(products(i + 2))
            else:
                made.append(products(i + 2))
                terms_of(i)
        sums0 = bank("sums0", [P, PACK, P], 4)
        for u in range(2):
            add_terms(sums0[:, 2 * u : 2 * u + 2, :], terms0[u], 2, range(terms0[u].shape[1]), u == 0, u == 1)
        sums1 = bank("sums1", [P, PACK, P], 5)
        for u in range(2):
            terms_of(last - 1 + u)
            if u == 0:
                add_terms(sums1[:, 0:2, :], terms1[0], 2, (1, 2, 0, 3), True, False)
            else:
                for t in range(2):
                    add_terms(sums1[:, 2 + t : 3 + t, :], terms1[1][:, :, t : t + 1, :], 1, ((1, 2, 0, 3), (0, 2, 1))[t], False, t == 1)
        w2_codes = keep.tile([P, N], U32, name="w2_codes", tag="pair_sum3", align_bytes=64)
        nc.vector.quantize_mx(out=w2_codes[:].bitcast(FP8X4), scales=w2_plane[:], in_=w2_bf[:].rearrange("p c j -> p (c j)"))

        z_bf = [keep.tile([P, P, PACK], BF16, name="z_bf0", tag=f"pair_sum{last}", align_bytes=64), sb("z_bf1", [P, P, PACK], BF16)]

        def scale_z(acc, v0, v1):
            nc.vector.tensor_tensor(
                out=z_bf[v0 // P][:, v0 % P : v0 % P + v1 - v0, :], in0=acc.rearrange("p t v -> p v t"),
                in1=unit_sb[:].unsqueeze(1).to_broadcast([P, v1 - v0, PACK]), op=ALU.mult,
            )

        def costs(v0, v1, number):
            z_codes = sb(f"z_codes{v0}", [P, v1 - v0], U32)
            z_plane = sb(f"z_plane{v0}", [P, v1 - v0], U8)
            nc.vector.quantize_mx(out=z_codes[:].bitcast(FP8X4), scales=z_plane[:], in_=z_bf[v0 // P][:, v0 % P : v0 % P + v1 - v0, :].rearrange("p v t -> p (v t)"))
            sc = bank(f"sc{v0}", [P, (v1 - v0) // D, D], number)
            nc.tensor.matmul_mx(
                out=sc[:].rearrange("p g d -> p (g d)"), lhsT=w2_codes[:].bitcast(FP8X4), lhsT_scale=w2_plane[:],
                rhs=z_codes[:].bitcast(FP8X4), rhs_scale=z_plane[:], start=True, stop=True,
            )
            return sc

        pixels = V // D
        shifted, ex, weighted = [sb(n, [P, pixels, D], F32) for n in ("shifted", "ex", "weighted")]
        top, total, inverse, weighted_total, result = [sb(n, [P, pixels], F32) for n in ("top", "total", "inverse", "weighted_total", "result")]
        depths = depth_sb[:].rearrange("p (g d) -> p g d", d=D)

        def largest(g, sc):
            nc.vector.tensor_reduce(out=top[:, g], in_=sc[:], axis=AXIS_X, op=ALU.max)

        def exponentials(g, sc):
            nc.vector.tensor_tensor(out=shifted[:, g], in0=sc[:], in1=top[:, g].unsqueeze(2).to_broadcast(sc.shape), op=ALU.subtract)
            nc.scalar.activation(out=ex[:, g], in_=shifted[:, g], func=ACT.Exp)

        def sums(g, engine):
            nc.vector.tensor_reduce(out=total[:, g], in_=ex[:, g], axis=AXIS_X, op=ALU.add)
            engine.tensor_tensor(out=weighted[:, g], in0=ex[:, g], in1=depths[:, g], op=ALU.mult)

        middle = P + P // 2
        early, late = slice(0, P // D), (slice(P // D, middle // D), slice(middle // D, pixels))
        scale_z(sums0[:], 0, P)
        early_costs = costs(0, P, 0)
        scale_z(sums1[:, :, 0 : P // 2], P, middle)
        scale_z(sums1[:, :, P // 2 : P], middle, V)
        late_costs = [costs(P, middle, 2)]
        largest(early, early_costs)
        late_costs.append(costs(middle, V, 6))
        exponentials(early, early_costs)
        for stage in (largest, exponentials):
            for g, sc in zip(late, late_costs):
                stage(g, sc)
        sums(early, nc.gpsimd)
        nc.vector.reciprocal(out=inverse[:, early], in_=total[:, early])
        for g in late:
            sums(g, nc.vector)
        ahead = slice(0, middle // D)
        for g, piece in ((ahead, late[0]), (late[1], late[1])):
            nc.vector.tensor_reduce(out=weighted_total[:, g], in_=weighted[:, g], axis=AXIS_X, op=ALU.add)
            nc.vector.reciprocal(out=inverse[:, piece], in_=total[:, piece])
        for g in (ahead, late[1]):
            nc.vector.tensor_tensor(out=result[:, g], in0=weighted_total[:, g], in1=inverse[:, g], op=ALU.mult)
        nc.sync.dma_start(out=out, in_=result[:])
